import numpy as np
import ml_dtypes


def mxq(x, axis, fmt="e4m3"):
    dtype, down = {"e4m3": (ml_dtypes.float8_e4m3fn, 7), "e5m2": (ml_dtypes.float8_e5m2, 14)}[fmt]
    v = np.moveaxis(np.asarray(x, np.float32).astype(ml_dtypes.bfloat16).astype(np.float64), axis, -1)
    blocks = v.reshape(v.shape[:-1] + (-1, 32))
    amax = np.abs(blocks).max(-1, keepdims=True)
    byte = np.maximum(np.where(amax > 0, np.frexp(amax)[1] - 1 + 127, 0) - down, 1)
    scale = np.exp2(byte - 127.0)
    codes = (blocks / scale).astype(np.float32).astype(dtype).astype(np.float64)
    return np.moveaxis((codes * scale).reshape(v.shape), -1, axis)


WIDE = False


def mx_kscale(k):
    if not WIDE:
        return np.ones(k)
    levels = np.array([24, -24, 12, -12, 0])
    if k % 512:
        return np.exp2(np.random.permutation(np.resize(levels, k // 32))).repeat(32)
    a = np.empty((k // 512, 16))
    for p in range(k // 512):
        a[p, :8] = np.random.permutation(np.resize(levels, 8))
        for g in range(8):
            far = levels[np.abs(levels - a[p, g]) >= 10]
            a[p, g + 8] = far[np.random.randint(len(far))]
    return np.exp2(a.ravel()).repeat(32)


def f64(x):
    return np.asarray(x).astype(np.float64)


def striped(idx):
    return np.tile(idx.reshape(-1, 16).T, (8, 1)).astype(np.uint16)


def unstriped(offs):
    return offs[:16].T.reshape(-1).astype(np.int64)


E2M1 = np.array([0.0, 0.5, 1.0, 1.5, 2.0, 3.0, 4.0, 6.0, -0.0, -0.5, -1.0, -1.5, -2.0, -3.0, -4.0, -6.0])


def pack_weight(w, fmt):
    k, n = w.shape
    w = f64(np.asarray(w, np.float32).astype(ml_dtypes.bfloat16)).reshape(k // 32, 32, n)
    amax = np.abs(w).max(1)
    if fmt == "e4m3":
        byte = np.frexp(amax)[1] - 1 + 127 - 7
    else:
        mant, ex = np.frexp(amax / 6.0)
        byte = np.where(mant > 0.5, ex, ex - 1) + 127
    byte = np.clip(np.where(amax > 0, byte, 1), 1, 254)
    scaled = (w * np.exp2(127.0 - byte)[:, None, :]).reshape(k, n).astype(np.float32)
    by_word = np.ascontiguousarray(scaled.reshape(k // 512, 128, 4, n).transpose(0, 1, 3, 2))
    if fmt == "e4m3":
        words = by_word.astype(ml_dtypes.float8_e4m3fn).view(np.uint8)
    else:
        c = by_word.astype(ml_dtypes.float4_e2m1fn).view(np.uint8) & 0xF
        words = (c[..., 0::2] | (c[..., 1::2] << 4)).reshape(k // 512, 128, 2 * n)
    return np.ascontiguousarray(words), np.ascontiguousarray(byte.astype(np.uint8).reshape(k // 512, 16, n))


def unpack_weight(words, scales, fmt):
    g, _, n = scales.shape
    words = np.ascontiguousarray(words).reshape(g, 128, n, -1)
    if fmt == "e4m3":
        vals = words.view(ml_dtypes.float8_e4m3fn).astype(np.float64)
    else:
        nib = np.empty((g, 128, n, 4), np.uint8)
        nib[..., 0::2] = words & 0xF
        nib[..., 1::2] = words >> 4
        vals = E2M1[nib]
    vals = vals * np.repeat(np.exp2(scales.astype(np.float64) - 127.0), 8, axis=1)[..., None]
    return vals.transpose(0, 1, 3, 2).reshape(g * 512, n)


def gelu(f):
    return 0.5 * f * (1.0 + np.tanh(np.sqrt(2.0 / np.pi) * (f + 0.044715 * f**3)))


K, R, N, T, J = 1024, 512, 512, 2048, 1024


def setup_inputs():
    n = np.random.standard_normal
    s = mx_kscale(K)[:, None]
    u = mx_kscale(R)[:, None]
    p_tab = pack_weight(n((K, T)) * s, "e4m3")
    p_wg = pack_weight(n((K, R)) / np.sqrt(K) / s, "e2m1")
    p_wd = pack_weight(n((R, N)) / np.sqrt(R) / u, "e2m1")
    return {
        "tab_words": p_tab[0],
        "tab_scales": p_tab[1],
        "wg_words": p_wg[0],
        "wg_scales": p_wg[1],
        "wu": (n((K, R)) / np.sqrt(K) / s * u.T).astype(np.float32),
        "wd_words": p_wd[0],
        "wd_scales": p_wd[1],
        "b": (0.3 * n(N)).astype(np.float32),
        "wgo": np.tile(np.random.uniform(0.5, 2.0, J), (128, 1)).astype(np.float32),
        "offs": striped(np.random.permutation(T)[:J]),
    }


def reference(tab_words, tab_scales, wg_words, wg_scales, wu, wd_words, wd_scales, b, wgo, offs):
    idx = unstriped(offs)
    tab_ = unpack_weight(tab_words, tab_scales, "e4m3")[:, idx]
    wg_ = unpack_weight(wg_words, wg_scales, "e2m1")
    wu_ = mxq(f64(wu), 0, "e4m3")
    ga = wg_.T @ tab_
    ub = wu_.T @ tab_
    h = gelu(ga) * ub
    h_ = mxq(h, 0, "e4m3")
    wd_ = unpack_weight(wd_words, wd_scales, "e2m1")
    y = wd_.T @ h_
    out = np.zeros((N, T))
    out[:, idx] = f64(wgo)[0] * (y + f64(b)[:, None])
    return out

@@ -1,0 +1,233 @@
+from contextlib import ExitStack
+
+import concourse.mybir as mybir
+
+K, R, N, T, J = 1024, 512, 512, 2048, 1024
+FLOPS = 2 * J * (2 * K * R + R * N)
+
+F32 = mybir.dt.float32
+BF16 = mybir.dt.bfloat16
+I32 = mybir.dt.int32
+U32 = mybir.dt.uint32
+U16 = mybir.dt.uint16
+U8 = mybir.dt.uint8
+FP8X4 = mybir.dt.float8_e4m3fn_x4
+FP4X4 = mybir.dt.float4_e2m1fn_x4
+MULT = mybir.AluOpType.mult
+GELU = mybir.ActivationFunctionType.Gelu_apprx_tanh
+IDENT = mybir.ActivationFunctionType.Identity
+
+P = 128
+PASSES = K // 512
+BLOCK = 128
+CHUNK = 256
+SCALAR_M = 64
+
+
+def tile_list_modp_ggelu_noneb_kernel(
+    tc, tab_words, tab_scales, wg_words, wg_scales, wu, wd_words, wd_scales, b, wgo, offs, out
+):
+    nc = tc.nc
+    with ExitStack() as ctx:
+        keep = ctx.enter_context(tc.tile_pool(name="keep", bufs=1))
+        ring = ctx.enter_context(tc.tile_pool(name="ring", bufs=1))
+        psum = ctx.enter_context(tc.psum_pool(name="psum", bufs=1))
+
+        offsets = keep.tile([P, J // 16], U16, name="offsets")
+        nc.sync.dma_start(offsets[:], offs)
+
+        def listed(j0, j1):
+            return offsets[:, j0 // 16 : j1 // 16]
+
+        tab_sc = keep.tile([P, T], U8, name="tab_sc", align_bytes=64)
+        wg_sc_raw = keep.tile([P, PASSES * R], U8, name="wg_sc_raw", align_bytes=64)
+        wd_sc = keep.tile([P, N], U8, name="wd_sc", align_bytes=64)
+        v_sc1 = keep.tile([P, J], U8, name="v_sc1", align_bytes=64)
+        nc.vector.memset(tab_sc[:].bitcast(I32), 0)
+        nc.vector.memset(wg_sc_raw[:].bitcast(I32), 0)
+        nc.vector.memset(wd_sc[:].bitcast(I32), 0)
+        for q in range(4):
+            nc.sync.dma_start(
+                tab_sc[32 * q : 32 * q + 8, :].bitcast(I32), tab_scales[:, 4 * q : 4 * q + 4, :].bitcast(I32)
+            )
+
+        wg_raw = keep.tile([P, PASSES * 2 * R], U8, name="wg_raw", align_bytes=64)
+        for a in range(PASSES):
+            nc.sync.dma_start(wg_raw[:, 2 * R * a : 2 * R * (a + 1)].bitcast(I32), wg_words[a].bitcast(I32))
+        wd = keep.tile([P, 2 * N], U8, name="wd", align_bytes=64)
+        nc.sync.dma_start(wd[:].bitcast(I32), wd_words[0].bitcast(I32))
+        wu_raw = []
+        tab = []
+        for a in range(PASSES):
+            raw = keep.tile([P, 4, R], F32, name=f"wu_raw{a}")
+            rows = wu[512 * a : 512 * (a + 1), :].rearrange("(p i) r -> p i r", i=4)
+            step = 1 if a == 0 else 4
+            for i in range(0, 4, step):
+                nc.sync.dma_start(raw[:, i : i + step, :], rows[:, i : i + step, :])
+            wu_raw.append(raw)
+            words = keep.tile([P, T], I32, name=f"tab{a}")
+            nc.sync.dma_start(words[:], tab_words[a].rearrange("p t i -> p (t i)").bitcast(I32))
+            tab.append(words)
+            if a == 0:
+                for q in range(4):
+                    nc.sync.dma_start(
+                        wg_sc_raw[32 * q : 32 * q + 4, :].bitcast(I32).rearrange("p (a n) -> p a n", a=PASSES),
+                        wg_scales[:, 4 * q : 4 * q + 4, :].rearrange("a r n -> r a n").bitcast(I32),
+                    )
+        for q in range(4):
+            nc.sync.dma_start(
+                wd_sc[32 * q : 32 * q + 4, :].bitcast(I32), wd_scales[0, 4 * q : 4 * q + 4, :].bitcast(I32)
+            )
+        bias = keep.tile([P, N // P], F32, name="bias")
+        with nc.allow_non_contiguous_dma(reason="one bias value a partition"):
+            nc.sync.dma_start(bias[:], b.rearrange("(c p) -> p c", p=P))
+        gate = keep.tile([P, J], F32, name="gate")
+        nc.sync.dma_start(gate[:], wgo)
+
+        pages = [keep.tile([P, T], F32, name=f"page{i}") for i in range(2)]
+        for page in pages:
+            nc.vector.memset(page[:], 0.0)
+        nc.vector.memset(v_sc1[:].bitcast(I32), 0)
+
+        wg = keep.tile([P, PASSES * 2 * R], U8, name="wg", align_bytes=64)
+        nc.vector.tensor_copy(
+            wg[:].bitcast(U16).rearrange("p (a t m) -> p a t m", a=PASSES, t=4),
+            wg_raw[:].bitcast(U16).rearrange("p (a m t) -> p a t m", a=PASSES, t=4),
+        )
+        v_sc = keep.tile([P, J], U8, name="v_sc", align_bytes=64)
+        nc.vector.tensor_copy(v_sc[:], tab_sc[:].indirect(offsets[:]))
+        nc.gpsimd.dma_start(v_sc1[0 : P - 4, :].bitcast(I32), v_sc[4:P, :].bitcast(I32))
+
+        wu_bf = [keep.tile([P, 4 * R], BF16, name=f"wu_bf{a}", align_bytes=64) for a in range(PASSES)]
+        wu_q = [keep.tile([P, R], U32, name=f"wu_q{a}", align_bytes=64) for a in range(PASSES)]
+        wu_sc = [keep.tile([P, R], U8, name=f"wu_sc{a}", align_bytes=64) for a in range(PASSES)]
+        v = [keep.tile([P, J], U32, name=f"v{a}", align_bytes=64) for a in range(PASSES)]
+
+        def cast_views(a, m0, m1):
+            dst = wu_bf[a][:].rearrange("p (t m i) -> p m i t", t=4, i=4)[:, m0:m1, :, :]
+            src = wu_raw[a][:].rearrange("p i (m t) -> p m i t", t=4)[:, m0:m1, :, :]
+            return dst, src
+
+        def quantise_wu(a):
+            nc.vector.quantize_mx(out=wu_q[a][:].bitcast(FP8X4), scales=wu_sc[a][:], in_=wu_bf[a][:])
+
+        def gather_words(a, j0, j1):
+            nc.vector.tensor_copy(v[a][:, j0:j1], tab[a][:].bitcast(U32).indirect(listed(j0, j1)))
+
+        nc.scalar.copy(*cast_views(0, 0, P))
+        gather_words(0, 0, J)
+        wg_sc = keep.tile([P, PASSES * R], U8, name="wg_sc", align_bytes=64)
+        nc.vector.tensor_copy(
+            wg_sc[:].rearrange("p (a t m) -> p a t m", a=PASSES, t=4),
+            wg_sc_raw[:].rearrange("p (a m t) -> p a t m", a=PASSES, t=4),
+        )
+        quantise_wu(0)
+        nc.scalar.copy(*cast_views(1, 0, SCALAR_M))
+        nc.vector.tensor_copy(*cast_views(1, SCALAR_M, P))
+        quantise_wu(1)
+        gather_words(1, 0, CHUNK)
+        gather_words(1, CHUNK, 2 * CHUNK)
+        gather_words(1, 2 * CHUNK, J)
+
+        v_planes = [v_sc, v_sc1]
+        h_bf = [keep.tile([P, 4 * CHUNK], BF16, name=f"h_bf{c}", align_bytes=64) for c in range(J // CHUNK)]
+        h_q = keep.tile([P, J], U32, name="h_q", align_bytes=64)
+        h_sc = keep.tile([P, J], U8, name="h_sc", align_bytes=64)
+        ga = {}
+        ub = {}
+
+        def first_stage(blk, a):
+            cols = slice(BLOCK * blk, BLOCK * (blk + 1))
+            if a == 0:
+                ga[blk] = psum.tile([P, 4 * BLOCK], F32, name="ga", tag="ga", bufs=3)
+                ub[blk] = psum.tile([P, 4 * BLOCK], F32, name="ub", tag="ub", bufs=3)
+            for t in range(4):
+                c0 = R * a + P * t
+                nc.tensor.matmul_mx(
+                    out=ga[blk][:, BLOCK * t : BLOCK * (t + 1)],
+                    lhsT=wg[:, 2 * c0 : 2 * (c0 + P)].bitcast(FP4X4),
+                    lhsT_scale=wg_sc[:, c0 : c0 + P],
+                    rhs=v[a][:, cols].bitcast(FP8X4),
+                    rhs_scale=v_planes[a][:, cols],
+                    start=(a == 0 and t == 0),
+                    stop=(a == PASSES - 1 and t == 3),
+                )
+            for t in range(4):
+                nc.tensor.matmul_mx(
+                    out=ub[blk][:, BLOCK * t : BLOCK * (t + 1)],
+                    lhsT=wu_q[a][:, P * t : P * (t + 1)].bitcast(FP8X4),
+                    lhsT_scale=wu_sc[a][:, P * t : P * (t + 1)],
+                    rhs=v[a][:, cols].bitcast(FP8X4),
+                    rhs_scale=v_planes[a][:, cols],
+                    start=(a == 0 and t == 0),
+                    stop=(a == PASSES - 1 and t == 3),
+                )
+
+        def hidden(blk):
+            gel = ring.tile([P, 4 * BLOCK], F32, name="gel", tag="gel", bufs=4)
+            by_token = "p (n t) -> p n t"
+            nc.scalar.activation(
+                gel[:].rearrange(by_token, t=4), ga[blk][:].rearrange("p (t n) -> p n t", t=4), GELU
+            )
+            half = blk % 2
+            nc.vector.tensor_tensor(
+                h_bf[blk // 2][:, 512 * half : 512 * (half + 1)].rearrange(by_token, t=4),
+                ub[blk][:].rearrange("p (t n) -> p n t", t=4),
+                gel[:].rearrange(by_token, t=4),
+                MULT,
+            )
+
+        def quantise_h(c):
+            cols = slice(CHUNK * c, CHUNK * (c + 1))
+            nc.vector.quantize_mx(out=h_q[:, cols].bitcast(FP8X4), scales=h_sc[:, cols], in_=h_bf[c][:])
+
+        def second_stage(c, j0, j1):
+            y = ring.tile([P, j1 - j0], F32, name="y", tag=f"y{c}_{j0}")
+            s = j0
+            while s < j1:
+                e = min(j1, (s // 512 + 1) * 512)
+                acc = psum.tile([P, 512], F32, name="acc", tag="acc", bufs=2)
+                nc.tensor.matmul_mx(
+                    out=acc[:, 0 : e - s],
+                    lhsT=wd[:, 2 * P * c : 2 * P * (c + 1)].bitcast(FP4X4),
+                    lhsT_scale=wd_sc[:, P * c : P * (c + 1)],
+                    rhs=h_q[:, s:e].bitcast(FP8X4),
+                    rhs_scale=h_sc[:, s:e],
+                    start=True,
+                    stop=True,
+                )
+                nc.scalar.activation(y[:, s - j0 : e - j0], acc[:, 0 : e - s], IDENT, bias=bias[:, c : c + 1])
+                s = e
+            page = pages[c % 2]
+            nc.vector.tensor_tensor(page[:].indirect(listed(j0, j1)), y[:], gate[:, j0:j1], MULT)
+            if j1 == J:
+                nc.sync.dma_start(out[P * c : P * (c + 1), :], page[:])
+
+        for blk in range(3):
+            first_stage(blk, 0)
+        for blk in range(3):
+            first_stage(blk, 1)
+            hidden(blk)
+            if blk == 1:
+                quantise_h(0)
+        first_stage(3, 0)
+        first_stage(3, 1)
+        hidden(3)
+        quantise_h(1)
+        second_stage(0, 0, CHUNK)
+        for blk in (4, 5):
+            first_stage(blk, 0)
+            first_stage(blk, 1)
+            hidden(blk)
+        quantise_h(2)
+        second_stage(0, CHUNK, 2 * CHUNK)
+        for blk in (6, 7):
+            first_stage(blk, 0)
+            first_stage(blk, 1)
+            hidden(blk)
+        quantise_h(3)
+        second_stage(1, 0, CHUNK)
+        second_stage(0, 2 * CHUNK, J)
+        second_stage(1, CHUNK, J)
+        second_stage(2, 0, J)
+        second_stage(3, 0, J)

@@ -21,7 +21,7 @@ P = 128
 PASSES = K // 512
 BLOCK = 128
 CHUNK = 256
-SCALAR_M = 64
+SCALAR_M = (64, 48)
 
 
 def tile_list_modp_ggelu_noneb_kernel(
@@ -39,55 +39,49 @@ def tile_list_modp_ggelu_noneb_kernel(
         def listed(j0, j1):
             return offsets[:, j0 // 16 : j1 // 16]
 
+        warm = keep.tile([P, 2], F32, name="warm")
+        nc.gpsimd.memset(warm[:, 0:1], 0.0)
+        nc.scalar.activation(warm[:, 1:2], warm[:, 0:1], GELU)
+
         tab_sc = keep.tile([P, T], U8, name="tab_sc", align_bytes=64)
-        wg_sc_raw = keep.tile([P, PASSES * R], U8, name="wg_sc_raw", align_bytes=64)
+        wg_sc_raw = ring.tile([P, PASSES * R], U8, name="wg_sc_raw", tag="wg_sc_raw", align_bytes=64)
         wd_sc = keep.tile([P, N], U8, name="wd_sc", align_bytes=64)
         v_sc1 = keep.tile([P, J], U8, name="v_sc1", align_bytes=64)
         nc.vector.memset(tab_sc[:].bitcast(I32), 0)
-        nc.vector.memset(wg_sc_raw[:].bitcast(I32), 0)
-        nc.vector.memset(wd_sc[:].bitcast(I32), 0)
+        nc.gpsimd.memset(wg_sc_raw[:].bitcast(I32), 0)
+        nc.gpsimd.memset(wd_sc[:].bitcast(I32), 0)
+        nc.gpsimd.memset(v_sc1[:].bitcast(I32), 0)
         for q in range(4):
             nc.sync.dma_start(
                 tab_sc[32 * q : 32 * q + 8, :].bitcast(I32), tab_scales[:, 4 * q : 4 * q + 4, :].bitcast(I32)
             )
 
         wg_raw = keep.tile([P, PASSES * 2 * R], U8, name="wg_raw", align_bytes=64)
-        for a in range(PASSES):
-            nc.sync.dma_start(wg_raw[:, 2 * R * a : 2 * R * (a + 1)].bitcast(I32), wg_words[a].bitcast(I32))
-        wd = keep.tile([P, 2 * N], U8, name="wd", align_bytes=64)
-        nc.sync.dma_start(wd[:].bitcast(I32), wd_words[0].bitcast(I32))
-        wu_raw = []
-        tab = []
-        for a in range(PASSES):
-            raw = keep.tile([P, 4, R], F32, name=f"wu_raw{a}")
-            rows = wu[512 * a : 512 * (a + 1), :].rearrange("(p i) r -> p i r", i=4)
-            step = 1 if a == 0 else 4
-            for i in range(0, 4, step):
-                nc.sync.dma_start(raw[:, i : i + step, :], rows[:, i : i + step, :])
-            wu_raw.append(raw)
-            words = keep.tile([P, T], I32, name=f"tab{a}")
-            nc.sync.dma_start(words[:], tab_words[a].rearrange("p t i -> p (t i)").bitcast(I32))
-            tab.append(words)
-            if a == 0:
-                for q in range(4):
-                    nc.sync.dma_start(
-                        wg_sc_raw[32 * q : 32 * q + 4, :].bitcast(I32).rearrange("p (a n) -> p a n", a=PASSES),
-                        wg_scales[:, 4 * q : 4 * q + 4, :].rearrange("a r n -> r a n").bitcast(I32),
-                    )
+        nc.sync.dma_start(
+            wg_raw[:].bitcast(I32).rearrange("p (a n) -> p a n", a=PASSES),
+            wg_words.rearrange("a p n -> p a n").bitcast(I32),
+        )
+        wu_raw = [ring.tile([P, 4, R], F32, name="wu_raw", tag=f"wu_raw{a}") for a in range(PASSES)]
+        tab = [keep.tile([P, T], I32, name=f"tab{a}") for a in range(PASSES)]
+
+        def load_wu(a):
+            nc.sync.dma_start(wu_raw[a][:], wu[512 * a : 512 * (a + 1), :].rearrange("(p i) r -> p i r", i=4))
+
+        def load_tab(a):
+            nc.sync.dma_start(tab[a][:], tab_words[a].rearrange("p t i -> p (t i)").bitcast(I32))
+
+        load_tab(0)
         for q in range(4):
             nc.sync.dma_start(
-                wd_sc[32 * q : 32 * q + 4, :].bitcast(I32), wd_scales[0, 4 * q : 4 * q + 4, :].bitcast(I32)
+                wg_sc_raw[32 * q : 32 * q + 4, :].bitcast(I32).rearrange("p (a n) -> p a n", a=PASSES),
+                wg_scales[:, 4 * q : 4 * q + 4, :].rearrange("a r n -> r a n").bitcast(I32),
             )
-        bias = keep.tile([P, N // P], F32, name="bias")
-        with nc.allow_non_contiguous_dma(reason="one bias value a partition"):
-            nc.sync.dma_start(bias[:], b.rearrange("(c p) -> p c", p=P))
-        gate = keep.tile([P, J], F32, name="gate")
-        nc.sync.dma_start(gate[:], wgo)
+        load_wu(0)
+        load_wu(1)
+        load_tab(1)
 
-        pages = [keep.tile([P, T], F32, name=f"page{i}") for i in range(2)]
-        for page in pages:
-            nc.vector.memset(page[:], 0.0)
-        nc.vector.memset(v_sc1[:].bitcast(I32), 0)
+        pages = [keep.tile([P, T], F32, name="page0")]
+        nc.vector.memset(pages[0][:].bitcast(I32), 0)
 
         wg = keep.tile([P, PASSES * 2 * R], U8, name="wg", align_bytes=64)
         nc.vector.tensor_copy(
@@ -96,9 +90,11 @@ def tile_list_modp_ggelu_noneb_kernel(
         )
         v_sc = keep.tile([P, J], U8, name="v_sc", align_bytes=64)
         nc.vector.tensor_copy(v_sc[:], tab_sc[:].indirect(offsets[:]))
-        nc.gpsimd.dma_start(v_sc1[0 : P - 4, :].bitcast(I32), v_sc[4:P, :].bitcast(I32))
+        for q in range(4):
+            nc.sync.dma_start(v_sc1[32 * q : 32 * q + 4, :].bitcast(I32), v_sc[32 * q + 4 : 32 * q + 8, :].bitcast(I32))
 
-        wu_bf = [keep.tile([P, 4 * R], BF16, name=f"wu_bf{a}", align_bytes=64) for a in range(PASSES)]
+
+        wu_bf = [ring.tile([P, 4 * R], BF16, name="wu_bf", tag=f"wu_bf{a}", align_bytes=64) for a in range(PASSES)]
         wu_q = [keep.tile([P, R], U32, name=f"wu_q{a}", align_bytes=64) for a in range(PASSES)]
         wu_sc = [keep.tile([P, R], U8, name=f"wu_sc{a}", align_bytes=64) for a in range(PASSES)]
         v = [keep.tile([P, J], U32, name=f"v{a}", align_bytes=64) for a in range(PASSES)]
@@ -114,33 +110,48 @@ def tile_list_modp_ggelu_noneb_kernel(
         def gather_words(a, j0, j1):
             nc.vector.tensor_copy(v[a][:, j0:j1], tab[a][:].bitcast(U32).indirect(listed(j0, j1)))
 
-        nc.scalar.copy(*cast_views(0, 0, P))
-        gather_words(0, 0, J)
+        nc.scalar.copy(*cast_views(0, 0, SCALAR_M[0]))
+        gather_words(0, 0, 2 * CHUNK)
         wg_sc = keep.tile([P, PASSES * R], U8, name="wg_sc", align_bytes=64)
         nc.vector.tensor_copy(
             wg_sc[:].rearrange("p (a t m) -> p a t m", a=PASSES, t=4),
             wg_sc_raw[:].rearrange("p (a m t) -> p a t m", a=PASSES, t=4),
         )
+        gather_words(0, 2 * CHUNK, J)
+        nc.vector.tensor_copy(*cast_views(0, SCALAR_M[0], P))
         quantise_wu(0)
-        nc.scalar.copy(*cast_views(1, 0, SCALAR_M))
-        nc.vector.tensor_copy(*cast_views(1, SCALAR_M, P))
+        nc.scalar.copy(*cast_views(1, 0, SCALAR_M[1]))
+        nc.vector.tensor_copy(*cast_views(1, SCALAR_M[1], P))
         quantise_wu(1)
+        wd = ring.tile([P, 2 * N], U8, name="wd", tag="wg_sc_raw", align_bytes=64)
+        nc.sync.dma_start(wd[:].bitcast(I32), wd_words[0].bitcast(I32))
+        for q in range(4):
+            nc.sync.dma_start(
+                wd_sc[32 * q : 32 * q + 4, :].bitcast(I32), wd_scales[0, 4 * q : 4 * q + 4, :].bitcast(I32)
+            )
+        bias = ring.tile([P, N // P], F32, name="bias", tag="wu_bf0", align_bytes=64)
+        with nc.allow_non_contiguous_dma(reason="one bias value a partition"):
+            nc.sync.dma_start(bias[:], b.rearrange("(c p) -> p c", p=P))
+        gate = ring.tile([P, J], F32, name="gate", tag="wu_raw0")
+        nc.sync.dma_start(gate[:], wgo)
         gather_words(1, 0, CHUNK)
         gather_words(1, CHUNK, 2 * CHUNK)
         gather_words(1, 2 * CHUNK, J)
 
         v_planes = [v_sc, v_sc1]
-        h_bf = [keep.tile([P, 4 * CHUNK], BF16, name=f"h_bf{c}", align_bytes=64) for c in range(J // CHUNK)]
+        h_bf = [ring.tile([P, 4 * CHUNK], BF16, name="h_bf", tag=f"h_bf{c}", align_bytes=64) for c in range(J // CHUNK)]
         h_q = keep.tile([P, J], U32, name="h_q", align_bytes=64)
         h_sc = keep.tile([P, J], U8, name="h_sc", align_bytes=64)
         ga = {}
         ub = {}
 
-        def first_stage(blk, a):
+        def bank(n):
+            return psum.tile([P, 512], F32, name="bank", tag=f"bank{n}")
+
+        def gate_pass(blk, a):
             cols = slice(BLOCK * blk, BLOCK * (blk + 1))
             if a == 0:
-                ga[blk] = psum.tile([P, 4 * BLOCK], F32, name="ga", tag="ga", bufs=3)
-                ub[blk] = psum.tile([P, 4 * BLOCK], F32, name="ub", tag="ub", bufs=3)
+                ga[blk] = bank(blk if blk < 4 else 1 + blk % 2)
             for t in range(4):
                 c0 = R * a + P * t
                 nc.tensor.matmul_mx(
@@ -152,6 +163,11 @@ def tile_list_modp_ggelu_noneb_kernel(
                     start=(a == 0 and t == 0),
                     stop=(a == PASSES - 1 and t == 3),
                 )
+
+        def up_pass(blk, a):
+            cols = slice(BLOCK * blk, BLOCK * (blk + 1))
+            if a == 0:
+                ub[blk] = bank(4 + blk % 4)
             for t in range(4):
                 nc.tensor.matmul_mx(
                     out=ub[blk][:, BLOCK * t : BLOCK * (t + 1)],
@@ -163,17 +179,22 @@ def tile_list_modp_ggelu_noneb_kernel(
                     stop=(a == PASSES - 1 and t == 3),
                 )
 
+        def first_stage(blk, a):
+            gate_pass(blk, a)
+            up_pass(blk, a)
+
+        accs = []
+
         def hidden(blk):
-            gel = ring.tile([P, 4 * BLOCK], F32, name="gel", tag="gel", bufs=4)
-            by_token = "p (n t) -> p n t"
-            nc.scalar.activation(
-                gel[:].rearrange(by_token, t=4), ga[blk][:].rearrange("p (t n) -> p n t", t=4), GELU
-            )
+            gel = ring.tile([P, 4 * BLOCK], F32, name="gel", tag=f"gel{blk}")
+            walk = "p (n t e) -> p n t e"
+            from_bank = "p (t n e) -> p n t e"
+            nc.scalar.activation(gel[:].rearrange(walk, t=4, e=2), ga[blk][:].rearrange(from_bank, t=4, e=2), GELU)
             half = blk % 2
             nc.vector.tensor_tensor(
-                h_bf[blk // 2][:, 512 * half : 512 * (half + 1)].rearrange(by_token, t=4),
-                ub[blk][:].rearrange("p (t n) -> p n t", t=4),
-                gel[:].rearrange(by_token, t=4),
+                h_bf[blk // 2][:, 512 * half : 512 * (half + 1)].rearrange("p (n e t) -> p n t e", t=4, e=2),
+                ub[blk][:].rearrange(from_bank, t=4, e=2),
+                gel[:].rearrange(walk, t=4, e=2),
                 MULT,
             )
 
@@ -181,12 +202,13 @@ def tile_list_modp_ggelu_noneb_kernel(
             cols = slice(CHUNK * c, CHUNK * (c + 1))
             nc.vector.quantize_mx(out=h_q[:, cols].bitcast(FP8X4), scales=h_sc[:, cols], in_=h_bf[c][:])
 
-        def second_stage(c, j0, j1):
-            y = ring.tile([P, j1 - j0], F32, name="y", tag=f"y{c}_{j0}")
+        def second_stage(c, j0, j1, slot=None):
+            y = ring.tile([P, j1 - j0], F32, name="y", tag=slot or f"y{c}_{j0}")
             s = j0
             while s < j1:
                 e = min(j1, (s // 512 + 1) * 512)
-                acc = psum.tile([P, 512], F32, name="acc", tag="acc", bufs=2)
+                acc = bank(3 * (len(accs) % 2))
+                accs.append(acc)
                 nc.tensor.matmul_mx(
                     out=acc[:, 0 : e - s],
                     lhsT=wd[:, 2 * P * c : 2 * P * (c + 1)].bitcast(FP4X4),
@@ -203,30 +225,31 @@ def tile_list_modp_ggelu_noneb_kernel(
             if j1 == J:
                 nc.sync.dma_start(out[P * c : P * (c + 1), :], page[:])
 
-        for blk in range(3):
-            first_stage(blk, 0)
-        for blk in range(3):
+        for blk in range(4):
+            gate_pass(blk, 0)
+        for blk in range(4):
+            up_pass(blk, 0)
+        for blk in range(4):
             first_stage(blk, 1)
             hidden(blk)
             if blk == 1:
                 quantise_h(0)
-        first_stage(3, 0)
-        first_stage(3, 1)
-        hidden(3)
         quantise_h(1)
-        second_stage(0, 0, CHUNK)
+        pages.append(ring.tile([P, T], F32, name="page1", tag="h_bf1", align_bytes=64))
+        nc.gpsimd.memset(pages[1][:].bitcast(I32), 0)
+        second_stage(0, 0, CHUNK, "gel3")
         for blk in (4, 5):
             first_stage(blk, 0)
             first_stage(blk, 1)
             hidden(blk)
         quantise_h(2)
-        second_stage(0, CHUNK, 2 * CHUNK)
+        second_stage(0, CHUNK, 2 * CHUNK, "gel5")
         for blk in (6, 7):
             first_stage(blk, 0)
             first_stage(blk, 1)
             hidden(blk)
         quantise_h(3)
-        second_stage(1, 0, CHUNK)
+        second_stage(1, 0, CHUNK, "gel7")
         second_stage(0, 2 * CHUNK, J)
         second_stage(1, CHUNK, J)
         second_stage(2, 0, J)

@@ -39,10 +39,6 @@ def tile_list_modp_ggelu_noneb_kernel(
         def listed(j0, j1):
             return offsets[:, j0 // 16 : j1 // 16]
 
-        warm = keep.tile([P, 2], F32, name="warm")
-        nc.gpsimd.memset(warm[:, 0:1], 0.0)
-        nc.scalar.activation(warm[:, 1:2], warm[:, 0:1], GELU)
-
         tab_sc = keep.tile([P, T], U8, name="tab_sc", align_bytes=64)
         wg_sc_raw = ring.tile([P, PASSES * R], U8, name="wg_sc_raw", tag="wg_sc_raw", align_bytes=64)
         wd_sc = keep.tile([P, N], U8, name="wd_sc", align_bytes=64)

@@ -21,7 +21,7 @@ P = 128
 PASSES = K // 512
 BLOCK = 128
 CHUNK = 256
-SCALAR_M = (64, 48)
+SCALAR_M = (72, 64)
 
 
 def tile_list_modp_ggelu_noneb_kernel(
@@ -39,66 +39,74 @@ def tile_list_modp_ggelu_noneb_kernel(
         def listed(j0, j1):
             return offsets[:, j0 // 16 : j1 // 16]
 
-        tab_sc = keep.tile([P, T], U8, name="tab_sc", align_bytes=64)
-        wg_sc_raw = ring.tile([P, PASSES * R], U8, name="wg_sc_raw", tag="wg_sc_raw", align_bytes=64)
-        wd_sc = keep.tile([P, N], U8, name="wd_sc", align_bytes=64)
-        v_sc1 = keep.tile([P, J], U8, name="v_sc1", align_bytes=64)
-        nc.vector.memset(tab_sc[:].bitcast(I32), 0)
-        nc.gpsimd.memset(wg_sc_raw[:].bitcast(I32), 0)
-        nc.gpsimd.memset(wd_sc[:].bitcast(I32), 0)
-        nc.gpsimd.memset(v_sc1[:].bitcast(I32), 0)
-        for q in range(4):
-            nc.sync.dma_start(
-                tab_sc[32 * q : 32 * q + 8, :].bitcast(I32), tab_scales[:, 4 * q : 4 * q + 4, :].bitcast(I32)
-            )
-
-        wg_raw = keep.tile([P, PASSES * 2 * R], U8, name="wg_raw", align_bytes=64)
+        tab_sc = ring.tile([P, T], U8, name="tab_sc", tag="tab_sc", align_bytes=64)
+        nc.sync.dma_start(tab_sc[0:32, :].bitcast(I32), tab_scales.rearrange("a q t -> q a t").bitcast(I32))
+        wg_raw = ring.tile([P, PASSES * 2 * R], U8, name="wg_raw", tag="wg_raw", align_bytes=64)
         nc.sync.dma_start(
             wg_raw[:].bitcast(I32).rearrange("p (a n) -> p a n", a=PASSES),
             wg_words.rearrange("a p n -> p a n").bitcast(I32),
         )
-        wu_raw = [ring.tile([P, 4, R], F32, name="wu_raw", tag=f"wu_raw{a}") for a in range(PASSES)]
-        tab = [keep.tile([P, T], I32, name=f"tab{a}") for a in range(PASSES)]
+        tab = []
 
-        def load_wu(a):
-            nc.sync.dma_start(wu_raw[a][:], wu[512 * a : 512 * (a + 1), :].rearrange("(p i) r -> p i r", i=4))
-
-        def load_tab(a):
+        def load_tab(a, slot):
+            tab.append(ring.tile([P, T], I32, name="tab", tag=slot, align_bytes=64))
             nc.sync.dma_start(tab[a][:], tab_words[a].rearrange("p t i -> p (t i)").bitcast(I32))
 
-        load_tab(0)
+        def load_wu(a, m0, m1, slot):
+            raw = ring.tile([P, 4, 4 * (m1 - m0)], F32, name="wu_raw", tag=slot, align_bytes=64)
+            rows = wu[512 * a : 512 * (a + 1), 4 * m0 : 4 * m1]
+            nc.sync.dma_start(raw[:], rows.rearrange("(p i) r -> p i r", i=4))
+            return raw
+
+        wg_sc_raw = ring.tile([P, PASSES * R], U8, name="wg_sc_raw", tag="wg_sc_raw", align_bytes=64)
+        v_sc = keep.tile([P, PASSES * J], U8, name="v_sc", align_bytes=64)
+        nc.gpsimd.memset(wg_sc_raw[:].bitcast(I32), 0)
         for q in range(4):
             nc.sync.dma_start(
                 wg_sc_raw[32 * q : 32 * q + 4, :].bitcast(I32).rearrange("p (a n) -> p a n", a=PASSES),
                 wg_scales[:, 4 * q : 4 * q + 4, :].rearrange("a r n -> r a n").bitcast(I32),
             )
-        load_wu(0)
-        load_wu(1)
-        load_tab(1)
+        load_tab(0, "tab0")
+        load_tab(1, "tab1")
+        nc.vector.memset(tab_sc[32:64, :].bitcast(I32), 0)
+        nc.vector.memset(tab_sc[64:P, :].bitcast(I32), 0)
+        nc.vector.memset(v_sc[:].bitcast(I32), 0)
+        warm = keep.tile([P, 2], F32, name="warm")
+        nc.vector.memset(warm[:, 0:1], 0.0)
+        nc.scalar.activation(warm[:, 1:2], warm[:, 0:1], GELU)
 
-        pages = [keep.tile([P, T], F32, name="page0")]
-        nc.vector.memset(pages[0][:].bitcast(I32), 0)
+        picked_sc = ring.tile([P, J], U8, name="picked_sc", tag="picked_sc", align_bytes=64)
+        nc.vector.tensor_copy(picked_sc[:], tab_sc[:].indirect(offsets[:]))
+        for q in range(4):
+            nc.sync.dma_start(
+                v_sc[32 * q : 32 * q + 4, :].bitcast(I32), picked_sc[8 * q : 8 * q + 8, :].bitcast(I32)
+            )
+        wu0 = load_wu(0, 0, P, "tab_sc")
 
         wg = keep.tile([P, PASSES * 2 * R], U8, name="wg", align_bytes=64)
         nc.vector.tensor_copy(
             wg[:].bitcast(U16).rearrange("p (a t m) -> p a t m", a=PASSES, t=4),
             wg_raw[:].bitcast(U16).rearrange("p (a m t) -> p a t m", a=PASSES, t=4),
         )
-        v_sc = keep.tile([P, J], U8, name="v_sc", align_bytes=64)
-        nc.vector.tensor_copy(v_sc[:], tab_sc[:].indirect(offsets[:]))
-        for q in range(4):
-            nc.sync.dma_start(v_sc1[32 * q : 32 * q + 4, :].bitcast(I32), v_sc[32 * q + 4 : 32 * q + 8, :].bitcast(I32))
+        pages = []
 
+        def zeroed_page(n, slot):
+            page = ring.tile([P, T], F32, name=f"page{n}", tag=slot, align_bytes=64)
+            nc.gpsimd.memset(page[:].bitcast(I32), 0)
+            pages.append(page)
+
+        wu1a = load_wu(1, 0, SCALAR_M[1], "wg_raw")
 
         wu_bf = [ring.tile([P, 4 * R], BF16, name="wu_bf", tag=f"wu_bf{a}", align_bytes=64) for a in range(PASSES)]
         wu_q = [keep.tile([P, R], U32, name=f"wu_q{a}", align_bytes=64) for a in range(PASSES)]
         wu_sc = [keep.tile([P, R], U8, name=f"wu_sc{a}", align_bytes=64) for a in range(PASSES)]
         v = [keep.tile([P, J], U32, name=f"v{a}", align_bytes=64) for a in range(PASSES)]
 
-        def cast_views(a, m0, m1):
-            dst = wu_bf[a][:].rearrange("p (t m i) -> p m i t", t=4, i=4)[:, m0:m1, :, :]
-            src = wu_raw[a][:].rearrange("p i (m t) -> p m i t", t=4)[:, m0:m1, :, :]
-            return dst, src
+        def rounded(a):
+            return wu_bf[a][:].rearrange("p (t m i) -> p m i t", t=4, i=4)
+
+        def dealt(raw):
+            return raw[:].rearrange("p i (m t) -> p m i t", t=4)
 
         def quantise_wu(a):
             nc.vector.quantize_mx(out=wu_q[a][:].bitcast(FP8X4), scales=wu_sc[a][:], in_=wu_bf[a][:])
@@ -106,21 +114,26 @@ def tile_list_modp_ggelu_noneb_kernel(
         def gather_words(a, j0, j1):
             nc.vector.tensor_copy(v[a][:, j0:j1], tab[a][:].bitcast(U32).indirect(listed(j0, j1)))
 
-        nc.scalar.copy(*cast_views(0, 0, SCALAR_M[0]))
-        gather_words(0, 0, 2 * CHUNK)
         wg_sc = keep.tile([P, PASSES * R], U8, name="wg_sc", align_bytes=64)
         nc.vector.tensor_copy(
             wg_sc[:].rearrange("p (a t m) -> p a t m", a=PASSES, t=4),
             wg_sc_raw[:].rearrange("p (a m t) -> p a t m", a=PASSES, t=4),
         )
-        gather_words(0, 2 * CHUNK, J)
-        nc.vector.tensor_copy(*cast_views(0, SCALAR_M[0], P))
+        wu1b = load_wu(1, SCALAR_M[1], P, "wg_sc_raw")
+        zeroed_page(0, "picked_sc")
+        gather_words(0, 0, J)
+        gather_words(1, 0, J // 2)
+        gather_words(1, J // 2, J)
+        nc.scalar.copy(rounded(0)[:, 0 : SCALAR_M[0]], dealt(wu0)[:, 0 : SCALAR_M[0]])
+        nc.vector.tensor_copy(rounded(0)[:, SCALAR_M[0] : P], dealt(wu0)[:, SCALAR_M[0] : P])
         quantise_wu(0)
-        nc.scalar.copy(*cast_views(1, 0, SCALAR_M[1]))
-        nc.vector.tensor_copy(*cast_views(1, SCALAR_M[1], P))
+        nc.scalar.copy(rounded(1)[:, 0 : SCALAR_M[1]], dealt(wu1a))
+        nc.vector.tensor_copy(rounded(1)[:, SCALAR_M[1] : P], dealt(wu1b))
         quantise_wu(1)
-        wd = ring.tile([P, 2 * N], U8, name="wd", tag="wg_sc_raw", align_bytes=64)
+        wd = ring.tile([P, 2 * N], U8, name="wd", tag="tab0", align_bytes=64)
         nc.sync.dma_start(wd[:].bitcast(I32), wd_words[0].bitcast(I32))
+        wd_sc = ring.tile([P, N], U8, name="wd_sc", tag="tab1", align_bytes=64)
+        nc.gpsimd.memset(wd_sc[:].bitcast(I32), 0)
         for q in range(4):
             nc.sync.dma_start(
                 wd_sc[32 * q : 32 * q + 4, :].bitcast(I32), wd_scales[0, 4 * q : 4 * q + 4, :].bitcast(I32)
@@ -128,18 +141,19 @@ def tile_list_modp_ggelu_noneb_kernel(
         bias = ring.tile([P, N // P], F32, name="bias", tag="wu_bf0", align_bytes=64)
         with nc.allow_non_contiguous_dma(reason="one bias value a partition"):
             nc.sync.dma_start(bias[:], b.rearrange("(c p) -> p c", p=P))
-        gate = ring.tile([P, J], F32, name="gate", tag="wu_raw0")
+        gate = ring.tile([P, J], F32, name="gate", tag="tab_sc", align_bytes=64)
         nc.sync.dma_start(gate[:], wgo)
-        gather_words(1, 0, CHUNK)
-        gather_words(1, CHUNK, 2 * CHUNK)
-        gather_words(1, 2 * CHUNK, J)
 
-        v_planes = [v_sc, v_sc1]
         h_bf = [ring.tile([P, 4 * CHUNK], BF16, name="h_bf", tag=f"h_bf{c}", align_bytes=64) for c in range(J // CHUNK)]
         h_q = keep.tile([P, J], U32, name="h_q", align_bytes=64)
         h_sc = keep.tile([P, J], U8, name="h_sc", align_bytes=64)
         ga = {}
         ub = {}
+        gel_early = ring.tile([P, 16 * BLOCK], F32, name="gel_early", tag="wg_raw", align_bytes=64)
+        gel_late = keep.tile([P, 16 * BLOCK], F32, name="gel_late")
+        gel = [(gel_early, gel_late)[blk // 4][:, 512 * (blk % 4) : 512 * (blk % 4 + 1)] for blk in range(8)]
+        walk = "p (n t e) -> p n t e"
+        from_bank = "p (t n e) -> p n t e"
 
         def bank(n):
             return psum.tile([P, 512], F32, name="bank", tag=f"bank{n}")
@@ -147,7 +161,7 @@ def tile_list_modp_ggelu_noneb_kernel(
         def gate_pass(blk, a):
             cols = slice(BLOCK * blk, BLOCK * (blk + 1))
             if a == 0:
-                ga[blk] = bank(blk if blk < 4 else 1 + blk % 2)
+                ga[blk] = bank(blk if blk < 4 else blk % 2)
             for t in range(4):
                 c0 = R * a + P * t
                 nc.tensor.matmul_mx(
@@ -155,9 +169,13 @@ def tile_list_modp_ggelu_noneb_kernel(
                     lhsT=wg[:, 2 * c0 : 2 * (c0 + P)].bitcast(FP4X4),
                     lhsT_scale=wg_sc[:, c0 : c0 + P],
                     rhs=v[a][:, cols].bitcast(FP8X4),
-                    rhs_scale=v_planes[a][:, cols],
+                    rhs_scale=v_sc[:, J * a + BLOCK * blk : J * a + BLOCK * (blk + 1)],
                     start=(a == 0 and t == 0),
                     stop=(a == PASSES - 1 and t == 3),
+                )
+            if a == PASSES - 1:
+                nc.scalar.activation(
+                    gel[blk].rearrange(walk, t=4, e=2), ga[blk][:].rearrange(from_bank, t=4, e=2), GELU
                 )
 
         def up_pass(blk, a):
@@ -170,27 +188,25 @@ def tile_list_modp_ggelu_noneb_kernel(
                     lhsT=wu_q[a][:, P * t : P * (t + 1)].bitcast(FP8X4),
                     lhsT_scale=wu_sc[a][:, P * t : P * (t + 1)],
                     rhs=v[a][:, cols].bitcast(FP8X4),
-                    rhs_scale=v_planes[a][:, cols],
+                    rhs_scale=v_sc[:, J * a + BLOCK * blk : J * a + BLOCK * (blk + 1)],
                     start=(a == 0 and t == 0),
                     stop=(a == PASSES - 1 and t == 3),
                 )
 
-        def first_stage(blk, a):
-            gate_pass(blk, a)
-            up_pass(blk, a)
+        def gate_block(blk):
+            gate_pass(blk, 0)
+            gate_pass(blk, 1)
 
-        accs = []
+        def up_block(blk):
+            up_pass(blk, 0)
+            up_pass(blk, 1)
 
-        def hidden(blk):
-            gel = ring.tile([P, 4 * BLOCK], F32, name="gel", tag=f"gel{blk}")
-            walk = "p (n t e) -> p n t e"
-            from_bank = "p (t n e) -> p n t e"
-            nc.scalar.activation(gel[:].rearrange(walk, t=4, e=2), ga[blk][:].rearrange(from_bank, t=4, e=2), GELU)
+        def product(blk):
             half = blk % 2
             nc.vector.tensor_tensor(
                 h_bf[blk // 2][:, 512 * half : 512 * (half + 1)].rearrange("p (n e t) -> p n t e", t=4, e=2),
                 ub[blk][:].rearrange(from_bank, t=4, e=2),
-                gel[:].rearrange(walk, t=4, e=2),
+                gel[blk].rearrange(walk, t=4, e=2),
                 MULT,
             )
 
@@ -198,12 +214,13 @@ def tile_list_modp_ggelu_noneb_kernel(
             cols = slice(CHUNK * c, CHUNK * (c + 1))
             nc.vector.quantize_mx(out=h_q[:, cols].bitcast(FP8X4), scales=h_sc[:, cols], in_=h_bf[c][:])
 
-        def second_stage(c, j0, j1, slot=None):
-            y = ring.tile([P, j1 - j0], F32, name="y", tag=slot or f"y{c}_{j0}")
-            s = j0
-            while s < j1:
-                e = min(j1, (s // 512 + 1) * 512)
-                acc = bank(3 * (len(accs) % 2))
+        accs = []
+
+        def down(c, j0, j1):
+            y = ring.tile([P, j1 - j0], F32, name="y", tag=f"y{c}_{j0}")
+            for s in range(j0, j1, 512):
+                e = min(j1, s + 512)
+                acc = bank(2 + len(accs) % 2)
                 accs.append(acc)
                 nc.tensor.matmul_mx(
                     out=acc[:, 0 : e - s],
@@ -215,8 +232,10 @@ def tile_list_modp_ggelu_noneb_kernel(
                     stop=True,
                 )
                 nc.scalar.activation(y[:, s - j0 : e - j0], acc[:, 0 : e - s], IDENT, bias=bias[:, c : c + 1])
-                s = e
-            page = pages[c % 2]
+            return y
+
+        def put(y, c, j0, j1):
+            page = pages[c % len(pages)]
             nc.vector.tensor_tensor(page[:].indirect(listed(j0, j1)), y[:], gate[:, j0:j1], MULT)
             if j1 == J:
                 nc.sync.dma_start(out[P * c : P * (c + 1), :], page[:])
@@ -224,29 +243,44 @@ def tile_list_modp_ggelu_noneb_kernel(
         for blk in range(4):
             gate_pass(blk, 0)
         for blk in range(4):
-            up_pass(blk, 0)
+            gate_pass(blk, 1)
         for blk in range(4):
-            first_stage(blk, 1)
-            hidden(blk)
-            if blk == 1:
-                quantise_h(0)
+            up_pass(blk, 0)
+        up_pass(0, 1)
+        up_pass(1, 1)
+        gate_block(4)
+        up_pass(2, 1)
+        up_pass(3, 1)
+        product(0)
+        up_block(4)
+        product(1)
+        gate_block(5)
+        product(2)
+        quantise_h(0)
+        y00 = down(0, 0, CHUNK)
+        up_block(5)
+        gate_block(6)
+        product(3)
+        up_block(6)
+        product(4)
         quantise_h(1)
-        pages.append(ring.tile([P, T], F32, name="page1", tag="h_bf1", align_bytes=64))
-        nc.gpsimd.memset(pages[1][:].bitcast(I32), 0)
-        second_stage(0, 0, CHUNK, "gel3")
-        for blk in (4, 5):
-            first_stage(blk, 0)
-            first_stage(blk, 1)
-            hidden(blk)
+        zeroed_page(1, "h_bf1")
+        y01 = down(0, CHUNK, 2 * CHUNK)
+        gate_block(7)
+        up_block(7)
+        put(y00, 0, 0, CHUNK)
+        product(5)
+        product(6)
         quantise_h(2)
-        second_stage(0, CHUNK, 2 * CHUNK, "gel5")
-        for blk in (6, 7):
-            first_stage(blk, 0)
-            first_stage(blk, 1)
-            hidden(blk)
+        product(7)
+        y10 = down(1, 0, J // 2)
+        put(y01, 0, CHUNK, 2 * CHUNK)
         quantise_h(3)
-        second_stage(1, 0, CHUNK, "gel7")
-        second_stage(0, 2 * CHUNK, J)
-        second_stage(1, CHUNK, J)
-        second_stage(2, 0, J)
-        second_stage(3, 0, J)
+        zeroed_page(2, "h_bf3")
+        y02 = down(0, J // 2, J)
+        y11 = down(1, J // 2, J)
+        put(y10, 1, 0, J // 2)
+        put(y02, 0, J // 2, J)
+        put(y11, 1, J // 2, J)
+        put(down(2, 0, J), 2, 0, J)
+        put(down(3, 0, J), 3, 0, J)

@@ -70,10 +70,11 @@ def tile_list_modp_ggelu_noneb_kernel(
         load_tab(1, "tab1")
         nc.vector.memset(tab_sc[32:64, :].bitcast(I32), 0)
         nc.vector.memset(tab_sc[64:P, :].bitcast(I32), 0)
-        nc.vector.memset(v_sc[:].bitcast(I32), 0)
-        warm = keep.tile([P, 2], F32, name="warm")
-        nc.vector.memset(warm[:, 0:1], 0.0)
-        nc.scalar.activation(warm[:, 1:2], warm[:, 0:1], GELU)
+        nc.gpsimd.memset(v_sc[:].bitcast(I32), 0)
+        pages = [keep.tile([P, T], F32, name="page0")]
+        nc.vector.memset(pages[0][:].bitcast(I32), 0)
+        warm = keep.tile([P, 1], F32, name="warm")
+        nc.scalar.activation(warm[:], pages[0][:, 0:1], GELU)
 
         picked_sc = ring.tile([P, J], U8, name="picked_sc", tag="picked_sc", align_bytes=64)
         nc.vector.tensor_copy(picked_sc[:], tab_sc[:].indirect(offsets[:]))
@@ -88,7 +89,6 @@ def tile_list_modp_ggelu_noneb_kernel(
             wg[:].bitcast(U16).rearrange("p (a t m) -> p a t m", a=PASSES, t=4),
             wg_raw[:].bitcast(U16).rearrange("p (a m t) -> p a t m", a=PASSES, t=4),
         )
-        pages = []
 
         def zeroed_page(n, slot):
             page = ring.tile([P, T], F32, name=f"page{n}", tag=slot, align_bytes=64)
@@ -120,7 +120,6 @@ def tile_list_modp_ggelu_noneb_kernel(
             wg_sc_raw[:].rearrange("p (a m t) -> p a t m", a=PASSES, t=4),
         )
         wu1b = load_wu(1, SCALAR_M[1], P, "wg_sc_raw")
-        zeroed_page(0, "picked_sc")
         gather_words(0, 0, J)
         gather_words(1, 0, J // 2)
         gather_words(1, J // 2, J)

@@ -21,7 +21,8 @@ P = 128
 PASSES = K // 512
 BLOCK = 128
 CHUNK = 256
-SCALAR_M = (72, 64)
+SCALAR_M = (80, 80)
+SHARED = 32
 
 
 def tile_list_modp_ggelu_noneb_kernel(
@@ -70,11 +71,11 @@ def tile_list_modp_ggelu_noneb_kernel(
         load_tab(1, "tab1")
         nc.vector.memset(tab_sc[32:64, :].bitcast(I32), 0)
         nc.vector.memset(tab_sc[64:P, :].bitcast(I32), 0)
-        nc.gpsimd.memset(v_sc[:].bitcast(I32), 0)
-        pages = [keep.tile([P, T], F32, name="page0")]
-        nc.vector.memset(pages[0][:].bitcast(I32), 0)
-        warm = keep.tile([P, 1], F32, name="warm")
-        nc.scalar.activation(warm[:], pages[0][:, 0:1], GELU)
+        nc.vector.memset(v_sc[:].bitcast(I32), 0)
+        pages = []
+        warm = keep.tile([P, 2], F32, name="warm")
+        nc.vector.memset(warm[:, 0:1], 0.0)
+        nc.scalar.activation(warm[:, 1:2], warm[:, 0:1], GELU)
 
         picked_sc = ring.tile([P, J], U8, name="picked_sc", tag="picked_sc", align_bytes=64)
         nc.vector.tensor_copy(picked_sc[:], tab_sc[:].indirect(offsets[:]))
@@ -97,22 +98,28 @@ def tile_list_modp_ggelu_noneb_kernel(
 
         wu1a = load_wu(1, 0, SCALAR_M[1], "wg_raw")
 
-        wu_bf = [ring.tile([P, 4 * R], BF16, name="wu_bf", tag=f"wu_bf{a}", align_bytes=64) for a in range(PASSES)]
+        both = ring.tile([P, 8 * R - SHARED], BF16, name="wu_bf", tag="wu_bf", align_bytes=64)
+        wu_bf = [both[:, 4 * R - SHARED :], both[:, 0 : 4 * R]]
         wu_q = [keep.tile([P, R], U32, name=f"wu_q{a}", align_bytes=64) for a in range(PASSES)]
         wu_sc = [keep.tile([P, R], U8, name=f"wu_sc{a}", align_bytes=64) for a in range(PASSES)]
-        v = [keep.tile([P, J], U32, name=f"v{a}", align_bytes=64) for a in range(PASSES)]
+        v = {}
 
         def rounded(a):
-            return wu_bf[a][:].rearrange("p (t m i) -> p m i t", t=4, i=4)
+            return wu_bf[a].rearrange("p (t m i) -> p m i t", t=4, i=4)
 
         def dealt(raw):
             return raw[:].rearrange("p i (m t) -> p m i t", t=4)
 
         def quantise_wu(a):
-            nc.vector.quantize_mx(out=wu_q[a][:].bitcast(FP8X4), scales=wu_sc[a][:], in_=wu_bf[a][:])
+            nc.vector.quantize_mx(out=wu_q[a][:].bitcast(FP8X4), scales=wu_sc[a][:], in_=wu_bf[a])
 
-        def gather_words(a, j0, j1):
-            nc.vector.tensor_copy(v[a][:, j0:j1], tab[a][:].bitcast(U32).indirect(listed(j0, j1)))
+        def gather_words(a, half, slot):
+            v[a, half] = ring.tile([P, J // 2], U32, name="v", tag=slot, align_bytes=64)
+            window = tab[a][:].bitcast(U32)
+            nc.vector.tensor_copy(v[a, half][:], window.indirect(listed(half * J // 2, (half + 1) * J // 2)))
+
+        def tokens(a, blk):
+            return v[a, blk // 4][:, BLOCK * (blk % 4) : BLOCK * (blk % 4 + 1)].bitcast(FP8X4)
 
         wg_sc = keep.tile([P, PASSES * R], U8, name="wg_sc", align_bytes=64)
         nc.vector.tensor_copy(
@@ -120,37 +127,41 @@ def tile_list_modp_ggelu_noneb_kernel(
             wg_sc_raw[:].rearrange("p (a m t) -> p a t m", a=PASSES, t=4),
         )
         wu1b = load_wu(1, SCALAR_M[1], P, "wg_sc_raw")
-        gather_words(0, 0, J)
-        gather_words(1, 0, J // 2)
-        gather_words(1, J // 2, J)
+        gather_words(0, 0, "v00")
+        gather_words(1, 0, "v10")
+        gather_words(0, 1, "picked_sc")
+        gather_words(1, 1, "v11")
         nc.scalar.copy(rounded(0)[:, 0 : SCALAR_M[0]], dealt(wu0)[:, 0 : SCALAR_M[0]])
         nc.vector.tensor_copy(rounded(0)[:, SCALAR_M[0] : P], dealt(wu0)[:, SCALAR_M[0] : P])
         quantise_wu(0)
         nc.scalar.copy(rounded(1)[:, 0 : SCALAR_M[1]], dealt(wu1a))
         nc.vector.tensor_copy(rounded(1)[:, SCALAR_M[1] : P], dealt(wu1b))
         quantise_wu(1)
-        wd = ring.tile([P, 2 * N], U8, name="wd", tag="tab0", align_bytes=64)
-        nc.sync.dma_start(wd[:].bitcast(I32), wd_words[0].bitcast(I32))
-        wd_sc = ring.tile([P, N], U8, name="wd_sc", tag="tab1", align_bytes=64)
-        nc.gpsimd.memset(wd_sc[:].bitcast(I32), 0)
+        zeroed_page(0, "wu_bf")
+        wd_bytes = ring.tile([P, 3 * N], U8, name="wd_bytes", tag="tab_sc", align_bytes=64)
+        wd = wd_bytes[:, 0 : 2 * N]
+        wd_sc = wd_bytes[:, 2 * N : 3 * N]
+        nc.sync.dma_start(wd.bitcast(I32), wd_words[0].bitcast(I32))
+        nc.gpsimd.memset(wd_sc.bitcast(I32), 0)
         for q in range(4):
             nc.sync.dma_start(
-                wd_sc[32 * q : 32 * q + 4, :].bitcast(I32), wd_scales[0, 4 * q : 4 * q + 4, :].bitcast(I32)
+                wd_bytes[32 * q : 32 * q + 4, 2 * N : 3 * N].bitcast(I32),
+                wd_scales[0, 4 * q : 4 * q + 4, :].bitcast(I32),
             )
-        bias = ring.tile([P, N // P], F32, name="bias", tag="wu_bf0", align_bytes=64)
+        late = ring.tile([P, J + N // P], F32, name="late", tag="wg_sc_raw", align_bytes=64)
+        gate = late[:, 0:J]
+        bias = late[:, J : J + N // P]
         with nc.allow_non_contiguous_dma(reason="one bias value a partition"):
-            nc.sync.dma_start(bias[:], b.rearrange("(c p) -> p c", p=P))
-        gate = ring.tile([P, J], F32, name="gate", tag="tab_sc", align_bytes=64)
-        nc.sync.dma_start(gate[:], wgo)
+            nc.sync.dma_start(bias, b.rearrange("(c p) -> p c", p=P))
+        nc.sync.dma_start(gate, wgo)
 
         h_bf = [ring.tile([P, 4 * CHUNK], BF16, name="h_bf", tag=f"h_bf{c}", align_bytes=64) for c in range(J // CHUNK)]
         h_q = keep.tile([P, J], U32, name="h_q", align_bytes=64)
         h_sc = keep.tile([P, J], U8, name="h_sc", align_bytes=64)
         ga = {}
         ub = {}
-        gel_early = ring.tile([P, 16 * BLOCK], F32, name="gel_early", tag="wg_raw", align_bytes=64)
-        gel_late = keep.tile([P, 16 * BLOCK], F32, name="gel_late")
-        gel = [(gel_early, gel_late)[blk // 4][:, 512 * (blk % 4) : 512 * (blk % 4 + 1)] for blk in range(8)]
+        gel_all = ring.tile([P, 8 * 4 * BLOCK], F32, name="gel_all", tag="wg_raw", align_bytes=64)
+        gel = [gel_all[:, 512 * n : 512 * (n + 1)] for n in range(8)]
         walk = "p (n t e) -> p n t e"
         from_bank = "p (t n e) -> p n t e"
 
@@ -158,45 +169,36 @@ def tile_list_modp_ggelu_noneb_kernel(
             return psum.tile([P, 512], F32, name="bank", tag=f"bank{n}")
 
         def gate_pass(blk, a):
-            cols = slice(BLOCK * blk, BLOCK * (blk + 1))
             if a == 0:
-                ga[blk] = bank(blk if blk < 4 else blk % 2)
+                ga[blk] = bank(blk)
             for t in range(4):
                 c0 = R * a + P * t
                 nc.tensor.matmul_mx(
                     out=ga[blk][:, BLOCK * t : BLOCK * (t + 1)],
                     lhsT=wg[:, 2 * c0 : 2 * (c0 + P)].bitcast(FP4X4),
                     lhsT_scale=wg_sc[:, c0 : c0 + P],
-                    rhs=v[a][:, cols].bitcast(FP8X4),
+                    rhs=tokens(a, blk),
                     rhs_scale=v_sc[:, J * a + BLOCK * blk : J * a + BLOCK * (blk + 1)],
                     start=(a == 0 and t == 0),
                     stop=(a == PASSES - 1 and t == 3),
                 )
-            if a == PASSES - 1:
-                nc.scalar.activation(
-                    gel[blk].rearrange(walk, t=4, e=2), ga[blk][:].rearrange(from_bank, t=4, e=2), GELU
-                )
 
         def up_pass(blk, a):
-            cols = slice(BLOCK * blk, BLOCK * (blk + 1))
             if a == 0:
-                ub[blk] = bank(4 + blk % 4)
+                ub[blk] = bank(blk)
             for t in range(4):
                 nc.tensor.matmul_mx(
                     out=ub[blk][:, BLOCK * t : BLOCK * (t + 1)],
                     lhsT=wu_q[a][:, P * t : P * (t + 1)].bitcast(FP8X4),
                     lhsT_scale=wu_sc[a][:, P * t : P * (t + 1)],
-                    rhs=v[a][:, cols].bitcast(FP8X4),
+                    rhs=tokens(a, blk),
                     rhs_scale=v_sc[:, J * a + BLOCK * blk : J * a + BLOCK * (blk + 1)],
                     start=(a == 0 and t == 0),
                     stop=(a == PASSES - 1 and t == 3),
                 )
 
-        def gate_block(blk):
-            gate_pass(blk, 0)
-            gate_pass(blk, 1)
-
         def up_block(blk):
+            nc.scalar.activation(gel[blk].rearrange(walk, t=4, e=2), ga[blk][:].rearrange(from_bank, t=4, e=2), GELU)
             up_pass(blk, 0)
             up_pass(blk, 1)
 
@@ -219,7 +221,7 @@ def tile_list_modp_ggelu_noneb_kernel(
             y = ring.tile([P, j1 - j0], F32, name="y", tag=f"y{c}_{j0}")
             for s in range(j0, j1, 512):
                 e = min(j1, s + 512)
-                acc = bank(2 + len(accs) % 2)
+                acc = bank(len(accs) % 2)
                 accs.append(acc)
                 nc.tensor.matmul_mx(
                     out=acc[:, 0 : e - s],
@@ -239,33 +241,31 @@ def tile_list_modp_ggelu_noneb_kernel(
             if j1 == J:
                 nc.sync.dma_start(out[P * c : P * (c + 1), :], page[:])
 
-        for blk in range(4):
+        def gate_block(blk):
             gate_pass(blk, 0)
-        for blk in range(4):
             gate_pass(blk, 1)
-        for blk in range(4):
-            up_pass(blk, 0)
-        up_pass(0, 1)
-        up_pass(1, 1)
-        gate_block(4)
-        up_pass(2, 1)
-        up_pass(3, 1)
+
+        for blk in range(6):
+            gate_block(blk)
+        up_block(0)
+        up_block(1)
+        gate_block(6)
+        up_block(2)
         product(0)
-        up_block(4)
+        up_block(3)
+        gate_block(7)
         product(1)
-        gate_block(5)
+        up_block(4)
         product(2)
         quantise_h(0)
         y00 = down(0, 0, CHUNK)
         up_block(5)
-        gate_block(6)
         product(3)
         up_block(6)
         product(4)
         quantise_h(1)
         zeroed_page(1, "h_bf1")
         y01 = down(0, CHUNK, 2 * CHUNK)
-        gate_block(7)
         up_block(7)
         put(y00, 0, 0, CHUNK)
         product(5)

@@ -21,7 +21,7 @@ P = 128
 PASSES = K // 512
 BLOCK = 128
 CHUNK = 256
-SCALAR_M = (80, 80)
+SCALAR_M = (88, 48)
 SHARED = 32
 
 
@@ -68,14 +68,11 @@ def tile_list_modp_ggelu_noneb_kernel(
                 wg_scales[:, 4 * q : 4 * q + 4, :].rearrange("a r n -> r a n").bitcast(I32),
             )
         load_tab(0, "tab0")
-        load_tab(1, "tab1")
+        wu0 = load_wu(0, 0, P, "wu0")
         nc.vector.memset(tab_sc[32:64, :].bitcast(I32), 0)
         nc.vector.memset(tab_sc[64:P, :].bitcast(I32), 0)
         nc.vector.memset(v_sc[:].bitcast(I32), 0)
         pages = []
-        warm = keep.tile([P, 2], F32, name="warm")
-        nc.vector.memset(warm[:, 0:1], 0.0)
-        nc.scalar.activation(warm[:, 1:2], warm[:, 0:1], GELU)
 
         picked_sc = ring.tile([P, J], U8, name="picked_sc", tag="picked_sc", align_bytes=64)
         nc.vector.tensor_copy(picked_sc[:], tab_sc[:].indirect(offsets[:]))
@@ -83,7 +80,7 @@ def tile_list_modp_ggelu_noneb_kernel(
             nc.sync.dma_start(
                 v_sc[32 * q : 32 * q + 4, :].bitcast(I32), picked_sc[8 * q : 8 * q + 8, :].bitcast(I32)
             )
-        wu0 = load_wu(0, 0, P, "tab_sc")
+        wu1 = load_wu(1, 0, P, "tab_sc")
 
         wg = keep.tile([P, PASSES * 2 * R], U8, name="wg", align_bytes=64)
         nc.vector.tensor_copy(
@@ -96,7 +93,7 @@ def tile_list_modp_ggelu_noneb_kernel(
             nc.gpsimd.memset(page[:].bitcast(I32), 0)
             pages.append(page)
 
-        wu1a = load_wu(1, 0, SCALAR_M[1], "wg_raw")
+        load_tab(1, "wg_raw")
 
         both = ring.tile([P, 8 * R - SHARED], BF16, name="wu_bf", tag="wu_bf", align_bytes=64)
         wu_bf = [both[:, 4 * R - SHARED :], both[:, 0 : 4 * R]]
@@ -113,32 +110,29 @@ def tile_list_modp_ggelu_noneb_kernel(
         def quantise_wu(a):
             nc.vector.quantize_mx(out=wu_q[a][:].bitcast(FP8X4), scales=wu_sc[a][:], in_=wu_bf[a])
 
-        def gather_words(a, half, slot):
-            v[a, half] = ring.tile([P, J // 2], U32, name="v", tag=slot, align_bytes=64)
-            window = tab[a][:].bitcast(U32)
-            nc.vector.tensor_copy(v[a, half][:], window.indirect(listed(half * J // 2, (half + 1) * J // 2)))
+        def gather_words(a, blk0, blk1):
+            picked = keep.tile([P, BLOCK * (blk1 - blk0)], U32, name=f"v{a}_{blk0}", align_bytes=64)
+            nc.vector.tensor_copy(picked[:], tab[a][:].bitcast(U32).indirect(listed(BLOCK * blk0, BLOCK * blk1)))
+            for blk in range(blk0, blk1):
+                v[a, blk] = picked[:, BLOCK * (blk - blk0) : BLOCK * (blk - blk0 + 1)]
 
         def tokens(a, blk):
-            return v[a, blk // 4][:, BLOCK * (blk % 4) : BLOCK * (blk % 4 + 1)].bitcast(FP8X4)
+            return v[a, blk].bitcast(FP8X4)
 
         wg_sc = keep.tile([P, PASSES * R], U8, name="wg_sc", align_bytes=64)
         nc.vector.tensor_copy(
             wg_sc[:].rearrange("p (a t m) -> p a t m", a=PASSES, t=4),
             wg_sc_raw[:].rearrange("p (a m t) -> p a t m", a=PASSES, t=4),
         )
-        wu1b = load_wu(1, SCALAR_M[1], P, "wg_sc_raw")
-        gather_words(0, 0, "v00")
-        gather_words(1, 0, "v10")
-        gather_words(0, 1, "picked_sc")
-        gather_words(1, 1, "v11")
-        nc.scalar.copy(rounded(0)[:, 0 : SCALAR_M[0]], dealt(wu0)[:, 0 : SCALAR_M[0]])
-        nc.vector.tensor_copy(rounded(0)[:, SCALAR_M[0] : P], dealt(wu0)[:, SCALAR_M[0] : P])
-        quantise_wu(0)
-        nc.scalar.copy(rounded(1)[:, 0 : SCALAR_M[1]], dealt(wu1a))
-        nc.vector.tensor_copy(rounded(1)[:, SCALAR_M[1] : P], dealt(wu1b))
-        quantise_wu(1)
-        zeroed_page(0, "wu_bf")
-        wd_bytes = ring.tile([P, 3 * N], U8, name="wd_bytes", tag="tab_sc", align_bytes=64)
+        gather_words(0, 0, 8)
+        for a, raw in enumerate((wu0, wu1)):
+            nc.scalar.copy(rounded(a)[:, 0 : SCALAR_M[a]], dealt(raw)[:, 0 : SCALAR_M[a]])
+            nc.vector.tensor_copy(rounded(a)[:, SCALAR_M[a] : P], dealt(raw)[:, SCALAR_M[a] : P])
+            quantise_wu(a)
+        for blk in range(0, 8, 2):
+            gather_words(1, blk, blk + 2)
+        zeroed_page(0, "wg_raw")
+        wd_bytes = ring.tile([P, 3 * N], U8, name="wd_bytes", tag="wu0", align_bytes=64)
         wd = wd_bytes[:, 0 : 2 * N]
         wd_sc = wd_bytes[:, 2 * N : 3 * N]
         nc.sync.dma_start(wd.bitcast(I32), wd_words[0].bitcast(I32))
@@ -148,7 +142,7 @@ def tile_list_modp_ggelu_noneb_kernel(
                 wd_bytes[32 * q : 32 * q + 4, 2 * N : 3 * N].bitcast(I32),
                 wd_scales[0, 4 * q : 4 * q + 4, :].bitcast(I32),
             )
-        late = ring.tile([P, J + N // P], F32, name="late", tag="wg_sc_raw", align_bytes=64)
+        late = ring.tile([P, J + N // P], F32, name="late", tag="wu_bf", align_bytes=64)
         gate = late[:, 0:J]
         bias = late[:, J : J + N // P]
         with nc.allow_non_contiguous_dma(reason="one bias value a partition"):
@@ -160,7 +154,7 @@ def tile_list_modp_ggelu_noneb_kernel(
         h_sc = keep.tile([P, J], U8, name="h_sc", align_bytes=64)
         ga = {}
         ub = {}
-        gel_all = ring.tile([P, 8 * 4 * BLOCK], F32, name="gel_all", tag="wg_raw", align_bytes=64)
+        gel_all = ring.tile([P, 8 * 4 * BLOCK], F32, name="gel_all", tag="tab_sc", align_bytes=64)
         gel = [gel_all[:, 512 * n : 512 * (n + 1)] for n in range(8)]
         walk = "p (n t e) -> p n t e"
         from_bank = "p (t n e) -> p n t e"
@@ -170,7 +164,7 @@ def tile_list_modp_ggelu_noneb_kernel(
 
         def gate_pass(blk, a):
             if a == 0:
-                ga[blk] = bank(blk)
+                ga[blk] = bank(blk if blk < 4 else blk % 2)
             for t in range(4):
                 c0 = R * a + P * t
                 nc.tensor.matmul_mx(
@@ -185,7 +179,7 @@ def tile_list_modp_ggelu_noneb_kernel(
 
         def up_pass(blk, a):
             if a == 0:
-                ub[blk] = bank(blk)
+                ub[blk] = bank(4 + blk % 4)
             for t in range(4):
                 nc.tensor.matmul_mx(
                     out=ub[blk][:, BLOCK * t : BLOCK * (t + 1)],
@@ -197,8 +191,10 @@ def tile_list_modp_ggelu_noneb_kernel(
                     stop=(a == PASSES - 1 and t == 3),
                 )
 
-        def up_block(blk):
+        def gelu(blk):
             nc.scalar.activation(gel[blk].rearrange(walk, t=4, e=2), ga[blk][:].rearrange(from_bank, t=4, e=2), GELU)
+
+        def up_block(blk):
             up_pass(blk, 0)
             up_pass(blk, 1)
 
@@ -221,7 +217,7 @@ def tile_list_modp_ggelu_noneb_kernel(
             y = ring.tile([P, j1 - j0], F32, name="y", tag=f"y{c}_{j0}")
             for s in range(j0, j1, 512):
                 e = min(j1, s + 512)
-                acc = bank(len(accs) % 2)
+                acc = bank(2 + len(accs) % 2)
                 accs.append(acc)
                 nc.tensor.matmul_mx(
                     out=acc[:, 0 : e - s],
@@ -245,27 +241,35 @@ def tile_list_modp_ggelu_noneb_kernel(
             gate_pass(blk, 0)
             gate_pass(blk, 1)
 
-        for blk in range(6):
-            gate_block(blk)
-        up_block(0)
-        up_block(1)
-        gate_block(6)
-        up_block(2)
+        for blk in range(4):
+            gate_pass(blk, 0)
+        for blk in range(4):
+            up_pass(blk, 0)
+        for blk in range(4):
+            gate_pass(blk, 1)
+            gelu(blk)
+            up_pass(blk, 1)
+        gate_block(4)
+        gelu(4)
         product(0)
-        up_block(3)
-        gate_block(7)
-        product(1)
         up_block(4)
+        product(1)
+        gate_block(5)
+        gelu(5)
         product(2)
         quantise_h(0)
         y00 = down(0, 0, CHUNK)
         up_block(5)
+        gate_block(6)
+        gelu(6)
         product(3)
         up_block(6)
         product(4)
         quantise_h(1)
         zeroed_page(1, "h_bf1")
         y01 = down(0, CHUNK, 2 * CHUNK)
+        gate_block(7)
+        gelu(7)
         up_block(7)
         put(y00, 0, 0, CHUNK)
         product(5)

@@ -19,10 +19,15 @@ IDENT = mybir.ActivationFunctionType.Identity
 
 P = 128
 PASSES = K // 512
+BANK = 512
 BLOCK = 128
-CHUNK = 256
+BLOCKS = J // BLOCK
+CHUNK = 2 * BLOCK
 SCALAR_M = (88, 48)
 SHARED = 32
+GATE_BANK = (0, 1, 2, 3, 0, 6, 0, 6)
+UP_BANK = (4, 5, 6, 7, 4, 1, 5, 7)
+DOWN_BANK = (2, 3)
 
 
 def tile_list_modp_ggelu_noneb_kernel(
@@ -40,75 +45,65 @@ def tile_list_modp_ggelu_noneb_kernel(
         def listed(j0, j1):
             return offsets[:, j0 // 16 : j1 // 16]
 
-        tab_sc = ring.tile([P, T], U8, name="tab_sc", tag="tab_sc", align_bytes=64)
-        nc.sync.dma_start(tab_sc[0:32, :].bitcast(I32), tab_scales.rearrange("a q t -> q a t").bitcast(I32))
+        tab_sc = ring.tile([P, T], U8, name="tab_sc", tag="scale_window", align_bytes=64)
+        nc.sync.dma_start(tab_sc[0:32, :].bitcast(I32), tab_scales.rearrange("a g t -> g a t").bitcast(I32))
         wg_raw = ring.tile([P, PASSES * 2 * R], U8, name="wg_raw", tag="wg_raw", align_bytes=64)
         nc.sync.dma_start(
             wg_raw[:].bitcast(I32).rearrange("p (a n) -> p a n", a=PASSES),
             wg_words.rearrange("a p n -> p a n").bitcast(I32),
         )
-        tab = []
 
         def load_tab(a, slot):
-            tab.append(ring.tile([P, T], I32, name="tab", tag=slot, align_bytes=64))
-            nc.sync.dma_start(tab[a][:], tab_words[a].rearrange("p t i -> p (t i)").bitcast(I32))
+            words = ring.tile([P, T], I32, name="tab", tag=slot, align_bytes=64)
+            nc.sync.dma_start(words[:], tab_words[a].rearrange("p t i -> p (t i)").bitcast(I32))
+            return words
 
-        def load_wu(a, m0, m1, slot):
-            raw = ring.tile([P, 4, 4 * (m1 - m0)], F32, name="wu_raw", tag=slot, align_bytes=64)
-            rows = wu[512 * a : 512 * (a + 1), 4 * m0 : 4 * m1]
-            nc.sync.dma_start(raw[:], rows.rearrange("(p i) r -> p i r", i=4))
+        def load_wu(a, slot):
+            raw = ring.tile([P, 4, R], F32, name="wu_raw", tag=slot, align_bytes=64)
+            nc.sync.dma_start(raw[:], wu[512 * a : 512 * (a + 1), :].rearrange("(p i) r -> p i r", i=4))
             return raw
 
-        wg_sc_raw = ring.tile([P, PASSES * R], U8, name="wg_sc_raw", tag="wg_sc_raw", align_bytes=64)
+        wg_sc_raw = keep.tile([P, PASSES * R], U8, name="wg_sc_raw", align_bytes=64)
         v_sc = keep.tile([P, PASSES * J], U8, name="v_sc", align_bytes=64)
         nc.gpsimd.memset(wg_sc_raw[:].bitcast(I32), 0)
         for q in range(4):
             nc.sync.dma_start(
                 wg_sc_raw[32 * q : 32 * q + 4, :].bitcast(I32).rearrange("p (a n) -> p a n", a=PASSES),
-                wg_scales[:, 4 * q : 4 * q + 4, :].rearrange("a r n -> r a n").bitcast(I32),
+                wg_scales[:, 4 * q : 4 * q + 4, :].rearrange("a g n -> g a n").bitcast(I32),
             )
-        load_tab(0, "tab0")
-        wu0 = load_wu(0, 0, P, "wu0")
+        tab = [load_tab(0, "tab0")]
+        wu_raw = [load_wu(0, "wu0")]
         nc.vector.memset(tab_sc[32:64, :].bitcast(I32), 0)
         nc.vector.memset(tab_sc[64:P, :].bitcast(I32), 0)
-        nc.vector.memset(v_sc[:].bitcast(I32), 0)
-        pages = []
+        nc.gpsimd.memset(v_sc[:].bitcast(I32), 0)
 
-        picked_sc = ring.tile([P, J], U8, name="picked_sc", tag="picked_sc", align_bytes=64)
+        pages = [keep.tile([P, T], F32, name="page0")]
+        nc.vector.memset(pages[0][:].bitcast(I32), 0)
+
+        def zeroed_page(slot):
+            page = ring.tile([P, T], F32, name="page", tag=slot, align_bytes=64)
+            nc.gpsimd.memset(page[:].bitcast(I32), 0)
+            pages.append(page)
+
+        picked_sc = keep.tile([P, J], U8, name="picked_sc", align_bytes=64)
         nc.vector.tensor_copy(picked_sc[:], tab_sc[:].indirect(offsets[:]))
         for q in range(4):
-            nc.sync.dma_start(
-                v_sc[32 * q : 32 * q + 4, :].bitcast(I32), picked_sc[8 * q : 8 * q + 8, :].bitcast(I32)
-            )
-        wu1 = load_wu(1, 0, P, "tab_sc")
+            nc.sync.dma_start(v_sc[32 * q : 32 * q + 4, :].bitcast(I32), picked_sc[8 * q : 8 * q + 8, :].bitcast(I32))
+        wu_raw.append(load_wu(1, "scale_window"))
 
         wg = keep.tile([P, PASSES * 2 * R], U8, name="wg", align_bytes=64)
         nc.vector.tensor_copy(
             wg[:].bitcast(U16).rearrange("p (a t m) -> p a t m", a=PASSES, t=4),
             wg_raw[:].bitcast(U16).rearrange("p (a m t) -> p a t m", a=PASSES, t=4),
         )
+        tab.append(load_tab(1, "wg_raw"))
+        wg_sc = keep.tile([P, PASSES * R], U8, name="wg_sc", align_bytes=64)
+        nc.vector.tensor_copy(
+            wg_sc[:].rearrange("p (a t m) -> p a t m", a=PASSES, t=4),
+            wg_sc_raw[:].rearrange("p (a m t) -> p a t m", a=PASSES, t=4),
+        )
 
-        def zeroed_page(n, slot):
-            page = ring.tile([P, T], F32, name=f"page{n}", tag=slot, align_bytes=64)
-            nc.gpsimd.memset(page[:].bitcast(I32), 0)
-            pages.append(page)
-
-        load_tab(1, "wg_raw")
-
-        both = ring.tile([P, 8 * R - SHARED], BF16, name="wu_bf", tag="wu_bf", align_bytes=64)
-        wu_bf = [both[:, 4 * R - SHARED :], both[:, 0 : 4 * R]]
-        wu_q = [keep.tile([P, R], U32, name=f"wu_q{a}", align_bytes=64) for a in range(PASSES)]
-        wu_sc = [keep.tile([P, R], U8, name=f"wu_sc{a}", align_bytes=64) for a in range(PASSES)]
         v = {}
-
-        def rounded(a):
-            return wu_bf[a].rearrange("p (t m i) -> p m i t", t=4, i=4)
-
-        def dealt(raw):
-            return raw[:].rearrange("p i (m t) -> p m i t", t=4)
-
-        def quantise_wu(a):
-            nc.vector.quantize_mx(out=wu_q[a][:].bitcast(FP8X4), scales=wu_sc[a][:], in_=wu_bf[a])
 
         def gather_words(a, blk0, blk1):
             picked = keep.tile([P, BLOCK * (blk1 - blk0)], U32, name=f"v{a}_{blk0}", align_bytes=64)
@@ -116,22 +111,22 @@ def tile_list_modp_ggelu_noneb_kernel(
             for blk in range(blk0, blk1):
                 v[a, blk] = picked[:, BLOCK * (blk - blk0) : BLOCK * (blk - blk0 + 1)]
 
-        def tokens(a, blk):
-            return v[a, blk].bitcast(FP8X4)
+        gather_words(0, 0, BLOCKS)
 
-        wg_sc = keep.tile([P, PASSES * R], U8, name="wg_sc", align_bytes=64)
-        nc.vector.tensor_copy(
-            wg_sc[:].rearrange("p (a t m) -> p a t m", a=PASSES, t=4),
-            wg_sc_raw[:].rearrange("p (a m t) -> p a t m", a=PASSES, t=4),
-        )
-        gather_words(0, 0, 8)
-        for a, raw in enumerate((wu0, wu1)):
-            nc.scalar.copy(rounded(a)[:, 0 : SCALAR_M[a]], dealt(raw)[:, 0 : SCALAR_M[a]])
-            nc.vector.tensor_copy(rounded(a)[:, SCALAR_M[a] : P], dealt(raw)[:, SCALAR_M[a] : P])
-            quantise_wu(a)
-        for blk in range(0, 8, 2):
-            gather_words(1, blk, blk + 2)
-        zeroed_page(0, "wg_raw")
+        wu_both = ring.tile([P, 8 * R - SHARED], BF16, name="wu_both", tag="wu_bf", align_bytes=64)
+        wu_bf = [wu_both[:, 4 * R - SHARED :], wu_both[:, 0 : 4 * R]]
+        wu_q = [keep.tile([P, R], U32, name=f"wu_q{a}", align_bytes=64) for a in range(PASSES)]
+        wu_sc = [keep.tile([P, R], U8, name=f"wu_sc{a}", align_bytes=64) for a in range(PASSES)]
+        for a in range(PASSES):
+            rounded = wu_bf[a].rearrange("p (t m i) -> p m i t", t=4, i=4)
+            dealt = wu_raw[a][:].rearrange("p i (m t) -> p m i t", t=4)
+            nc.scalar.copy(rounded[:, 0 : SCALAR_M[a]], dealt[:, 0 : SCALAR_M[a]])
+            nc.vector.tensor_copy(rounded[:, SCALAR_M[a] : P], dealt[:, SCALAR_M[a] : P])
+            nc.vector.quantize_mx(out=wu_q[a][:].bitcast(FP8X4), scales=wu_sc[a][:], in_=wu_bf[a])
+
+        for blk in range(0, BLOCKS, CHUNK // BLOCK):
+            gather_words(1, blk, blk + CHUNK // BLOCK)
+
         wd_bytes = ring.tile([P, 3 * N], U8, name="wd_bytes", tag="wu0", align_bytes=64)
         wd = wd_bytes[:, 0 : 2 * N]
         wd_sc = wd_bytes[:, 2 * N : 3 * N]
@@ -142,104 +137,106 @@ def tile_list_modp_ggelu_noneb_kernel(
                 wd_bytes[32 * q : 32 * q + 4, 2 * N : 3 * N].bitcast(I32),
                 wd_scales[0, 4 * q : 4 * q + 4, :].bitcast(I32),
             )
-        late = ring.tile([P, J + N // P], F32, name="late", tag="wu_bf", align_bytes=64)
-        gate = late[:, 0:J]
-        bias = late[:, J : J + N // P]
+        epilogue = ring.tile([P, J + N // P], F32, name="epilogue", tag="wu_bf", align_bytes=64)
+        router_w = epilogue[:, 0:J]
+        bias = epilogue[:, J : J + N // P]
         with nc.allow_non_contiguous_dma(reason="one bias value a partition"):
             nc.sync.dma_start(bias, b.rearrange("(c p) -> p c", p=P))
-        nc.sync.dma_start(gate, wgo)
+        nc.sync.dma_start(router_w, wgo)
 
-        h_bf = [ring.tile([P, 4 * CHUNK], BF16, name="h_bf", tag=f"h_bf{c}", align_bytes=64) for c in range(J // CHUNK)]
+        h_bf = [ring.tile([P, 4 * CHUNK], BF16, name="h_bf", tag=f"h_bf{n}", align_bytes=64) for n in range(J // CHUNK)]
         h_q = keep.tile([P, J], U32, name="h_q", align_bytes=64)
         h_sc = keep.tile([P, J], U8, name="h_sc", align_bytes=64)
+        gel = ring.tile([P, BLOCKS, BANK], F32, name="gel", tag="scale_window", align_bytes=64)
         ga = {}
         ub = {}
-        gel_all = ring.tile([P, 8 * 4 * BLOCK], F32, name="gel_all", tag="tab_sc", align_bytes=64)
-        gel = [gel_all[:, 512 * n : 512 * (n + 1)] for n in range(8)]
-        walk = "p (n t e) -> p n t e"
         from_bank = "p (t n e) -> p n t e"
+        by_pairs = "p (n t e) -> p n t e"
 
         def bank(n):
-            return psum.tile([P, 512], F32, name="bank", tag=f"bank{n}")
+            return psum.tile([P, BANK], F32, name="bank", tag=f"bank{n}")
 
-        def gate_pass(blk, a):
-            if a == 0:
-                ga[blk] = bank(blk if blk < 4 else blk % 2)
+        def first_stage_pass(sums, blk, a, codes, scales):
             for t in range(4):
-                c0 = R * a + P * t
                 nc.tensor.matmul_mx(
-                    out=ga[blk][:, BLOCK * t : BLOCK * (t + 1)],
-                    lhsT=wg[:, 2 * c0 : 2 * (c0 + P)].bitcast(FP4X4),
-                    lhsT_scale=wg_sc[:, c0 : c0 + P],
-                    rhs=tokens(a, blk),
+                    out=sums[:, BLOCK * t : BLOCK * (t + 1)],
+                    lhsT=codes(t),
+                    lhsT_scale=scales[:, P * t : P * (t + 1)],
+                    rhs=v[a, blk].bitcast(FP8X4),
                     rhs_scale=v_sc[:, J * a + BLOCK * blk : J * a + BLOCK * (blk + 1)],
                     start=(a == 0 and t == 0),
                     stop=(a == PASSES - 1 and t == 3),
+                )
+
+        def gate_pass(blk, a):
+            if a == 0:
+                ga[blk] = bank(GATE_BANK[blk])
+
+            def codes(t):
+                c0 = R * a + P * t
+                return wg[:, 2 * c0 : 2 * (c0 + P)].bitcast(FP4X4)
+
+            first_stage_pass(ga[blk], blk, a, codes, wg_sc[:, R * a : R * (a + 1)])
+            if a == PASSES - 1:
+                nc.scalar.activation(
+                    gel[:, blk, :].rearrange(by_pairs, t=4, e=2), ga[blk][:].rearrange(from_bank, t=4, e=2), GELU
                 )
 
         def up_pass(blk, a):
             if a == 0:
-                ub[blk] = bank(4 + blk % 4)
-            for t in range(4):
-                nc.tensor.matmul_mx(
-                    out=ub[blk][:, BLOCK * t : BLOCK * (t + 1)],
-                    lhsT=wu_q[a][:, P * t : P * (t + 1)].bitcast(FP8X4),
-                    lhsT_scale=wu_sc[a][:, P * t : P * (t + 1)],
-                    rhs=tokens(a, blk),
-                    rhs_scale=v_sc[:, J * a + BLOCK * blk : J * a + BLOCK * (blk + 1)],
-                    start=(a == 0 and t == 0),
-                    stop=(a == PASSES - 1 and t == 3),
-                )
+                ub[blk] = bank(UP_BANK[blk])
 
-        def gelu(blk):
-            nc.scalar.activation(gel[blk].rearrange(walk, t=4, e=2), ga[blk][:].rearrange(from_bank, t=4, e=2), GELU)
+            def codes(t):
+                return wu_q[a][:, P * t : P * (t + 1)].bitcast(FP8X4)
+
+            first_stage_pass(ub[blk], blk, a, codes, wu_sc[a])
+
+        def gate_block(blk):
+            for a in range(PASSES):
+                gate_pass(blk, a)
 
         def up_block(blk):
-            up_pass(blk, 0)
-            up_pass(blk, 1)
+            for a in range(PASSES):
+                up_pass(blk, a)
 
         def product(blk):
-            half = blk % 2
+            start = BANK * (blk % 2)
             nc.vector.tensor_tensor(
-                h_bf[blk // 2][:, 512 * half : 512 * (half + 1)].rearrange("p (n e t) -> p n t e", t=4, e=2),
+                h_bf[blk // 2][:, start : start + BANK].rearrange("p (n e t) -> p n t e", t=4, e=2),
                 ub[blk][:].rearrange(from_bank, t=4, e=2),
-                gel[blk].rearrange(walk, t=4, e=2),
+                gel[:, blk, :].rearrange(by_pairs, t=4, e=2),
                 MULT,
             )
 
-        def quantise_h(c):
-            cols = slice(CHUNK * c, CHUNK * (c + 1))
-            nc.vector.quantize_mx(out=h_q[:, cols].bitcast(FP8X4), scales=h_sc[:, cols], in_=h_bf[c][:])
+        def quantise_h(n):
+            cols = slice(CHUNK * n, CHUNK * (n + 1))
+            nc.vector.quantize_mx(out=h_q[:, cols].bitcast(FP8X4), scales=h_sc[:, cols], in_=h_bf[n][:])
 
-        accs = []
+        down_sums = []
 
         def down(c, j0, j1):
-            y = ring.tile([P, j1 - j0], F32, name="y", tag=f"y{c}_{j0}")
-            for s in range(j0, j1, 512):
-                e = min(j1, s + 512)
-                acc = bank(2 + len(accs) % 2)
-                accs.append(acc)
+            y = keep.tile([P, j1 - j0], F32, name=f"y{c}_{j0}")
+            for s in range(j0, j1, BANK):
+                width = min(j1 - s, BANK)
+                sums = bank(DOWN_BANK[len(down_sums) % 2])
+                down_sums.append(sums)
                 nc.tensor.matmul_mx(
-                    out=acc[:, 0 : e - s],
+                    out=sums[:, 0:width],
                     lhsT=wd[:, 2 * P * c : 2 * P * (c + 1)].bitcast(FP4X4),
                     lhsT_scale=wd_sc[:, P * c : P * (c + 1)],
-                    rhs=h_q[:, s:e].bitcast(FP8X4),
-                    rhs_scale=h_sc[:, s:e],
+                    rhs=h_q[:, s : s + width].bitcast(FP8X4),
+                    rhs_scale=h_sc[:, s : s + width],
                     start=True,
                     stop=True,
                 )
-                nc.scalar.activation(y[:, s - j0 : e - j0], acc[:, 0 : e - s], IDENT, bias=bias[:, c : c + 1])
+                nc.scalar.activation(y[:, s - j0 : s - j0 + width], sums[:, 0:width], IDENT, bias=bias[:, c : c + 1])
             return y
 
         def put(y, c, j0, j1):
-            page = pages[c % len(pages)]
-            nc.vector.tensor_tensor(page[:].indirect(listed(j0, j1)), y[:], gate[:, j0:j1], MULT)
+            page = pages[c % 3]
+            nc.vector.tensor_tensor(page[:].indirect(listed(j0, j1)), y[:], router_w[:, j0:j1], MULT)
             if j1 == J:
                 nc.sync.dma_start(out[P * c : P * (c + 1), :], page[:])
-
-        def gate_block(blk):
-            gate_pass(blk, 0)
-            gate_pass(blk, 1)
 
         for blk in range(4):
             gate_pass(blk, 0)
@@ -247,43 +244,38 @@ def tile_list_modp_ggelu_noneb_kernel(
             up_pass(blk, 0)
         for blk in range(4):
             gate_pass(blk, 1)
-            gelu(blk)
             up_pass(blk, 1)
         gate_block(4)
-        gelu(4)
         product(0)
         up_block(4)
         product(1)
-        gate_block(5)
-        gelu(5)
         product(2)
         quantise_h(0)
-        y00 = down(0, 0, CHUNK)
+        rows0_chunk0 = down(0, 0, CHUNK)
         up_block(5)
+        gate_block(5)
         gate_block(6)
-        gelu(6)
         product(3)
         up_block(6)
         product(4)
         quantise_h(1)
-        zeroed_page(1, "h_bf1")
-        y01 = down(0, CHUNK, 2 * CHUNK)
+        zeroed_page("h_bf1")
+        rows0_chunk1 = down(0, CHUNK, 2 * CHUNK)
         gate_block(7)
-        gelu(7)
         up_block(7)
-        put(y00, 0, 0, CHUNK)
+        put(rows0_chunk0, 0, 0, CHUNK)
         product(5)
         product(6)
         quantise_h(2)
         product(7)
-        y10 = down(1, 0, J // 2)
-        put(y01, 0, CHUNK, 2 * CHUNK)
+        rows1_first = down(1, 0, J // 2)
+        put(rows0_chunk1, 0, CHUNK, 2 * CHUNK)
         quantise_h(3)
-        zeroed_page(2, "h_bf3")
-        y02 = down(0, J // 2, J)
-        y11 = down(1, J // 2, J)
-        put(y10, 1, 0, J // 2)
-        put(y02, 0, J // 2, J)
-        put(y11, 1, J // 2, J)
-        put(down(2, 0, J), 2, 0, J)
-        put(down(3, 0, J), 3, 0, J)
+        zeroed_page("h_bf3")
+        rows0_second = down(0, J // 2, J)
+        rows1_second = down(1, J // 2, J)
+        put(rows1_first, 1, 0, J // 2)
+        put(rows0_second, 0, J // 2, J)
+        put(rows1_second, 1, J // 2, J)
+        for c in range(2, N // P):
+            put(down(c, 0, J), c, 0, J)

@@ -14,6 +14,7 @@ U8 = mybir.dt.uint8
 FP8X4 = mybir.dt.float8_e4m3fn_x4
 FP4X4 = mybir.dt.float4_e2m1fn_x4
 MULT = mybir.AluOpType.mult
+ADD = mybir.AluOpType.add
 GELU = mybir.ActivationFunctionType.Gelu_apprx_tanh
 IDENT = mybir.ActivationFunctionType.Identity
 
@@ -23,11 +24,13 @@ BANK = 512
 BLOCK = 128
 BLOCKS = J // BLOCK
 CHUNK = 2 * BLOCK
-SCALAR_M = (88, 48)
+SCALAR_M = (128, 80)
 SHARED = 32
-GATE_BANK = (0, 1, 2, 3, 0, 6, 0, 6)
-UP_BANK = (4, 5, 6, 7, 4, 1, 5, 7)
-DOWN_BANK = (2, 3)
+GATE_BANK = (0, 1, 2, 3, 0, 1, 2, 5)
+UP_BANK = (4, 5, 6, 7, 7, 4, 0, 3)
+EARLY_DOWN_BANK = {(0, 0): 1, (1, 0): 4, (2, 0): 2, (0, 1): 5, (1, 1): 3, (2, 1): 6}
+DOWN_BANK = (7, 1)
+VECTOR_BLOCKS = 4
 
 
 def tile_list_modp_ggelu_noneb_kernel(
@@ -63,7 +66,7 @@ def tile_list_modp_ggelu_noneb_kernel(
             nc.sync.dma_start(raw[:], wu[512 * a : 512 * (a + 1), :].rearrange("(p i) r -> p i r", i=4))
             return raw
 
-        wg_sc_raw = keep.tile([P, PASSES * R], U8, name="wg_sc_raw", align_bytes=64)
+        wg_sc_raw = ring.tile([P, PASSES * R], U8, name="wg_sc_raw", tag="wg_sc_raw", align_bytes=64)
         v_sc = keep.tile([P, PASSES * J], U8, name="v_sc", align_bytes=64)
         nc.gpsimd.memset(wg_sc_raw[:].bitcast(I32), 0)
         for q in range(4):
@@ -77,13 +80,14 @@ def tile_list_modp_ggelu_noneb_kernel(
         nc.vector.memset(tab_sc[64:P, :].bitcast(I32), 0)
         nc.gpsimd.memset(v_sc[:].bitcast(I32), 0)
 
-        pages = [keep.tile([P, T], F32, name="page0")]
-        nc.vector.memset(pages[0][:].bitcast(I32), 0)
+        pages = []
 
         def zeroed_page(slot):
             page = ring.tile([P, T], F32, name="page", tag=slot, align_bytes=64)
-            nc.gpsimd.memset(page[:].bitcast(I32), 0)
+            nc.vector.memset(page[:].bitcast(I32), 0)
             pages.append(page)
+
+        zeroed_page("page0")
 
         picked_sc = keep.tile([P, J], U8, name="picked_sc", align_bytes=64)
         nc.vector.tensor_copy(picked_sc[:], tab_sc[:].indirect(offsets[:]))
@@ -112,6 +116,8 @@ def tile_list_modp_ggelu_noneb_kernel(
                 v[a, blk] = picked[:, BLOCK * (blk - blk0) : BLOCK * (blk - blk0 + 1)]
 
         gather_words(0, 0, BLOCKS)
+        zeroed_page("wg_sc_raw")
+        zeroed_page("tab0")
 
         wu_both = ring.tile([P, 8 * R - SHARED], BF16, name="wu_both", tag="wu_bf", align_bytes=64)
         wu_bf = [wu_both[:, 4 * R - SHARED :], wu_both[:, 0 : 4 * R]]
@@ -121,7 +127,8 @@ def tile_list_modp_ggelu_noneb_kernel(
             rounded = wu_bf[a].rearrange("p (t m i) -> p m i t", t=4, i=4)
             dealt = wu_raw[a][:].rearrange("p i (m t) -> p m i t", t=4)
             nc.scalar.copy(rounded[:, 0 : SCALAR_M[a]], dealt[:, 0 : SCALAR_M[a]])
-            nc.vector.tensor_copy(rounded[:, SCALAR_M[a] : P], dealt[:, SCALAR_M[a] : P])
+            if SCALAR_M[a] < P:
+                nc.vector.tensor_copy(rounded[:, SCALAR_M[a] : P], dealt[:, SCALAR_M[a] : P])
             nc.vector.quantize_mx(out=wu_q[a][:].bitcast(FP8X4), scales=wu_sc[a][:], in_=wu_bf[a])
 
         for blk in range(0, BLOCKS, CHUNK // BLOCK):
@@ -144,14 +151,22 @@ def tile_list_modp_ggelu_noneb_kernel(
             nc.sync.dma_start(bias, b.rearrange("(c p) -> p c", p=P))
         nc.sync.dma_start(router_w, wgo)
 
-        h_bf = [ring.tile([P, 4 * CHUNK], BF16, name="h_bf", tag=f"h_bf{n}", align_bytes=64) for n in range(J // CHUNK)]
+        h_bf = [
+            ring.tile([P, 4 * width], BF16, name="h_bf", tag=f"h_bf{n}", align_bytes=64)
+            for n, width in enumerate((CHUNK, CHUNK, J // 2))
+        ]
         h_q = keep.tile([P, J], U32, name="h_q", align_bytes=64)
         h_sc = keep.tile([P, J], U8, name="h_sc", align_bytes=64)
-        gel = ring.tile([P, BLOCKS, BANK], F32, name="gel", tag="scale_window", align_bytes=64)
+        gel = ring.tile([P, VECTOR_BLOCKS, BANK], F32, name="gel", tag="scale_window", align_bytes=64)
+        factors = {
+            blk: ring.tile([P, 2, BANK], F32, name="factors", tag=f"factors{blk}")
+            for blk in range(VECTOR_BLOCKS, BLOCKS)
+        }
         ga = {}
         ub = {}
         from_bank = "p (t n e) -> p n t e"
         by_pairs = "p (n t e) -> p n t e"
+        by_token = "p (n e t) -> p n t e"
 
         def bank(n):
             return psum.tile([P, BANK], F32, name="bank", tag=f"bank{n}")
@@ -178,9 +193,11 @@ def tile_list_modp_ggelu_noneb_kernel(
 
             first_stage_pass(ga[blk], blk, a, codes, wg_sc[:, R * a : R * (a + 1)])
             if a == PASSES - 1:
-                nc.scalar.activation(
-                    gel[:, blk, :].rearrange(by_pairs, t=4, e=2), ga[blk][:].rearrange(from_bank, t=4, e=2), GELU
-                )
+                if blk < VECTOR_BLOCKS:
+                    result = gel[:, blk, :].rearrange(by_pairs, t=4, e=2)
+                else:
+                    result = factors[blk][:, 0, :].rearrange(by_token, t=4, e=2)
+                nc.scalar.activation(result, ga[blk][:].rearrange(from_bank, t=4, e=2), GELU)
 
         def up_pass(blk, a):
             if a == 0:
@@ -190,6 +207,10 @@ def tile_list_modp_ggelu_noneb_kernel(
                 return wu_q[a][:, P * t : P * (t + 1)].bitcast(FP8X4)
 
             first_stage_pass(ub[blk], blk, a, codes, wu_sc[a])
+            if a == PASSES - 1 and blk >= VECTOR_BLOCKS:
+                nc.scalar.copy(
+                    factors[blk][:, 1, :].rearrange(by_token, t=4, e=2), ub[blk][:].rearrange(from_bank, t=4, e=2)
+                )
 
         def gate_block(blk):
             for a in range(PASSES):
@@ -202,41 +223,61 @@ def tile_list_modp_ggelu_noneb_kernel(
         def product(blk):
             start = BANK * (blk % 2)
             nc.vector.tensor_tensor(
-                h_bf[blk // 2][:, start : start + BANK].rearrange("p (n e t) -> p n t e", t=4, e=2),
+                h_bf[blk // 2][:, start : start + BANK].rearrange(by_token, t=4, e=2),
                 ub[blk][:].rearrange(from_bank, t=4, e=2),
                 gel[:, blk, :].rearrange(by_pairs, t=4, e=2),
                 MULT,
             )
 
-        def quantise_h(n):
-            cols = slice(CHUNK * n, CHUNK * (n + 1))
-            nc.vector.quantize_mx(out=h_q[:, cols].bitcast(FP8X4), scales=h_sc[:, cols], in_=h_bf[n][:])
+        def product_on_gpsimd(blk):
+            start = BANK * (blk - VECTOR_BLOCKS)
+            nc.gpsimd.tensor_tensor(
+                h_bf[2][:, start : start + BANK], factors[blk][:, 0, :], factors[blk][:, 1, :], MULT
+            )
 
-        down_sums = []
+        def quantise_h(n, j0, j1):
+            nc.vector.quantize_mx(out=h_q[:, j0:j1].bitcast(FP8X4), scales=h_sc[:, j0:j1], in_=h_bf[n][:])
 
-        def down(c, j0, j1):
-            y = keep.tile([P, j1 - j0], F32, name=f"y{c}_{j0}")
-            for s in range(j0, j1, BANK):
-                width = min(j1 - s, BANK)
-                sums = bank(DOWN_BANK[len(down_sums) % 2])
-                down_sums.append(sums)
-                nc.tensor.matmul_mx(
-                    out=sums[:, 0:width],
-                    lhsT=wd[:, 2 * P * c : 2 * P * (c + 1)].bitcast(FP4X4),
-                    lhsT_scale=wd_sc[:, P * c : P * (c + 1)],
-                    rhs=h_q[:, s : s + width].bitcast(FP8X4),
-                    rhs_scale=h_sc[:, s : s + width],
-                    start=True,
-                    stop=True,
-                )
-                nc.scalar.activation(y[:, s - j0 : s - j0 + width], sums[:, 0:width], IDENT, bias=bias[:, c : c + 1])
-            return y
+        def down_sums(c, j0, j1, n):
+            sums = bank(n)
+            nc.tensor.matmul_mx(
+                out=sums[:, 0 : j1 - j0],
+                lhsT=wd[:, 2 * P * c : 2 * P * (c + 1)].bitcast(FP4X4),
+                lhsT_scale=wd_sc[:, P * c : P * (c + 1)],
+                rhs=h_q[:, j0:j1].bitcast(FP8X4),
+                rhs_scale=h_sc[:, j0:j1],
+                start=True,
+                stop=True,
+            )
+            return sums[:, 0 : j1 - j0]
+
+        def early_sums(c, n):
+            return down_sums(c, CHUNK * n, CHUNK * (n + 1), EARLY_DOWN_BANK[c, n])
+
+        def with_bias(sums, c, y):
+            nc.scalar.activation(y, sums, IDENT, bias=bias[:, c : c + 1])
+
+        def scaled_on_gpsimd(c, n, slot):
+            y = keep.tile([P, CHUNK], F32, name=f"y{c}_{n}")
+            with_bias(early_sums(c, n), c, y[:])
+            scaled = ring.tile([P, CHUNK], F32, name="scaled", tag=slot, align_bytes=64)
+            nc.gpsimd.tensor_tensor(scaled[:], y[:], router_w[:, CHUNK * n : CHUNK * (n + 1)], MULT)
+            return scaled
+
+        def put_scaled(scaled, c, n):
+            nc.vector.tensor_copy(pages[c][:].indirect(listed(CHUNK * n, CHUNK * (n + 1))), scaled[:])
 
         def put(y, c, j0, j1):
             page = pages[c % 3]
             nc.vector.tensor_tensor(page[:].indirect(listed(j0, j1)), y[:], router_w[:, j0:j1], MULT)
             if j1 == J:
                 nc.sync.dma_start(out[P * c : P * (c + 1), :], page[:])
+
+        def down(c, j0, j1):
+            y = keep.tile([P, j1 - j0], F32, name=f"late_y{c}")
+            for s in range(j0, j1, BANK):
+                with_bias(down_sums(c, s, s + BANK, DOWN_BANK[(c + s // BANK) % 2]), c, y[:, s - j0 : s - j0 + BANK])
+            return y
 
         for blk in range(4):
             gate_pass(blk, 0)
@@ -247,35 +288,37 @@ def tile_list_modp_ggelu_noneb_kernel(
             up_pass(blk, 1)
         gate_block(4)
         product(0)
-        up_block(4)
         product(1)
         product(2)
-        quantise_h(0)
-        rows0_chunk0 = down(0, 0, CHUNK)
-        up_block(5)
-        gate_block(5)
-        gate_block(6)
+        quantise_h(0, 0, CHUNK)
+        first_sums = early_sums(0, 0)
         product(3)
-        up_block(6)
-        product(4)
-        quantise_h(1)
-        zeroed_page("h_bf1")
-        rows0_chunk1 = down(0, CHUNK, 2 * CHUNK)
-        gate_block(7)
-        up_block(7)
-        put(rows0_chunk0, 0, 0, CHUNK)
-        product(5)
-        product(6)
-        quantise_h(2)
-        product(7)
-        rows1_first = down(1, 0, J // 2)
-        put(rows0_chunk1, 0, CHUNK, 2 * CHUNK)
-        quantise_h(3)
-        zeroed_page("h_bf3")
-        rows0_second = down(0, J // 2, J)
-        rows1_second = down(1, J // 2, J)
-        put(rows1_first, 1, 0, J // 2)
-        put(rows0_second, 0, J // 2, J)
-        put(rows1_second, 1, J // 2, J)
-        for c in range(2, N // P):
-            put(down(c, 0, J), c, 0, J)
+        first = keep.tile([P, CHUNK], F32, name="first")
+        nc.vector.scalar_tensor_tensor(first[:], first_sums, bias[:, 0:1], router_w[:, 0:CHUNK], ADD, MULT)
+        quantise_h(1, CHUNK, 2 * CHUNK)
+        put_scaled(first, 0, 0)
+        scaled10 = scaled_on_gpsimd(1, 0, "h_bf1")
+        scaled20 = scaled_on_gpsimd(2, 0, "scaled20")
+        up_block(4)
+        put_scaled(scaled10, 1, 0)
+        product_on_gpsimd(4)
+        gate_block(5)
+        scaled01 = scaled_on_gpsimd(0, 1, "scaled01")
+        scaled11 = scaled_on_gpsimd(1, 1, "scaled11")
+        held_sums = early_sums(2, 1)
+        put_scaled(scaled20, 2, 0)
+        put_scaled(scaled01, 0, 1)
+        put_scaled(scaled11, 1, 1)
+        up_block(5)
+        product_on_gpsimd(5)
+        for blk in (6, 7):
+            gate_block(blk)
+            up_block(blk)
+            product_on_gpsimd(blk)
+        quantise_h(2, J // 2, J)
+        held = ring.tile([P, CHUNK], F32, name="held", tag=f"factors{BLOCKS - 1}")
+        with_bias(held_sums, 2, held[:])
+        put(held, 2, CHUNK, 2 * CHUNK)
+        for c in range(3):
+            put(down(c, J // 2, J), c, J // 2, J)
+        put(down(3, 0, J), 3, 0, J)

@@ -24,12 +24,12 @@ BANK = 512
 BLOCK = 128
 BLOCKS = J // BLOCK
 CHUNK = 2 * BLOCK
-SCALAR_M = (128, 80)
+SCALAR_M = (128, 64)
 SHARED = 32
 GATE_BANK = (0, 1, 2, 3, 0, 1, 2, 5)
-UP_BANK = (4, 5, 6, 7, 7, 4, 0, 3)
-EARLY_DOWN_BANK = {(0, 0): 1, (1, 0): 4, (2, 0): 2, (0, 1): 5, (1, 1): 3, (2, 1): 6}
-DOWN_BANK = (7, 1)
+UP_BANK = (4, 5, 6, 7, 7, 4, 6, 3)
+EARLY_DOWN_BANK = {(0, 0): 1, (1, 0): 4, (0, 1): 5, (1, 1): 3, (0, 2): 1, (1, 2): 7, (0, 3): 1, (1, 3): 4}
+DOWN_BANK = (0, 2)
 VECTOR_BLOCKS = 4
 
 
@@ -116,7 +116,6 @@ def tile_list_modp_ggelu_noneb_kernel(
                 v[a, blk] = picked[:, BLOCK * (blk - blk0) : BLOCK * (blk - blk0 + 1)]
 
         gather_words(0, 0, BLOCKS)
-        zeroed_page("wg_sc_raw")
         zeroed_page("tab0")
 
         wu_both = ring.tile([P, 8 * R - SHARED], BF16, name="wu_both", tag="wu_bf", align_bytes=64)
@@ -152,14 +151,13 @@ def tile_list_modp_ggelu_noneb_kernel(
         nc.sync.dma_start(router_w, wgo)
 
         h_bf = [
-            ring.tile([P, 4 * width], BF16, name="h_bf", tag=f"h_bf{n}", align_bytes=64)
-            for n, width in enumerate((CHUNK, CHUNK, J // 2))
+            ring.tile([P, 4 * CHUNK], BF16, name="h_bf", tag=f"h_bf{min(n, 2)}", align_bytes=64) for n in range(3)
         ]
         h_q = keep.tile([P, J], U32, name="h_q", align_bytes=64)
         h_sc = keep.tile([P, J], U8, name="h_sc", align_bytes=64)
         gel = ring.tile([P, VECTOR_BLOCKS, BANK], F32, name="gel", tag="scale_window", align_bytes=64)
         factors = {
-            blk: ring.tile([P, 2, BANK], F32, name="factors", tag=f"factors{blk}")
+            blk: ring.tile([P, 2, BANK], F32, name="factors", tag=f"factors{blk}", align_bytes=64)
             for blk in range(VECTOR_BLOCKS, BLOCKS)
         }
         ga = {}
@@ -230,9 +228,9 @@ def tile_list_modp_ggelu_noneb_kernel(
             )
 
         def product_on_gpsimd(blk):
-            start = BANK * (blk - VECTOR_BLOCKS)
+            start = BANK * (blk % 2)
             nc.gpsimd.tensor_tensor(
-                h_bf[2][:, start : start + BANK], factors[blk][:, 0, :], factors[blk][:, 1, :], MULT
+                h_bf[blk // 2][:, start : start + BANK], factors[blk][:, 0, :], factors[blk][:, 1, :], MULT
             )
 
         def quantise_h(n, j0, j1):
@@ -264,6 +262,13 @@ def tile_list_modp_ggelu_noneb_kernel(
             nc.gpsimd.tensor_tensor(scaled[:], y[:], router_w[:, CHUNK * n : CHUNK * (n + 1)], MULT)
             return scaled
 
+        def scaled_on_vector(sums, c, n):
+            scaled = keep.tile([P, CHUNK], F32, name=f"scaled{c}_{n}")
+            nc.vector.scalar_tensor_tensor(
+                scaled[:], sums, bias[:, c : c + 1], router_w[:, CHUNK * n : CHUNK * (n + 1)], ADD, MULT
+            )
+            return scaled
+
         def put_scaled(scaled, c, n):
             nc.vector.tensor_copy(pages[c][:].indirect(listed(CHUNK * n, CHUNK * (n + 1))), scaled[:])
 
@@ -293,32 +298,41 @@ def tile_list_modp_ggelu_noneb_kernel(
         quantise_h(0, 0, CHUNK)
         first_sums = early_sums(0, 0)
         product(3)
-        first = keep.tile([P, CHUNK], F32, name="first")
-        nc.vector.scalar_tensor_tensor(first[:], first_sums, bias[:, 0:1], router_w[:, 0:CHUNK], ADD, MULT)
+        first = scaled_on_vector(first_sums, 0, 0)
         quantise_h(1, CHUNK, 2 * CHUNK)
         put_scaled(first, 0, 0)
         scaled10 = scaled_on_gpsimd(1, 0, "h_bf1")
-        scaled20 = scaled_on_gpsimd(2, 0, "scaled20")
         up_block(4)
         put_scaled(scaled10, 1, 0)
         product_on_gpsimd(4)
         gate_block(5)
         scaled01 = scaled_on_gpsimd(0, 1, "scaled01")
-        scaled11 = scaled_on_gpsimd(1, 1, "scaled11")
-        held_sums = early_sums(2, 1)
-        put_scaled(scaled20, 2, 0)
-        put_scaled(scaled01, 0, 1)
-        put_scaled(scaled11, 1, 1)
         up_block(5)
         product_on_gpsimd(5)
-        for blk in (6, 7):
-            gate_block(blk)
-            up_block(blk)
-            product_on_gpsimd(blk)
-        quantise_h(2, J // 2, J)
-        held = ring.tile([P, CHUNK], F32, name="held", tag=f"factors{BLOCKS - 1}")
-        with_bias(held_sums, 2, held[:])
-        put(held, 2, CHUNK, 2 * CHUNK)
-        for c in range(3):
-            put(down(c, J // 2, J), c, J // 2, J)
-        put(down(3, 0, J), 3, 0, J)
+        scaled11 = scaled_on_gpsimd(1, 1, "factors5")
+        put_scaled(scaled01, 0, 1)
+        quantise_h(2, 2 * CHUNK, 3 * CHUNK)
+        put_scaled(scaled11, 1, 1)
+        h_bf.append(ring.tile([P, 4 * CHUNK], BF16, name="h_bf", tag="h_bf2", align_bytes=64))
+        gate_block(6)
+        up_block(6)
+        product_on_gpsimd(6)
+        gate_block(7)
+        up_block(7)
+        scaled02 = scaled_on_vector(early_sums(0, 2), 0, 2)
+        held_sums = early_sums(1, 2)
+        product_on_gpsimd(7)
+        put_scaled(scaled02, 0, 2)
+        quantise_h(3, 3 * CHUNK, J)
+        held = ring.tile([P, CHUNK], F32, name="held", tag=f"factors{BLOCKS - 1}", align_bytes=64)
+        with_bias(held_sums, 1, held[:])
+        put(held, 1, 2 * CHUNK, 3 * CHUNK)
+        page = ring.tile([P, T], F32, name="page", tag="h_bf2", align_bytes=64)
+        nc.gpsimd.memset(page[:].bitcast(I32), 0)
+        pages.append(page)
+        for c in range(2):
+            y = keep.tile([P, CHUNK], F32, name=f"y{c}_3")
+            with_bias(early_sums(c, 3), c, y[:])
+            put(y, c, 3 * CHUNK, J)
+        for c in range(2, N // P):
+            put(down(c, 0, J), c, 0, J)

@@ -24,13 +24,13 @@ BANK = 512
 BLOCK = 128
 BLOCKS = J // BLOCK
 CHUNK = 2 * BLOCK
-SCALAR_M = (128, 64)
+SCALAR_M = (88, 48)
 SHARED = 32
-GATE_BANK = (0, 1, 2, 3, 0, 1, 2, 5)
-UP_BANK = (4, 5, 6, 7, 7, 4, 6, 3)
-EARLY_DOWN_BANK = {(0, 0): 1, (1, 0): 4, (0, 1): 5, (1, 1): 3, (0, 2): 1, (1, 2): 7, (0, 3): 1, (1, 3): 4}
-DOWN_BANK = (0, 2)
-VECTOR_BLOCKS = 4
+GATE_BANK = (0, 1, 2, 3, 0, 1, 4, 1)
+UP_BANK = (4, 5, 6, 7, 5, 7, 2, 7)
+EARLY_DOWN_BANK = {(0, 0): 1, (1, 0): 4, (2, 0): 2, (0, 1): 0, (1, 1): 5, (2, 1): 3}
+DOWN_BANK = (6, 0)
+VECTOR_BLOCKS = 5
 
 
 def tile_list_modp_ggelu_noneb_kernel(
@@ -80,14 +80,13 @@ def tile_list_modp_ggelu_noneb_kernel(
         nc.vector.memset(tab_sc[64:P, :].bitcast(I32), 0)
         nc.gpsimd.memset(v_sc[:].bitcast(I32), 0)
 
-        pages = []
+        pages = [keep.tile([P, T], F32, name="page0")]
+        nc.vector.memset(pages[0][:].bitcast(I32), 0)
 
         def zeroed_page(slot):
             page = ring.tile([P, T], F32, name="page", tag=slot, align_bytes=64)
-            nc.vector.memset(page[:].bitcast(I32), 0)
+            nc.gpsimd.memset(page[:].bitcast(I32), 0)
             pages.append(page)
-
-        zeroed_page("page0")
 
         picked_sc = keep.tile([P, J], U8, name="picked_sc", align_bytes=64)
         nc.vector.tensor_copy(picked_sc[:], tab_sc[:].indirect(offsets[:]))
@@ -116,7 +115,6 @@ def tile_list_modp_ggelu_noneb_kernel(
                 v[a, blk] = picked[:, BLOCK * (blk - blk0) : BLOCK * (blk - blk0 + 1)]
 
         gather_words(0, 0, BLOCKS)
-        zeroed_page("tab0")
 
         wu_both = ring.tile([P, 8 * R - SHARED], BF16, name="wu_both", tag="wu_bf", align_bytes=64)
         wu_bf = [wu_both[:, 4 * R - SHARED :], wu_both[:, 0 : 4 * R]]
@@ -126,8 +124,7 @@ def tile_list_modp_ggelu_noneb_kernel(
             rounded = wu_bf[a].rearrange("p (t m i) -> p m i t", t=4, i=4)
             dealt = wu_raw[a][:].rearrange("p i (m t) -> p m i t", t=4)
             nc.scalar.copy(rounded[:, 0 : SCALAR_M[a]], dealt[:, 0 : SCALAR_M[a]])
-            if SCALAR_M[a] < P:
-                nc.vector.tensor_copy(rounded[:, SCALAR_M[a] : P], dealt[:, SCALAR_M[a] : P])
+            nc.vector.tensor_copy(rounded[:, SCALAR_M[a] : P], dealt[:, SCALAR_M[a] : P])
             nc.vector.quantize_mx(out=wu_q[a][:].bitcast(FP8X4), scales=wu_sc[a][:], in_=wu_bf[a])
 
         for blk in range(0, BLOCKS, CHUNK // BLOCK):
@@ -151,9 +148,10 @@ def tile_list_modp_ggelu_noneb_kernel(
         nc.sync.dma_start(router_w, wgo)
 
         h_bf = [
-            ring.tile([P, 4 * CHUNK], BF16, name="h_bf", tag=f"h_bf{min(n, 2)}", align_bytes=64) for n in range(3)
+            ring.tile([P, 4 * width], BF16, name="h_bf", tag=f"h_bf{n}", align_bytes=64)
+            for n, width in enumerate((CHUNK, CHUNK, J // 2))
         ]
-        h_q = keep.tile([P, J], U32, name="h_q", align_bytes=64)
+        h_q = {}
         h_sc = keep.tile([P, J], U8, name="h_sc", align_bytes=64)
         gel = ring.tile([P, VECTOR_BLOCKS, BANK], F32, name="gel", tag="scale_window", align_bytes=64)
         factors = {
@@ -218,49 +216,42 @@ def tile_list_modp_ggelu_noneb_kernel(
             for a in range(PASSES):
                 up_pass(blk, a)
 
+        def h_block(blk):
+            n = min(blk // 2, 2)
+            return h_bf[n][:, BANK * (blk - 2 * n) : BANK * (blk - 2 * n + 1)]
+
         def product(blk):
-            start = BANK * (blk % 2)
             nc.vector.tensor_tensor(
-                h_bf[blk // 2][:, start : start + BANK].rearrange(by_token, t=4, e=2),
+                h_block(blk).rearrange(by_token, t=4, e=2),
                 ub[blk][:].rearrange(from_bank, t=4, e=2),
                 gel[:, blk, :].rearrange(by_pairs, t=4, e=2),
                 MULT,
             )
 
         def product_on_gpsimd(blk):
-            start = BANK * (blk % 2)
-            nc.gpsimd.tensor_tensor(
-                h_bf[blk // 2][:, start : start + BANK], factors[blk][:, 0, :], factors[blk][:, 1, :], MULT
-            )
+            nc.gpsimd.tensor_tensor(h_block(blk), factors[blk][:, 0, :], factors[blk][:, 1, :], MULT)
 
         def quantise_h(n, j0, j1):
-            nc.vector.quantize_mx(out=h_q[:, j0:j1].bitcast(FP8X4), scales=h_sc[:, j0:j1], in_=h_bf[n][:])
+            h_q[j0] = ring.tile([P, j1 - j0], U32, name="h_q", tag=f"h_q{n}", align_bytes=64)
+            nc.vector.quantize_mx(out=h_q[j0][:].bitcast(FP8X4), scales=h_sc[:, j0:j1], in_=h_bf[n][:])
 
-        def down_sums(c, j0, j1, n):
-            sums = bank(n)
+        def down_sums(c, j0, j1, sums):
             nc.tensor.matmul_mx(
-                out=sums[:, 0 : j1 - j0],
+                out=sums,
                 lhsT=wd[:, 2 * P * c : 2 * P * (c + 1)].bitcast(FP4X4),
                 lhsT_scale=wd_sc[:, P * c : P * (c + 1)],
-                rhs=h_q[:, j0:j1].bitcast(FP8X4),
+                rhs=h_q[j0][:].bitcast(FP8X4),
                 rhs_scale=h_sc[:, j0:j1],
                 start=True,
                 stop=True,
             )
-            return sums[:, 0 : j1 - j0]
+            return sums
 
         def early_sums(c, n):
-            return down_sums(c, CHUNK * n, CHUNK * (n + 1), EARLY_DOWN_BANK[c, n])
+            return down_sums(c, CHUNK * n, CHUNK * (n + 1), bank(EARLY_DOWN_BANK[c, n])[:, 0:CHUNK])
 
         def with_bias(sums, c, y):
             nc.scalar.activation(y, sums, IDENT, bias=bias[:, c : c + 1])
-
-        def scaled_on_gpsimd(c, n, slot):
-            y = keep.tile([P, CHUNK], F32, name=f"y{c}_{n}")
-            with_bias(early_sums(c, n), c, y[:])
-            scaled = ring.tile([P, CHUNK], F32, name="scaled", tag=slot, align_bytes=64)
-            nc.gpsimd.tensor_tensor(scaled[:], y[:], router_w[:, CHUNK * n : CHUNK * (n + 1)], MULT)
-            return scaled
 
         def scaled_on_vector(sums, c, n):
             scaled = keep.tile([P, CHUNK], F32, name=f"scaled{c}_{n}")
@@ -269,20 +260,29 @@ def tile_list_modp_ggelu_noneb_kernel(
             )
             return scaled
 
+        def biased(c, n, slot):
+            y = ring.tile([P, CHUNK], F32, name="y", tag=slot, align_bytes=64)
+            with_bias(early_sums(c, n), c, y[:])
+            return y[:]
+
         def put_scaled(scaled, c, n):
             nc.vector.tensor_copy(pages[c][:].indirect(listed(CHUNK * n, CHUNK * (n + 1))), scaled[:])
 
         def put(y, c, j0, j1):
             page = pages[c % 3]
-            nc.vector.tensor_tensor(page[:].indirect(listed(j0, j1)), y[:], router_w[:, j0:j1], MULT)
+            nc.vector.tensor_tensor(page[:].indirect(listed(j0, j1)), y, router_w[:, j0:j1], MULT)
             if j1 == J:
                 nc.sync.dma_start(out[P * c : P * (c + 1), :], page[:])
 
         def down(c, j0, j1):
             y = keep.tile([P, j1 - j0], F32, name=f"late_y{c}")
             for s in range(j0, j1, BANK):
-                with_bias(down_sums(c, s, s + BANK, DOWN_BANK[(c + s // BANK) % 2]), c, y[:, s - j0 : s - j0 + BANK])
-            return y
+                sums = bank(DOWN_BANK[(c + s // BANK) % 2])
+                starts = [j for j in h_q if s <= j < s + BANK]
+                for a0, a1 in zip(starts, starts[1:] + [s + BANK]):
+                    down_sums(c, a0, a1, sums[:, a0 - s : a1 - s])
+                with_bias(sums[:], c, y[:, s - j0 : s - j0 + BANK])
+            return y[:]
 
         for blk in range(4):
             gate_pass(blk, 0)
@@ -292,47 +292,36 @@ def tile_list_modp_ggelu_noneb_kernel(
             gate_pass(blk, 1)
             up_pass(blk, 1)
         gate_block(4)
+        up_block(4)
         product(0)
         product(1)
         product(2)
         quantise_h(0, 0, CHUNK)
-        first_sums = early_sums(0, 0)
+        zeroed_page("h_bf0")
+        y00 = biased(0, 0, "h_q1")
+        sums20 = early_sums(2, 0)
+        y10 = biased(1, 0, "y10")
         product(3)
-        first = scaled_on_vector(first_sums, 0, 0)
+        product(4)
+        scaled20 = scaled_on_vector(sums20, 2, 0)
+        put(y00, 0, 0, CHUNK)
         quantise_h(1, CHUNK, 2 * CHUNK)
-        put_scaled(first, 0, 0)
-        scaled10 = scaled_on_gpsimd(1, 0, "h_bf1")
-        up_block(4)
-        put_scaled(scaled10, 1, 0)
-        product_on_gpsimd(4)
-        gate_block(5)
-        scaled01 = scaled_on_gpsimd(0, 1, "scaled01")
-        up_block(5)
-        product_on_gpsimd(5)
-        scaled11 = scaled_on_gpsimd(1, 1, "factors5")
+        zeroed_page("h_bf1")
+        put(y10, 1, 0, CHUNK)
+        scaled01 = scaled_on_vector(early_sums(0, 1), 0, 1)
+        scaled11 = scaled_on_vector(early_sums(1, 1), 1, 1)
+        held_sums = early_sums(2, 1)
         put_scaled(scaled01, 0, 1)
-        quantise_h(2, 2 * CHUNK, 3 * CHUNK)
         put_scaled(scaled11, 1, 1)
-        h_bf.append(ring.tile([P, 4 * CHUNK], BF16, name="h_bf", tag="h_bf2", align_bytes=64))
-        gate_block(6)
-        up_block(6)
-        product_on_gpsimd(6)
-        gate_block(7)
-        up_block(7)
-        scaled02 = scaled_on_vector(early_sums(0, 2), 0, 2)
-        held_sums = early_sums(1, 2)
-        product_on_gpsimd(7)
-        put_scaled(scaled02, 0, 2)
-        quantise_h(3, 3 * CHUNK, J)
+        put_scaled(scaled20, 2, 0)
+        for blk in range(VECTOR_BLOCKS, BLOCKS):
+            gate_block(blk)
+            up_block(blk)
+            product_on_gpsimd(blk)
+        quantise_h(2, J // 2, J)
         held = ring.tile([P, CHUNK], F32, name="held", tag=f"factors{BLOCKS - 1}", align_bytes=64)
-        with_bias(held_sums, 1, held[:])
-        put(held, 1, 2 * CHUNK, 3 * CHUNK)
-        page = ring.tile([P, T], F32, name="page", tag="h_bf2", align_bytes=64)
-        nc.gpsimd.memset(page[:].bitcast(I32), 0)
-        pages.append(page)
-        for c in range(2):
-            y = keep.tile([P, CHUNK], F32, name=f"y{c}_3")
-            with_bias(early_sums(c, 3), c, y[:])
-            put(y, c, 3 * CHUNK, J)
-        for c in range(2, N // P):
-            put(down(c, 0, J), c, 0, J)
+        with_bias(held_sums, 2, held[:])
+        put(held[:], 2, CHUNK, 2 * CHUNK)
+        for c in range(3):
+            put(down(c, J // 2, J), c, J // 2, J)
+        put(down(3, 0, J), 3, 0, J)

@@ -40,6 +40,7 @@ def tile_list_modp_ggelu_noneb_kernel(
     with ExitStack() as ctx:
         keep = ctx.enter_context(tc.tile_pool(name="keep", bufs=1))
         ring = ctx.enter_context(tc.tile_pool(name="ring", bufs=1))
+        placed = ctx.enter_context(tc.tile_pool(name="placed", bufs=1))
         psum = ctx.enter_context(tc.psum_pool(name="psum", bufs=1))
 
         offsets = keep.tile([P, J // 16], U16, name="offsets")
@@ -48,7 +49,8 @@ def tile_list_modp_ggelu_noneb_kernel(
         def listed(j0, j1):
             return offsets[:, j0 // 16 : j1 // 16]
 
-        tab_sc = ring.tile([P, T], U8, name="tab_sc", tag="scale_window", align_bytes=64)
+        tab_sc_tile = placed.tile([P, T + 64], U8, name="tab_sc", align_bytes=64, offset=0)
+        tab_sc = tab_sc_tile[:, 0:T]
         nc.sync.dma_start(tab_sc[0:32, :].bitcast(I32), tab_scales.rearrange("a g t -> g a t").bitcast(I32))
         wg_raw = ring.tile([P, PASSES * 2 * R], U8, name="wg_raw", tag="wg_raw", align_bytes=64)
         nc.sync.dma_start(
@@ -61,13 +63,15 @@ def tile_list_modp_ggelu_noneb_kernel(
             nc.sync.dma_start(words[:], tab_words[a].rearrange("p t i -> p (t i)").bitcast(I32))
             return words
 
-        def load_wu(a, slot):
-            raw = ring.tile([P, 4, R], F32, name="wu_raw", tag=slot, align_bytes=64)
+        def load_wu(a, raw):
             nc.sync.dma_start(raw[:], wu[512 * a : 512 * (a + 1), :].rearrange("(p i) r -> p i r", i=4))
             return raw
 
+        warm = keep.tile([P, 2], F32, name="warm")
+        nc.gpsimd.memset(warm[:, 0:1], 0.0)
+        nc.scalar.activation(warm[:, 1:2], warm[:, 0:1], GELU)
+
         wg_sc_raw = ring.tile([P, PASSES * R], U8, name="wg_sc_raw", tag="wg_sc_raw", align_bytes=64)
-        v_sc = keep.tile([P, PASSES * J], U8, name="v_sc", align_bytes=64)
         nc.gpsimd.memset(wg_sc_raw[:].bitcast(I32), 0)
         for q in range(4):
             nc.sync.dma_start(
@@ -75,10 +79,9 @@ def tile_list_modp_ggelu_noneb_kernel(
                 wg_scales[:, 4 * q : 4 * q + 4, :].rearrange("a g n -> g a n").bitcast(I32),
             )
         tab = [load_tab(0, "tab0")]
-        wu_raw = [load_wu(0, "wu0")]
+        wu_raw = [load_wu(0, ring.tile([P, 4, R], F32, name="wu_raw", tag="wu0", align_bytes=64))]
         nc.vector.memset(tab_sc[32:64, :].bitcast(I32), 0)
         nc.vector.memset(tab_sc[64:P, :].bitcast(I32), 0)
-        nc.gpsimd.memset(v_sc[:].bitcast(I32), 0)
 
         pages = [keep.tile([P, T], F32, name="page0")]
         nc.vector.memset(pages[0][:].bitcast(I32), 0)
@@ -89,10 +92,11 @@ def tile_list_modp_ggelu_noneb_kernel(
             pages.append(page)
 
         picked_sc = keep.tile([P, J], U8, name="picked_sc", align_bytes=64)
-        nc.vector.tensor_copy(picked_sc[:], tab_sc[:].indirect(offsets[:]))
+        nc.vector.tensor_copy(picked_sc[:], tab_sc.indirect(offsets[:]))
+        v_sc = placed.tile([P, PASSES * J], U8, name="v_sc", align_bytes=64, offset=0)
         for q in range(4):
             nc.sync.dma_start(v_sc[32 * q : 32 * q + 4, :].bitcast(I32), picked_sc[8 * q : 8 * q + 8, :].bitcast(I32))
-        wu_raw.append(load_wu(1, "scale_window"))
+        wu_raw.append(load_wu(1, placed.tile([P, 4, R], F32, name="wu_raw1", align_bytes=64, offset=T)))
 
         wg = keep.tile([P, PASSES * 2 * R], U8, name="wg", align_bytes=64)
         nc.vector.tensor_copy(
@@ -114,7 +118,8 @@ def tile_list_modp_ggelu_noneb_kernel(
             for blk in range(blk0, blk1):
                 v[a, blk] = picked[:, BLOCK * (blk - blk0) : BLOCK * (blk - blk0 + 1)]
 
-        gather_words(0, 0, BLOCKS)
+        gather_words(0, 0, 2)
+        gather_words(0, 2, 4)
 
         wu_both = ring.tile([P, 8 * R - SHARED], BF16, name="wu_both", tag="wu_bf", align_bytes=64)
         wu_bf = [wu_both[:, 4 * R - SHARED :], wu_both[:, 0 : 4 * R]]
@@ -125,6 +130,8 @@ def tile_list_modp_ggelu_noneb_kernel(
             dealt = wu_raw[a][:].rearrange("p i (m t) -> p m i t", t=4)
             nc.scalar.copy(rounded[:, 0 : SCALAR_M[a]], dealt[:, 0 : SCALAR_M[a]])
             nc.vector.tensor_copy(rounded[:, SCALAR_M[a] : P], dealt[:, SCALAR_M[a] : P])
+            if a == 0:
+                gather_words(0, BLOCKS // 2, BLOCKS)
             nc.vector.quantize_mx(out=wu_q[a][:].bitcast(FP8X4), scales=wu_sc[a][:], in_=wu_bf[a])
 
         for blk in range(0, BLOCKS, CHUNK // BLOCK):
@@ -134,7 +141,6 @@ def tile_list_modp_ggelu_noneb_kernel(
         wd = wd_bytes[:, 0 : 2 * N]
         wd_sc = wd_bytes[:, 2 * N : 3 * N]
         nc.sync.dma_start(wd.bitcast(I32), wd_words[0].bitcast(I32))
-        nc.gpsimd.memset(wd_sc.bitcast(I32), 0)
         for q in range(4):
             nc.sync.dma_start(
                 wd_bytes[32 * q : 32 * q + 4, 2 * N : 3 * N].bitcast(I32),
@@ -153,7 +159,7 @@ def tile_list_modp_ggelu_noneb_kernel(
         ]
         h_q = {}
         h_sc = keep.tile([P, J], U8, name="h_sc", align_bytes=64)
-        gel = ring.tile([P, VECTOR_BLOCKS, BANK], F32, name="gel", tag="scale_window", align_bytes=64)
+        gel = placed.tile([P, VECTOR_BLOCKS, BANK], F32, name="gel", align_bytes=64, offset=T)
         factors = {
             blk: ring.tile([P, 2, BANK], F32, name="factors", tag=f"factors{blk}", align_bytes=64)
             for blk in range(VECTOR_BLOCKS, BLOCKS)

@@ -24,13 +24,16 @@ BANK = 512
 BLOCK = 128
 BLOCKS = J // BLOCK
 CHUNK = 2 * BLOCK
+HALF = J // 2
+PAGES = 3
 SCALAR_M = (88, 48)
 SHARED = 32
+SPARE = 64
+VECTOR_BLOCKS = 5
 GATE_BANK = (0, 1, 2, 3, 0, 1, 4, 1)
 UP_BANK = (4, 5, 6, 7, 5, 7, 2, 7)
 EARLY_DOWN_BANK = {(0, 0): 1, (1, 0): 4, (2, 0): 2, (0, 1): 0, (1, 1): 5, (2, 1): 3}
-DOWN_BANK = (6, 0)
-VECTOR_BLOCKS = 5
+LATE_DOWN_BANK = (6, 0)
 
 
 def tile_list_modp_ggelu_noneb_kernel(
@@ -49,7 +52,7 @@ def tile_list_modp_ggelu_noneb_kernel(
         def listed(j0, j1):
             return offsets[:, j0 // 16 : j1 // 16]
 
-        tab_sc_tile = placed.tile([P, T + 64], U8, name="tab_sc", align_bytes=64, offset=0)
+        tab_sc_tile = placed.tile([P, T + SPARE], U8, name="tab_sc", align_bytes=64, offset=0)
         tab_sc = tab_sc_tile[:, 0:T]
         nc.sync.dma_start(tab_sc[0:32, :].bitcast(I32), tab_scales.rearrange("a g t -> g a t").bitcast(I32))
         wg_raw = ring.tile([P, PASSES * 2 * R], U8, name="wg_raw", tag="wg_raw", align_bytes=64)
@@ -66,10 +69,6 @@ def tile_list_modp_ggelu_noneb_kernel(
         def load_wu(a, raw):
             nc.sync.dma_start(raw[:], wu[512 * a : 512 * (a + 1), :].rearrange("(p i) r -> p i r", i=4))
             return raw
-
-        warm = keep.tile([P, 2], F32, name="warm")
-        nc.gpsimd.memset(warm[:, 0:1], 0.0)
-        nc.scalar.activation(warm[:, 1:2], warm[:, 0:1], GELU)
 
         wg_sc_raw = ring.tile([P, PASSES * R], U8, name="wg_sc_raw", tag="wg_sc_raw", align_bytes=64)
         nc.gpsimd.memset(wg_sc_raw[:].bitcast(I32), 0)
@@ -118,8 +117,8 @@ def tile_list_modp_ggelu_noneb_kernel(
             for blk in range(blk0, blk1):
                 v[a, blk] = picked[:, BLOCK * (blk - blk0) : BLOCK * (blk - blk0 + 1)]
 
-        gather_words(0, 0, 2)
-        gather_words(0, 2, 4)
+        for blk in range(0, BLOCKS // 2, CHUNK // BLOCK):
+            gather_words(0, blk, blk + CHUNK // BLOCK)
 
         wu_both = ring.tile([P, 8 * R - SHARED], BF16, name="wu_both", tag="wu_bf", align_bytes=64)
         wu_bf = [wu_both[:, 4 * R - SHARED :], wu_both[:, 0 : 4 * R]]
@@ -155,7 +154,7 @@ def tile_list_modp_ggelu_noneb_kernel(
 
         h_bf = [
             ring.tile([P, 4 * width], BF16, name="h_bf", tag=f"h_bf{n}", align_bytes=64)
-            for n, width in enumerate((CHUNK, CHUNK, J // 2))
+            for n, width in enumerate((CHUNK, CHUNK, HALF))
         ]
         h_q = {}
         h_sc = keep.tile([P, J], U8, name="h_sc", align_bytes=64)
@@ -275,7 +274,7 @@ def tile_list_modp_ggelu_noneb_kernel(
             nc.vector.tensor_copy(pages[c][:].indirect(listed(CHUNK * n, CHUNK * (n + 1))), scaled[:])
 
         def put(y, c, j0, j1):
-            page = pages[c % 3]
+            page = pages[c % PAGES]
             nc.vector.tensor_tensor(page[:].indirect(listed(j0, j1)), y, router_w[:, j0:j1], MULT)
             if j1 == J:
                 nc.sync.dma_start(out[P * c : P * (c + 1), :], page[:])
@@ -283,18 +282,18 @@ def tile_list_modp_ggelu_noneb_kernel(
         def down(c, j0, j1):
             y = keep.tile([P, j1 - j0], F32, name=f"late_y{c}")
             for s in range(j0, j1, BANK):
-                sums = bank(DOWN_BANK[(c + s // BANK) % 2])
+                sums = bank(LATE_DOWN_BANK[(c + s // BANK) % 2])
                 starts = [j for j in h_q if s <= j < s + BANK]
                 for a0, a1 in zip(starts, starts[1:] + [s + BANK]):
                     down_sums(c, a0, a1, sums[:, a0 - s : a1 - s])
                 with_bias(sums[:], c, y[:, s - j0 : s - j0 + BANK])
             return y[:]
 
-        for blk in range(4):
+        for blk in range(BLOCKS // 2):
             gate_pass(blk, 0)
-        for blk in range(4):
+        for blk in range(BLOCKS // 2):
             up_pass(blk, 0)
-        for blk in range(4):
+        for blk in range(BLOCKS // 2):
             gate_pass(blk, 1)
             up_pass(blk, 1)
         gate_block(4)
@@ -311,12 +310,12 @@ def tile_list_modp_ggelu_noneb_kernel(
         product(4)
         scaled20 = scaled_on_vector(sums20, 2, 0)
         put(y00, 0, 0, CHUNK)
-        quantise_h(1, CHUNK, 2 * CHUNK)
+        quantise_h(1, CHUNK, HALF)
         zeroed_page("h_bf1")
         put(y10, 1, 0, CHUNK)
         scaled01 = scaled_on_vector(early_sums(0, 1), 0, 1)
         scaled11 = scaled_on_vector(early_sums(1, 1), 1, 1)
-        held_sums = early_sums(2, 1)
+        sums21 = early_sums(2, 1)
         put_scaled(scaled01, 0, 1)
         put_scaled(scaled11, 1, 1)
         put_scaled(scaled20, 2, 0)
@@ -324,10 +323,10 @@ def tile_list_modp_ggelu_noneb_kernel(
             gate_block(blk)
             up_block(blk)
             product_on_gpsimd(blk)
-        quantise_h(2, J // 2, J)
-        held = ring.tile([P, CHUNK], F32, name="held", tag=f"factors{BLOCKS - 1}", align_bytes=64)
-        with_bias(held_sums, 2, held[:])
-        put(held[:], 2, CHUNK, 2 * CHUNK)
-        for c in range(3):
-            put(down(c, J // 2, J), c, J // 2, J)
-        put(down(3, 0, J), 3, 0, J)
+        quantise_h(2, HALF, J)
+        y21 = ring.tile([P, CHUNK], F32, name="y21", tag=f"factors{BLOCKS - 1}", align_bytes=64)
+        with_bias(sums21, 2, y21[:])
+        put(y21[:], 2, CHUNK, HALF)
+        for c in range(PAGES):
+            put(down(c, HALF, J), c, HALF, J)
+        put(down(PAGES, 0, J), PAGES, 0, J)

@@ -26,14 +26,18 @@ BLOCKS = J // BLOCK
 CHUNK = 2 * BLOCK
 HALF = J // 2
 PAGES = 3
-SCALAR_M = (88, 48)
+SCALAR_M = (80, 56)
 SHARED = 32
-SPARE = 64
-VECTOR_BLOCKS = 5
-GATE_BANK = (0, 1, 2, 3, 0, 1, 4, 1)
-UP_BANK = (4, 5, 6, 7, 5, 7, 2, 7)
-EARLY_DOWN_BANK = {(0, 0): 1, (1, 0): 4, (2, 0): 2, (0, 1): 0, (1, 1): 5, (2, 1): 3}
-LATE_DOWN_BANK = (6, 0)
+VECTOR_BLOCKS = 4
+GATE_BANK = (0, 1, 2, 3, 0, 2, 7, 2)
+UP_BANK = (4, 5, 6, 7, 1, 6, 0, 1)
+EARLY_DOWN_BANK = ((0, 1, 2), (3, 4, 5))
+LATE_DOWN_BANK = (3, 4)
+AT_WU_BF = T
+AT_GEL0 = AT_WU_BF + 16 * R
+AT_H = AT_GEL0 + 4 * BANK
+OVERLAP = 64
+AT_WG_SC = AT_H + 32 * CHUNK + 8 * BLOCK
 
 
 def tile_list_modp_ggelu_noneb_kernel(
@@ -52,17 +56,20 @@ def tile_list_modp_ggelu_noneb_kernel(
         def listed(j0, j1):
             return offsets[:, j0 // 16 : j1 // 16]
 
-        tab_sc_tile = placed.tile([P, T + SPARE], U8, name="tab_sc", align_bytes=64, offset=0)
-        tab_sc = tab_sc_tile[:, 0:T]
-        nc.sync.dma_start(tab_sc[0:32, :].bitcast(I32), tab_scales.rearrange("a g t -> g a t").bitcast(I32))
-        wg_raw = ring.tile([P, PASSES * 2 * R], U8, name="wg_raw", tag="wg_raw", align_bytes=64)
+        wg_raw = keep.tile([P, PASSES * 2 * R], U8, name="wg_raw", align_bytes=64)
         nc.sync.dma_start(
             wg_raw[:].bitcast(I32).rearrange("p (a n) -> p a n", a=PASSES),
             wg_words.rearrange("a p n -> p a n").bitcast(I32),
         )
+        tab_sc = placed.tile([P, T], U8, name="tab_sc", align_bytes=64, offset=0)
+        nc.vector.memset(tab_sc[:].bitcast(I32), 0)
+        for q in range(4):
+            nc.sync.dma_start(
+                tab_sc[32 * q : 32 * q + 8, :].bitcast(I32), tab_scales[:, 4 * q : 4 * q + 4, :].bitcast(I32)
+            )
 
-        def load_tab(a, slot):
-            words = ring.tile([P, T], I32, name="tab", tag=slot, align_bytes=64)
+        def load_tab(a):
+            words = keep.tile([P, T], I32, name=f"tab{a}", align_bytes=64)
             nc.sync.dma_start(words[:], tab_words[a].rearrange("p t i -> p (t i)").bitcast(I32))
             return words
 
@@ -70,57 +77,61 @@ def tile_list_modp_ggelu_noneb_kernel(
             nc.sync.dma_start(raw[:], wu[512 * a : 512 * (a + 1), :].rearrange("(p i) r -> p i r", i=4))
             return raw
 
-        wg_sc_raw = ring.tile([P, PASSES * R], U8, name="wg_sc_raw", tag="wg_sc_raw", align_bytes=64)
+        tab = [load_tab(0)]
+        wg_sc_raw = placed.tile([P, PASSES * R], U8, name="wg_sc_raw", align_bytes=64, offset=AT_WG_SC)
         nc.gpsimd.memset(wg_sc_raw[:].bitcast(I32), 0)
         for q in range(4):
             nc.sync.dma_start(
                 wg_sc_raw[32 * q : 32 * q + 4, :].bitcast(I32).rearrange("p (a n) -> p a n", a=PASSES),
                 wg_scales[:, 4 * q : 4 * q + 4, :].rearrange("a g n -> g a n").bitcast(I32),
             )
-        tab = [load_tab(0, "tab0")]
-        wu_raw = [load_wu(0, ring.tile([P, 4, R], F32, name="wu_raw", tag="wu0", align_bytes=64))]
-        nc.vector.memset(tab_sc[32:64, :].bitcast(I32), 0)
-        nc.vector.memset(tab_sc[64:P, :].bitcast(I32), 0)
+        wu_raw = [
+            load_wu(0, ring.tile([P, 4, R], F32, name="wu_raw", tag="wu0", align_bytes=64)),
+            load_wu(1, keep.tile([P, 4, R], F32, name="wu_raw1", align_bytes=64)),
+        ]
+        tab.append(load_tab(1))
 
-        pages = [keep.tile([P, T], F32, name="page0")]
-        nc.vector.memset(pages[0][:].bitcast(I32), 0)
-
-        def zeroed_page(slot):
-            page = ring.tile([P, T], F32, name="page", tag=slot, align_bytes=64)
-            nc.gpsimd.memset(page[:].bitcast(I32), 0)
-            pages.append(page)
+        pages = [keep.tile([P, T], F32, name=f"page{c}") for c in range(PAGES)]
+        for page in pages:
+            nc.vector.memset(page[:].bitcast(I32), 0)
 
         picked_sc = keep.tile([P, J], U8, name="picked_sc", align_bytes=64)
-        nc.vector.tensor_copy(picked_sc[:], tab_sc.indirect(offsets[:]))
-        v_sc = placed.tile([P, PASSES * J], U8, name="v_sc", align_bytes=64, offset=0)
+        nc.vector.tensor_copy(picked_sc[:], tab_sc[:].indirect(offsets[:]))
+        moved_sc = placed.tile([P, J], U8, name="moved_sc", align_bytes=64, offset=0)
         for q in range(4):
-            nc.sync.dma_start(v_sc[32 * q : 32 * q + 4, :].bitcast(I32), picked_sc[8 * q : 8 * q + 8, :].bitcast(I32))
-        wu_raw.append(load_wu(1, placed.tile([P, 4, R], F32, name="wu_raw1", align_bytes=64, offset=T)))
+            nc.sync.dma_start(
+                moved_sc[32 * q : 32 * q + 4, :].bitcast(I32), picked_sc[32 * q + 4 : 32 * q + 8, :].bitcast(I32)
+            )
+        v_sc = [picked_sc, moved_sc]
 
         wg = keep.tile([P, PASSES * 2 * R], U8, name="wg", align_bytes=64)
-        nc.vector.tensor_copy(
+        nc.scalar.copy(
             wg[:].bitcast(U16).rearrange("p (a t m) -> p a t m", a=PASSES, t=4),
             wg_raw[:].bitcast(U16).rearrange("p (a m t) -> p a t m", a=PASSES, t=4),
         )
-        tab.append(load_tab(1, "wg_raw"))
+
+        v = {}
+
+        def gather_words(a, blk0, blk1, at=None):
+            shape = [P, BLOCK * (blk1 - blk0)]
+            if at is None:
+                picked = keep.tile(shape, U32, name=f"v{a}_{blk0}", align_bytes=64)
+            else:
+                picked = placed.tile(shape, U32, name=f"v{a}_{blk0}", align_bytes=64, offset=at)
+            nc.vector.tensor_copy(picked[:], tab[a][:].bitcast(U32).indirect(listed(BLOCK * blk0, BLOCK * blk1)))
+            for blk in range(blk0, blk1):
+                v[a, blk] = picked[:, BLOCK * (blk - blk0) : BLOCK * (blk - blk0 + 1)]
+
+        gather_words(0, 0, 2)
         wg_sc = keep.tile([P, PASSES * R], U8, name="wg_sc", align_bytes=64)
         nc.vector.tensor_copy(
             wg_sc[:].rearrange("p (a t m) -> p a t m", a=PASSES, t=4),
             wg_sc_raw[:].rearrange("p (a m t) -> p a t m", a=PASSES, t=4),
         )
+        gather_words(0, 2, 4, AT_WG_SC - 8 * BLOCK + OVERLAP)
+        gather_words(0, 4, 8, AT_WG_SC + OVERLAP)
 
-        v = {}
-
-        def gather_words(a, blk0, blk1):
-            picked = keep.tile([P, BLOCK * (blk1 - blk0)], U32, name=f"v{a}_{blk0}", align_bytes=64)
-            nc.vector.tensor_copy(picked[:], tab[a][:].bitcast(U32).indirect(listed(BLOCK * blk0, BLOCK * blk1)))
-            for blk in range(blk0, blk1):
-                v[a, blk] = picked[:, BLOCK * (blk - blk0) : BLOCK * (blk - blk0 + 1)]
-
-        for blk in range(0, BLOCKS // 2, CHUNK // BLOCK):
-            gather_words(0, blk, blk + CHUNK // BLOCK)
-
-        wu_both = ring.tile([P, 8 * R - SHARED], BF16, name="wu_both", tag="wu_bf", align_bytes=64)
+        wu_both = placed.tile([P, 8 * R - SHARED], BF16, name="wu_both", align_bytes=64, offset=AT_WU_BF)
         wu_bf = [wu_both[:, 4 * R - SHARED :], wu_both[:, 0 : 4 * R]]
         wu_q = [keep.tile([P, R], U32, name=f"wu_q{a}", align_bytes=64) for a in range(PASSES)]
         wu_sc = [keep.tile([P, R], U8, name=f"wu_sc{a}", align_bytes=64) for a in range(PASSES)]
@@ -129,12 +140,10 @@ def tile_list_modp_ggelu_noneb_kernel(
             dealt = wu_raw[a][:].rearrange("p i (m t) -> p m i t", t=4)
             nc.scalar.copy(rounded[:, 0 : SCALAR_M[a]], dealt[:, 0 : SCALAR_M[a]])
             nc.vector.tensor_copy(rounded[:, SCALAR_M[a] : P], dealt[:, SCALAR_M[a] : P])
-            if a == 0:
-                gather_words(0, BLOCKS // 2, BLOCKS)
             nc.vector.quantize_mx(out=wu_q[a][:].bitcast(FP8X4), scales=wu_sc[a][:], in_=wu_bf[a])
 
-        for blk in range(0, BLOCKS, CHUNK // BLOCK):
-            gather_words(1, blk, blk + CHUNK // BLOCK)
+        for blk0, blk1 in ((0, 1), (1, 2), (2, 4), (4, 6)):
+            gather_words(1, blk0, blk1, AT_WU_BF + 4 * BLOCK * blk0)
 
         wd_bytes = ring.tile([P, 3 * N], U8, name="wd_bytes", tag="wu0", align_bytes=64)
         wd = wd_bytes[:, 0 : 2 * N]
@@ -145,7 +154,7 @@ def tile_list_modp_ggelu_noneb_kernel(
                 wd_bytes[32 * q : 32 * q + 4, 2 * N : 3 * N].bitcast(I32),
                 wd_scales[0, 4 * q : 4 * q + 4, :].bitcast(I32),
             )
-        epilogue = ring.tile([P, J + N // P], F32, name="epilogue", tag="wu_bf", align_bytes=64)
+        epilogue = placed.tile([P, J + N // P], F32, name="epilogue", align_bytes=64, offset=AT_WU_BF + 4 * BLOCK * 6)
         router_w = epilogue[:, 0:J]
         bias = epilogue[:, J : J + N // P]
         with nc.allow_non_contiguous_dma(reason="one bias value a partition"):
@@ -153,12 +162,14 @@ def tile_list_modp_ggelu_noneb_kernel(
         nc.sync.dma_start(router_w, wgo)
 
         h_bf = [
-            ring.tile([P, 4 * width], BF16, name="h_bf", tag=f"h_bf{n}", align_bytes=64)
+            placed.tile([P, 4 * width], BF16, name=f"h_bf{n}", align_bytes=64, offset=AT_H + n * (8 * CHUNK - OVERLAP))
             for n, width in enumerate((CHUNK, CHUNK, HALF))
         ]
         h_q = {}
         h_sc = keep.tile([P, J], U8, name="h_sc", align_bytes=64)
-        gel = placed.tile([P, VECTOR_BLOCKS, BANK], F32, name="gel", align_bytes=64, offset=T)
+        gel = [placed.tile([P, BANK], F32, name="gel0", align_bytes=64, offset=AT_GEL0)] + [
+            keep.tile([P, BANK], F32, name=f"gel{blk}", align_bytes=64) for blk in range(1, VECTOR_BLOCKS)
+        ]
         factors = {
             blk: ring.tile([P, 2, BANK], F32, name="factors", tag=f"factors{blk}", align_bytes=64)
             for blk in range(VECTOR_BLOCKS, BLOCKS)
@@ -179,7 +190,7 @@ def tile_list_modp_ggelu_noneb_kernel(
                     lhsT=codes(t),
                     lhsT_scale=scales[:, P * t : P * (t + 1)],
                     rhs=v[a, blk].bitcast(FP8X4),
-                    rhs_scale=v_sc[:, J * a + BLOCK * blk : J * a + BLOCK * (blk + 1)],
+                    rhs_scale=v_sc[a][:, BLOCK * blk : BLOCK * (blk + 1)],
                     start=(a == 0 and t == 0),
                     stop=(a == PASSES - 1 and t == 3),
                 )
@@ -195,7 +206,7 @@ def tile_list_modp_ggelu_noneb_kernel(
             first_stage_pass(ga[blk], blk, a, codes, wg_sc[:, R * a : R * (a + 1)])
             if a == PASSES - 1:
                 if blk < VECTOR_BLOCKS:
-                    result = gel[:, blk, :].rearrange(by_pairs, t=4, e=2)
+                    result = gel[blk][:].rearrange(by_pairs, t=4, e=2)
                 else:
                     result = factors[blk][:, 0, :].rearrange(by_token, t=4, e=2)
                 nc.scalar.activation(result, ga[blk][:].rearrange(from_bank, t=4, e=2), GELU)
@@ -213,11 +224,9 @@ def tile_list_modp_ggelu_noneb_kernel(
                     factors[blk][:, 1, :].rearrange(by_token, t=4, e=2), ub[blk][:].rearrange(from_bank, t=4, e=2)
                 )
 
-        def gate_block(blk):
+        def both_sums(blk):
             for a in range(PASSES):
                 gate_pass(blk, a)
-
-        def up_block(blk):
             for a in range(PASSES):
                 up_pass(blk, a)
 
@@ -229,7 +238,7 @@ def tile_list_modp_ggelu_noneb_kernel(
             nc.vector.tensor_tensor(
                 h_block(blk).rearrange(by_token, t=4, e=2),
                 ub[blk][:].rearrange(from_bank, t=4, e=2),
-                gel[:, blk, :].rearrange(by_pairs, t=4, e=2),
+                gel[blk][:].rearrange(by_pairs, t=4, e=2),
                 MULT,
             )
 
@@ -253,22 +262,17 @@ def tile_list_modp_ggelu_noneb_kernel(
             return sums
 
         def early_sums(c, n):
-            return down_sums(c, CHUNK * n, CHUNK * (n + 1), bank(EARLY_DOWN_BANK[c, n])[:, 0:CHUNK])
+            return down_sums(c, CHUNK * n, CHUNK * (n + 1), bank(EARLY_DOWN_BANK[n][c])[:, 0:CHUNK])
 
-        def with_bias(sums, c, y):
-            nc.scalar.activation(y, sums, IDENT, bias=bias[:, c : c + 1])
-
-        def scaled_on_vector(sums, c, n):
-            scaled = keep.tile([P, CHUNK], F32, name=f"scaled{c}_{n}")
-            nc.vector.scalar_tensor_tensor(
-                scaled[:], sums, bias[:, c : c + 1], router_w[:, CHUNK * n : CHUNK * (n + 1)], ADD, MULT
-            )
-            return scaled
-
-        def biased(c, n, slot):
+        def with_bias(sums, c, slot):
             y = ring.tile([P, CHUNK], F32, name="y", tag=slot, align_bytes=64)
-            with_bias(early_sums(c, n), c, y[:])
+            nc.scalar.activation(y[:], sums, IDENT, bias=bias[:, c : c + 1])
             return y[:]
+
+        def scaled_on_gpsimd(y, c, n):
+            scaled = keep.tile([P, CHUNK], F32, name=f"scaled{c}_{n}")
+            nc.gpsimd.tensor_tensor(scaled[:], y, router_w[:, CHUNK * n : CHUNK * (n + 1)], MULT)
+            return scaled
 
         def put_scaled(scaled, c, n):
             nc.vector.tensor_copy(pages[c][:].indirect(listed(CHUNK * n, CHUNK * (n + 1))), scaled[:])
@@ -286,47 +290,40 @@ def tile_list_modp_ggelu_noneb_kernel(
                 starts = [j for j in h_q if s <= j < s + BANK]
                 for a0, a1 in zip(starts, starts[1:] + [s + BANK]):
                     down_sums(c, a0, a1, sums[:, a0 - s : a1 - s])
-                with_bias(sums[:], c, y[:, s - j0 : s - j0 + BANK])
+                nc.scalar.activation(y[:, s - j0 : s - j0 + BANK], sums[:], IDENT, bias=bias[:, c : c + 1])
             return y[:]
 
-        for blk in range(BLOCKS // 2):
+        for blk in range(VECTOR_BLOCKS):
             gate_pass(blk, 0)
-        for blk in range(BLOCKS // 2):
+        for blk in range(VECTOR_BLOCKS):
             up_pass(blk, 0)
-        for blk in range(BLOCKS // 2):
+        for blk in range(VECTOR_BLOCKS):
             gate_pass(blk, 1)
             up_pass(blk, 1)
-        gate_block(4)
-        up_block(4)
         product(0)
         product(1)
-        product(2)
+        gather_words(1, 6, 7, AT_GEL0)
         quantise_h(0, 0, CHUNK)
-        zeroed_page("h_bf0")
-        y00 = biased(0, 0, "h_q1")
-        sums20 = early_sums(2, 0)
-        y10 = biased(1, 0, "y10")
+        gather_words(1, 7, 8, AT_H)
+        scaled = [
+            scaled_on_gpsimd(with_bias(early_sums(c, 0), c, slot), c, 0) for c, slot in enumerate(("h_q1", "y10", "y20"))
+        ]
+        product(2)
         product(3)
-        product(4)
-        scaled20 = scaled_on_vector(sums20, 2, 0)
-        put(y00, 0, 0, CHUNK)
+        put_scaled(scaled[0], 0, 0)
         quantise_h(1, CHUNK, HALF)
-        zeroed_page("h_bf1")
-        put(y10, 1, 0, CHUNK)
-        scaled01 = scaled_on_vector(early_sums(0, 1), 0, 1)
-        scaled11 = scaled_on_vector(early_sums(1, 1), 1, 1)
-        sums21 = early_sums(2, 1)
-        put_scaled(scaled01, 0, 1)
-        put_scaled(scaled11, 1, 1)
-        put_scaled(scaled20, 2, 0)
-        for blk in range(VECTOR_BLOCKS, BLOCKS):
-            gate_block(blk)
-            up_block(blk)
+        put_scaled(scaled[1], 1, 0)
+        put_scaled(scaled[2], 2, 0)
+        sums = [early_sums(c, 1) for c in range(PAGES)]
+        for c in range(2):
+            both_sums(4 + c)
+            product_on_gpsimd(4 + c)
+            put_scaled(scaled_on_gpsimd(with_bias(sums[c], c, f"y{c}1"), c, 1), c, 1)
+        for blk in (6, 7):
+            both_sums(blk)
             product_on_gpsimd(blk)
         quantise_h(2, HALF, J)
-        y21 = ring.tile([P, CHUNK], F32, name="y21", tag=f"factors{BLOCKS - 1}", align_bytes=64)
-        with_bias(sums21, 2, y21[:])
-        put(y21[:], 2, CHUNK, HALF)
+        put(with_bias(sums[2], 2, f"factors{BLOCKS - 1}"), 2, CHUNK, HALF)
         for c in range(PAGES):
             put(down(c, HALF, J), c, HALF, J)
         put(down(PAGES, 0, J), PAGES, 0, J)

@@ -26,18 +26,21 @@ BLOCKS = J // BLOCK
 CHUNK = 2 * BLOCK
 HALF = J // 2
 PAGES = 3
-SCALAR_M = (80, 56)
-SHARED = 32
+SCALAR_M = (88, 64)
+VECTOR_ZEROES = 1280
 VECTOR_BLOCKS = 4
 GATE_BANK = (0, 1, 2, 3, 0, 2, 7, 2)
 UP_BANK = (4, 5, 6, 7, 1, 6, 0, 1)
 EARLY_DOWN_BANK = ((0, 1, 2), (3, 4, 5))
 LATE_DOWN_BANK = (3, 4)
-AT_WU_BF = T
-AT_GEL0 = AT_WU_BF + 16 * R
-AT_H = AT_GEL0 + 4 * BANK
 OVERLAP = 64
+AT_WU_BF0 = T
+AT_WU_BF1 = AT_WU_BF0 + 8 * R
+AT_GEL0 = AT_WU_BF1 + 16 * R
+AT_H = AT_GEL0 + 4 * BANK
 AT_WG_SC = AT_H + 32 * CHUNK + 8 * BLOCK
+AT_WU0 = AT_WG_SC + 16 * BLOCK
+AT_WU1 = AT_WU0 + 16 * R
 
 
 def tile_list_modp_ggelu_noneb_kernel(
@@ -62,7 +65,7 @@ def tile_list_modp_ggelu_noneb_kernel(
             wg_words.rearrange("a p n -> p a n").bitcast(I32),
         )
         tab_sc = placed.tile([P, T], U8, name="tab_sc", align_bytes=64, offset=0)
-        nc.vector.memset(tab_sc[:].bitcast(I32), 0)
+        nc.gpsimd.memset(tab_sc[:].bitcast(I32), 0)
         for q in range(4):
             nc.sync.dma_start(
                 tab_sc[32 * q : 32 * q + 8, :].bitcast(I32), tab_scales[:, 4 * q : 4 * q + 4, :].bitcast(I32)
@@ -86,14 +89,17 @@ def tile_list_modp_ggelu_noneb_kernel(
                 wg_scales[:, 4 * q : 4 * q + 4, :].rearrange("a g n -> g a n").bitcast(I32),
             )
         wu_raw = [
-            load_wu(0, ring.tile([P, 4, R], F32, name="wu_raw", tag="wu0", align_bytes=64)),
-            load_wu(1, keep.tile([P, 4, R], F32, name="wu_raw1", align_bytes=64)),
+            load_wu(0, placed.tile([P, 4, R], F32, name="wu_raw0", align_bytes=64, offset=AT_WU0)),
+            load_wu(1, placed.tile([P, 4, R], F32, name="wu_raw1", align_bytes=64, offset=AT_WU1)),
         ]
         tab.append(load_tab(1))
 
         pages = [keep.tile([P, T], F32, name=f"page{c}") for c in range(PAGES)]
-        for page in pages:
-            nc.vector.memset(page[:].bitcast(I32), 0)
+        for page, width in ((pages[0], T), (pages[1], VECTOR_ZEROES)):
+            nc.vector.memset(page[:, 0 : width - 1].bitcast(I32), 0)
+            nc.vector.memset(page[:, width - 1 : width].bitcast(I32), 0)
+        nc.gpsimd.memset(pages[1][:, VECTOR_ZEROES:T].bitcast(I32), 0)
+        nc.gpsimd.memset(pages[2][:].bitcast(I32), 0)
 
         picked_sc = keep.tile([P, J], U8, name="picked_sc", align_bytes=64)
         nc.vector.tensor_copy(picked_sc[:], tab_sc[:].indirect(offsets[:]))
@@ -129,10 +135,12 @@ def tile_list_modp_ggelu_noneb_kernel(
             wg_sc_raw[:].rearrange("p (a m t) -> p a t m", a=PASSES, t=4),
         )
         gather_words(0, 2, 4, AT_WG_SC - 8 * BLOCK + OVERLAP)
-        gather_words(0, 4, 8, AT_WG_SC + OVERLAP)
+        gather_words(0, 4, 7, AT_WG_SC + OVERLAP)
 
-        wu_both = placed.tile([P, 8 * R - SHARED], BF16, name="wu_both", align_bytes=64, offset=AT_WU_BF)
-        wu_bf = [wu_both[:, 4 * R - SHARED :], wu_both[:, 0 : 4 * R]]
+        wu_bf = [
+            placed.tile([P, 4 * R], BF16, name=f"wu_bf{a}", align_bytes=64, offset=at)[:]
+            for a, at in enumerate((AT_WU_BF0, AT_WU_BF1))
+        ]
         wu_q = [keep.tile([P, R], U32, name=f"wu_q{a}", align_bytes=64) for a in range(PASSES)]
         wu_sc = [keep.tile([P, R], U8, name=f"wu_sc{a}", align_bytes=64) for a in range(PASSES)]
         for a in range(PASSES):
@@ -143,9 +151,9 @@ def tile_list_modp_ggelu_noneb_kernel(
             nc.vector.quantize_mx(out=wu_q[a][:].bitcast(FP8X4), scales=wu_sc[a][:], in_=wu_bf[a])
 
         for blk0, blk1 in ((0, 1), (1, 2), (2, 4), (4, 6)):
-            gather_words(1, blk0, blk1, AT_WU_BF + 4 * BLOCK * blk0)
+            gather_words(1, blk0, blk1, AT_WU1 + 4 * BLOCK * blk0)
 
-        wd_bytes = ring.tile([P, 3 * N], U8, name="wd_bytes", tag="wu0", align_bytes=64)
+        wd_bytes = placed.tile([P, 3 * N], U8, name="wd_bytes", align_bytes=64, offset=AT_WU0)
         wd = wd_bytes[:, 0 : 2 * N]
         wd_sc = wd_bytes[:, 2 * N : 3 * N]
         nc.sync.dma_start(wd.bitcast(I32), wd_words[0].bitcast(I32))
@@ -154,7 +162,7 @@ def tile_list_modp_ggelu_noneb_kernel(
                 wd_bytes[32 * q : 32 * q + 4, 2 * N : 3 * N].bitcast(I32),
                 wd_scales[0, 4 * q : 4 * q + 4, :].bitcast(I32),
             )
-        epilogue = placed.tile([P, J + N // P], F32, name="epilogue", align_bytes=64, offset=AT_WU_BF + 4 * BLOCK * 6)
+        epilogue = placed.tile([P, J + N // P], F32, name="epilogue", align_bytes=64, offset=AT_WU_BF1 + 4 * BLOCK * 6)
         router_w = epilogue[:, 0:J]
         bias = epilogue[:, J : J + N // P]
         with nc.allow_non_contiguous_dma(reason="one bias value a partition"):
@@ -304,7 +312,8 @@ def tile_list_modp_ggelu_noneb_kernel(
         product(1)
         gather_words(1, 6, 7, AT_GEL0)
         quantise_h(0, 0, CHUNK)
-        gather_words(1, 7, 8, AT_H)
+        for a in range(PASSES):
+            gather_words(a, 7, 8, AT_H + 4 * BLOCK * a)
         scaled = [
             scaled_on_gpsimd(with_bias(early_sums(c, 0), c, slot), c, 0) for c, slot in enumerate(("h_q1", "y10", "y20"))
         ]

@@ -29,18 +29,20 @@ PAGES = 3
 SCALAR_M = (88, 64)
 VECTOR_ZEROES = 1280
 VECTOR_BLOCKS = 4
-GATE_BANK = (0, 1, 2, 3, 0, 2, 7, 2)
-UP_BANK = (4, 5, 6, 7, 1, 6, 0, 1)
-EARLY_DOWN_BANK = ((0, 1, 2), (3, 4, 5))
-LATE_DOWN_BANK = (3, 4)
+GATE_BANK = (0, 1, 2, 3, 4, 1, 4, 1)
+UP_BANK = (4, 5, 6, 7, 0, 2, 0, 2)
+EARLY_DOWN_BANK = ((0, 1, 2), (3, 6, 7))
+LATE_DOWN_BANK = (3, 5)
 OVERLAP = 64
-AT_WU_BF0 = T
+AT_TAB_SC = 4 * J
+AT_WU_BF0 = AT_TAB_SC + 2 * T
 AT_WU_BF1 = AT_WU_BF0 + 8 * R
 AT_GEL0 = AT_WU_BF1 + 16 * R
 AT_H = AT_GEL0 + 4 * BANK
 AT_WG_SC = AT_H + 32 * CHUNK + 8 * BLOCK
 AT_WU0 = AT_WG_SC + 16 * BLOCK
 AT_WU1 = AT_WU0 + 16 * R
+AT_Y00 = AT_WU1 + 16 * R + 4 * CHUNK
 
 
 def tile_list_modp_ggelu_noneb_kernel(
@@ -64,11 +66,11 @@ def tile_list_modp_ggelu_noneb_kernel(
             wg_raw[:].bitcast(I32).rearrange("p (a n) -> p a n", a=PASSES),
             wg_words.rearrange("a p n -> p a n").bitcast(I32),
         )
-        tab_sc = placed.tile([P, T], U8, name="tab_sc", align_bytes=64, offset=0)
+        tab_sc = placed.tile([P, T], U8, name="tab_sc", align_bytes=64, offset=AT_TAB_SC)
         nc.gpsimd.memset(tab_sc[:].bitcast(I32), 0)
-        for q in range(4):
+        for r in range(4):
             nc.sync.dma_start(
-                tab_sc[32 * q : 32 * q + 8, :].bitcast(I32), tab_scales[:, 4 * q : 4 * q + 4, :].bitcast(I32)
+                tab_sc[r:P:16, :].bitcast(I32), tab_scales[:, r:16:4, :].rearrange("a q t -> q a t").bitcast(I32)
             )
 
         def load_tab(a):
@@ -103,10 +105,10 @@ def tile_list_modp_ggelu_noneb_kernel(
 
         picked_sc = keep.tile([P, J], U8, name="picked_sc", align_bytes=64)
         nc.vector.tensor_copy(picked_sc[:], tab_sc[:].indirect(offsets[:]))
-        moved_sc = placed.tile([P, J], U8, name="moved_sc", align_bytes=64, offset=0)
+        moved_sc = placed.tile([P, J], U8, name="moved_sc", align_bytes=64, offset=AT_TAB_SC + OVERLAP)
         for q in range(4):
             nc.sync.dma_start(
-                moved_sc[32 * q : 32 * q + 4, :].bitcast(I32), picked_sc[32 * q + 4 : 32 * q + 8, :].bitcast(I32)
+                moved_sc[32 * q : 32 * q + 4, :].bitcast(I32), picked_sc[32 * q + 16 : 32 * q + 20, :].bitcast(I32)
             )
         v_sc = [picked_sc, moved_sc]
 
@@ -153,21 +155,21 @@ def tile_list_modp_ggelu_noneb_kernel(
         for blk0, blk1 in ((0, 1), (1, 2), (2, 4), (4, 6)):
             gather_words(1, blk0, blk1, AT_WU1 + 4 * BLOCK * blk0)
 
-        wd_bytes = placed.tile([P, 3 * N], U8, name="wd_bytes", align_bytes=64, offset=AT_WU0)
-        wd = wd_bytes[:, 0 : 2 * N]
-        wd_sc = wd_bytes[:, 2 * N : 3 * N]
-        nc.sync.dma_start(wd.bitcast(I32), wd_words[0].bitcast(I32))
-        for q in range(4):
-            nc.sync.dma_start(
-                wd_bytes[32 * q : 32 * q + 4, 2 * N : 3 * N].bitcast(I32),
-                wd_scales[0, 4 * q : 4 * q + 4, :].bitcast(I32),
-            )
-        epilogue = placed.tile([P, J + N // P], F32, name="epilogue", align_bytes=64, offset=AT_WU_BF1 + 4 * BLOCK * 6)
+        wd_bytes = placed.tile([P, 3 * N], U8, name="wd_bytes", align_bytes=64, offset=AT_TAB_SC + OVERLAP + J)
+        wd_sc = wd_bytes[:, 0:N]
+        wd = wd_bytes[:, N : 3 * N]
+        epilogue = placed.tile([P, J + N // P], F32, name="epilogue", align_bytes=64, offset=AT_TAB_SC - 4 * J)
         router_w = epilogue[:, 0:J]
         bias = epilogue[:, J : J + N // P]
+        nc.sync.dma_start(wd.bitcast(I32), wd_words[0].bitcast(I32))
+        nc.sync.dma_start(router_w[:, 0:HALF], wgo[:, 0:HALF])
         with nc.allow_non_contiguous_dma(reason="one bias value a partition"):
             nc.sync.dma_start(bias, b.rearrange("(c p) -> p c", p=P))
-        nc.sync.dma_start(router_w, wgo)
+        for q in range(4):
+            nc.sync.dma_start(
+                wd_bytes[32 * q : 32 * q + 4, 0:N].bitcast(I32), wd_scales[0, 4 * q : 4 * q + 4, :].bitcast(I32)
+            )
+        nc.sync.dma_start(router_w[:, HALF:J], wgo[:, HALF:J])
 
         h_bf = [
             placed.tile([P, 4 * width], BF16, name=f"h_bf{n}", align_bytes=64, offset=AT_H + n * (8 * CHUNK - OVERLAP))
@@ -180,8 +182,11 @@ def tile_list_modp_ggelu_noneb_kernel(
         ]
         factors = {
             blk: ring.tile([P, 2, BANK], F32, name="factors", tag=f"factors{blk}", align_bytes=64)
-            for blk in range(VECTOR_BLOCKS, BLOCKS)
+            for blk in range(VECTOR_BLOCKS + 1, BLOCKS)
         }
+        factors[VECTOR_BLOCKS] = placed.tile(
+            [P, 2, BANK], F32, name="factors4", align_bytes=64, offset=AT_Y00 + OVERLAP
+        )
         ga = {}
         ub = {}
         from_bank = "p (t n e) -> p n t e"
@@ -232,11 +237,17 @@ def tile_list_modp_ggelu_noneb_kernel(
                     factors[blk][:, 1, :].rearrange(by_token, t=4, e=2), ub[blk][:].rearrange(from_bank, t=4, e=2)
                 )
 
-        def both_sums(blk):
+        def gate_sums(blk):
             for a in range(PASSES):
                 gate_pass(blk, a)
+
+        def up_sums(blk):
             for a in range(PASSES):
                 up_pass(blk, a)
+
+        def both_sums(blk):
+            gate_sums(blk)
+            up_sums(blk)
 
         def h_block(blk):
             n = min(blk // 2, 2)
@@ -254,7 +265,12 @@ def tile_list_modp_ggelu_noneb_kernel(
             nc.gpsimd.tensor_tensor(h_block(blk), factors[blk][:, 0, :], factors[blk][:, 1, :], MULT)
 
         def quantise_h(n, j0, j1):
-            h_q[j0] = ring.tile([P, j1 - j0], U32, name="h_q", tag=f"h_q{n}", align_bytes=64)
+            if n == 1:
+                h_q[j0] = placed.tile(
+                    [P, j1 - j0], U32, name="h_q1", align_bytes=64, offset=AT_Y00 + OVERLAP - 4 * CHUNK
+                )
+            else:
+                h_q[j0] = keep.tile([P, j1 - j0], U32, name=f"h_q{n}", align_bytes=64)
             nc.vector.quantize_mx(out=h_q[j0][:].bitcast(FP8X4), scales=h_sc[:, j0:j1], in_=h_bf[n][:])
 
         def down_sums(c, j0, j1, sums):
@@ -273,13 +289,23 @@ def tile_list_modp_ggelu_noneb_kernel(
             return down_sums(c, CHUNK * n, CHUNK * (n + 1), bank(EARLY_DOWN_BANK[n][c])[:, 0:CHUNK])
 
         def with_bias(sums, c, slot):
-            y = ring.tile([P, CHUNK], F32, name="y", tag=slot, align_bytes=64)
+            if slot == "y00":
+                y = placed.tile([P, CHUNK], F32, name="y00", align_bytes=64, offset=AT_Y00)
+            else:
+                y = ring.tile([P, CHUNK], F32, name="y", tag=slot, align_bytes=64)
             nc.scalar.activation(y[:], sums, IDENT, bias=bias[:, c : c + 1])
             return y[:]
 
         def scaled_on_gpsimd(y, c, n):
             scaled = keep.tile([P, CHUNK], F32, name=f"scaled{c}_{n}")
             nc.gpsimd.tensor_tensor(scaled[:], y, router_w[:, CHUNK * n : CHUNK * (n + 1)], MULT)
+            return scaled
+
+        def scaled_on_vector(sums, c, n):
+            scaled = keep.tile([P, CHUNK], F32, name=f"scaled{c}_{n}")
+            nc.vector.scalar_tensor_tensor(
+                scaled[:], sums, bias[:, c : c + 1], router_w[:, CHUNK * n : CHUNK * (n + 1)], ADD, MULT
+            )
             return scaled
 
         def put_scaled(scaled, c, n):
@@ -315,7 +341,7 @@ def tile_list_modp_ggelu_noneb_kernel(
         for a in range(PASSES):
             gather_words(a, 7, 8, AT_H + 4 * BLOCK * a)
         scaled = [
-            scaled_on_gpsimd(with_bias(early_sums(c, 0), c, slot), c, 0) for c, slot in enumerate(("h_q1", "y10", "y20"))
+            scaled_on_gpsimd(with_bias(early_sums(c, 0), c, slot), c, 0) for c, slot in enumerate(("y00", "y10", "y20"))
         ]
         product(2)
         product(3)
@@ -323,11 +349,16 @@ def tile_list_modp_ggelu_noneb_kernel(
         quantise_h(1, CHUNK, HALF)
         put_scaled(scaled[1], 1, 0)
         put_scaled(scaled[2], 2, 0)
+        both_sums(4)
+        product_on_gpsimd(4)
+        gate_sums(5)
         sums = [early_sums(c, 1) for c in range(PAGES)]
-        for c in range(2):
-            both_sums(4 + c)
-            product_on_gpsimd(4 + c)
-            put_scaled(scaled_on_gpsimd(with_bias(sums[c], c, f"y{c}1"), c, 1), c, 1)
+        scaled01 = scaled_on_gpsimd(with_bias(sums[0], 0, "y01"), 0, 1)
+        scaled11 = scaled_on_vector(sums[1], 1, 1)
+        put_scaled(scaled01, 0, 1)
+        put_scaled(scaled11, 1, 1)
+        up_sums(5)
+        product_on_gpsimd(5)
         for blk in (6, 7):
             both_sums(blk)
             product_on_gpsimd(blk)

@@ -26,13 +26,12 @@ BLOCKS = J // BLOCK
 CHUNK = 2 * BLOCK
 HALF = J // 2
 PAGES = 3
-SCALAR_M = (88, 64)
-VECTOR_ZEROES = 1280
+SCALAR_M = (80, 56)
 VECTOR_BLOCKS = 4
-GATE_BANK = (0, 1, 2, 3, 4, 1, 4, 1)
-UP_BANK = (4, 5, 6, 7, 0, 2, 0, 2)
+GATE_BANK = (0, 1, 2, 3, 4, 1, 1, 2)
+UP_BANK = (4, 5, 6, 7, 0, 2, 0, 1)
 EARLY_DOWN_BANK = ((0, 1, 2), (3, 6, 7))
-LATE_DOWN_BANK = (3, 5)
+LATE_DOWN_BANK = (4, 5)
 OVERLAP = 64
 AT_TAB_SC = 4 * J
 AT_WU_BF0 = AT_TAB_SC + 2 * T
@@ -40,7 +39,7 @@ AT_WU_BF1 = AT_WU_BF0 + 8 * R
 AT_GEL0 = AT_WU_BF1 + 16 * R
 AT_H = AT_GEL0 + 4 * BANK
 AT_WG_SC = AT_H + 32 * CHUNK + 8 * BLOCK
-AT_WU0 = AT_WG_SC + 16 * BLOCK
+AT_WU0 = AT_WG_SC + 32 * BLOCK
 AT_WU1 = AT_WU0 + 16 * R
 AT_Y00 = AT_WU1 + 16 * R + 4 * CHUNK
 
@@ -74,7 +73,7 @@ def tile_list_modp_ggelu_noneb_kernel(
             )
 
         def load_tab(a):
-            words = keep.tile([P, T], I32, name=f"tab{a}", align_bytes=64)
+            words = ring.tile([P, T], I32, name="tab", tag=f"tab{a}", align_bytes=64)
             nc.sync.dma_start(words[:], tab_words[a].rearrange("p t i -> p (t i)").bitcast(I32))
             return words
 
@@ -96,12 +95,10 @@ def tile_list_modp_ggelu_noneb_kernel(
         ]
         tab.append(load_tab(1))
 
-        pages = [keep.tile([P, T], F32, name=f"page{c}") for c in range(PAGES)]
-        for page, width in ((pages[0], T), (pages[1], VECTOR_ZEROES)):
-            nc.vector.memset(page[:, 0 : width - 1].bitcast(I32), 0)
-            nc.vector.memset(page[:, width - 1 : width].bitcast(I32), 0)
-        nc.gpsimd.memset(pages[1][:, VECTOR_ZEROES:T].bitcast(I32), 0)
-        nc.gpsimd.memset(pages[2][:].bitcast(I32), 0)
+        pages = [keep.tile([P, T], F32, name=f"page{c}") for c in range(PAGES - 1)]
+        nc.vector.memset(pages[0][:, 0 : T - 1].bitcast(I32), 0)
+        nc.vector.memset(pages[0][:, T - 1 : T].bitcast(I32), 0)
+        nc.gpsimd.memset(pages[1][:].bitcast(I32), 0)
 
         picked_sc = keep.tile([P, J], U8, name="picked_sc", align_bytes=64)
         nc.vector.tensor_copy(picked_sc[:], tab_sc[:].indirect(offsets[:]))
@@ -137,7 +134,7 @@ def tile_list_modp_ggelu_noneb_kernel(
             wg_sc_raw[:].rearrange("p (a m t) -> p a t m", a=PASSES, t=4),
         )
         gather_words(0, 2, 4, AT_WG_SC - 8 * BLOCK + OVERLAP)
-        gather_words(0, 4, 7, AT_WG_SC + OVERLAP)
+        gather_words(0, 4, 8, AT_WG_SC + OVERLAP)
 
         wu_bf = [
             placed.tile([P, 4 * R], BF16, name=f"wu_bf{a}", align_bytes=64, offset=at)[:]
@@ -182,11 +179,8 @@ def tile_list_modp_ggelu_noneb_kernel(
         ]
         factors = {
             blk: ring.tile([P, 2, BANK], F32, name="factors", tag=f"factors{blk}", align_bytes=64)
-            for blk in range(VECTOR_BLOCKS + 1, BLOCKS)
+            for blk in range(VECTOR_BLOCKS, BLOCKS)
         }
-        factors[VECTOR_BLOCKS] = placed.tile(
-            [P, 2, BANK], F32, name="factors4", align_bytes=64, offset=AT_Y00 + OVERLAP
-        )
         ga = {}
         ub = {}
         from_bank = "p (t n e) -> p n t e"
@@ -267,7 +261,7 @@ def tile_list_modp_ggelu_noneb_kernel(
         def quantise_h(n, j0, j1):
             if n == 1:
                 h_q[j0] = placed.tile(
-                    [P, j1 - j0], U32, name="h_q1", align_bytes=64, offset=AT_Y00 + OVERLAP - 4 * CHUNK
+                    [P, j1 - j0], U32, name="h_q1", align_bytes=64, offset=AT_Y00 - 4 * CHUNK
                 )
             else:
                 h_q[j0] = keep.tile([P, j1 - j0], U32, name=f"h_q{n}", align_bytes=64)
@@ -289,8 +283,10 @@ def tile_list_modp_ggelu_noneb_kernel(
             return down_sums(c, CHUNK * n, CHUNK * (n + 1), bank(EARLY_DOWN_BANK[n][c])[:, 0:CHUNK])
 
         def with_bias(sums, c, slot):
-            if slot == "y00":
-                y = placed.tile([P, CHUNK], F32, name="y00", align_bytes=64, offset=AT_Y00)
+            if slot in ("y00", "y10"):
+                y = placed.tile(
+                    [P, CHUNK], F32, name=slot, align_bytes=64, offset=AT_Y00 - (4 * CHUNK if slot == "y10" else 0)
+                )
             else:
                 y = ring.tile([P, CHUNK], F32, name="y", tag=slot, align_bytes=64)
             nc.scalar.activation(y[:], sums, IDENT, bias=bias[:, c : c + 1])
@@ -338,22 +334,24 @@ def tile_list_modp_ggelu_noneb_kernel(
         product(1)
         gather_words(1, 6, 7, AT_GEL0)
         quantise_h(0, 0, CHUNK)
-        for a in range(PASSES):
-            gather_words(a, 7, 8, AT_H + 4 * BLOCK * a)
-        scaled = [
-            scaled_on_gpsimd(with_bias(early_sums(c, 0), c, slot), c, 0) for c, slot in enumerate(("y00", "y10", "y20"))
-        ]
+        gather_words(1, 7, 8, AT_H)
+        pages.append(ring.tile([P, T], F32, name="page2", tag="tab1", align_bytes=64))
+        nc.gpsimd.memset(pages[2][:].bitcast(I32), 0)
+        y00 = with_bias(early_sums(0, 0), 0, "y00")
+        sums20 = early_sums(2, 0)
+        scaled10 = scaled_on_gpsimd(with_bias(early_sums(1, 0), 1, "y10"), 1, 0)
         product(2)
         product(3)
-        put_scaled(scaled[0], 0, 0)
+        scaled20 = scaled_on_vector(sums20, 2, 0)
+        put(y00, 0, 0, CHUNK)
+        put_scaled(scaled20, 2, 0)
         quantise_h(1, CHUNK, HALF)
-        put_scaled(scaled[1], 1, 0)
-        put_scaled(scaled[2], 2, 0)
+        put_scaled(scaled10, 1, 0)
         both_sums(4)
         product_on_gpsimd(4)
         gate_sums(5)
         sums = [early_sums(c, 1) for c in range(PAGES)]
-        scaled01 = scaled_on_gpsimd(with_bias(sums[0], 0, "y01"), 0, 1)
+        scaled01 = scaled_on_vector(sums[0], 0, 1)
         scaled11 = scaled_on_vector(sums[1], 1, 1)
         put_scaled(scaled01, 0, 1)
         put_scaled(scaled11, 1, 1)

@@ -26,7 +26,7 @@ BLOCKS = J // BLOCK
 CHUNK = 2 * BLOCK
 HALF = J // 2
 PAGES = 3
-SCALAR_M = (80, 56)
+SCALAR_M = (88, 48)
 VECTOR_BLOCKS = 4
 GATE_BANK = (0, 1, 2, 3, 4, 1, 1, 2)
 UP_BANK = (4, 5, 6, 7, 0, 2, 0, 1)
@@ -36,12 +36,15 @@ OVERLAP = 64
 AT_TAB_SC = 4 * J
 AT_WU_BF0 = AT_TAB_SC + 2 * T
 AT_WU_BF1 = AT_WU_BF0 + 8 * R
-AT_GEL0 = AT_WU_BF1 + 16 * R
-AT_H = AT_GEL0 + 4 * BANK
-AT_WG_SC = AT_H + 32 * CHUNK + 8 * BLOCK
+AT_GEL0 = AT_WU_BF1 + 8 * R
+AT_H0 = AT_GEL0 + 4 * BANK
+AT_WG_SC = AT_H0 + 4 * T + 8 * BLOCK
 AT_WU0 = AT_WG_SC + 32 * BLOCK
 AT_WU1 = AT_WU0 + 16 * R
-AT_Y00 = AT_WU1 + 16 * R + 4 * CHUNK
+AT_Y00 = AT_WU1 + 16 * R
+AT_TAB = (AT_Y00 + 4 * CHUNK, AT_Y00 + 4 * CHUNK + 4 * T)
+AT_H1 = AT_TAB[1] + 4 * T - OVERLAP
+AT_H2 = AT_H1 + 8 * CHUNK - OVERLAP
 
 
 def tile_list_modp_ggelu_noneb_kernel(
@@ -73,7 +76,7 @@ def tile_list_modp_ggelu_noneb_kernel(
             )
 
         def load_tab(a):
-            words = ring.tile([P, T], I32, name="tab", tag=f"tab{a}", align_bytes=64)
+            words = placed.tile([P, T], I32, name=f"tab{a}", align_bytes=64, offset=AT_TAB[a])
             nc.sync.dma_start(words[:], tab_words[a].rearrange("p t i -> p (t i)").bitcast(I32))
             return words
 
@@ -149,7 +152,7 @@ def tile_list_modp_ggelu_noneb_kernel(
             nc.vector.tensor_copy(rounded[:, SCALAR_M[a] : P], dealt[:, SCALAR_M[a] : P])
             nc.vector.quantize_mx(out=wu_q[a][:].bitcast(FP8X4), scales=wu_sc[a][:], in_=wu_bf[a])
 
-        for blk0, blk1 in ((0, 1), (1, 2), (2, 4), (4, 6)):
+        for blk0, blk1 in ((0, 1), (1, 2), (2, 4), (4, 7)):
             gather_words(1, blk0, blk1, AT_WU1 + 4 * BLOCK * blk0)
 
         wd_bytes = placed.tile([P, 3 * N], U8, name="wd_bytes", align_bytes=64, offset=AT_TAB_SC + OVERLAP + J)
@@ -169,8 +172,8 @@ def tile_list_modp_ggelu_noneb_kernel(
         nc.sync.dma_start(router_w[:, HALF:J], wgo[:, HALF:J])
 
         h_bf = [
-            placed.tile([P, 4 * width], BF16, name=f"h_bf{n}", align_bytes=64, offset=AT_H + n * (8 * CHUNK - OVERLAP))
-            for n, width in enumerate((CHUNK, CHUNK, HALF))
+            placed.tile([P, 4 * width], BF16, name=f"h_bf{n}", align_bytes=64, offset=at)
+            for n, (width, at) in enumerate(((CHUNK, AT_H0), (CHUNK, AT_H1), (HALF, AT_H2)))
         ]
         h_q = {}
         h_sc = keep.tile([P, J], U8, name="h_sc", align_bytes=64)
@@ -261,7 +264,7 @@ def tile_list_modp_ggelu_noneb_kernel(
         def quantise_h(n, j0, j1):
             if n == 1:
                 h_q[j0] = placed.tile(
-                    [P, j1 - j0], U32, name="h_q1", align_bytes=64, offset=AT_Y00 - 4 * CHUNK
+                    [P, j1 - j0], U32, name="h_q1", align_bytes=64, offset=AT_Y00
                 )
             else:
                 h_q[j0] = keep.tile([P, j1 - j0], U32, name=f"h_q{n}", align_bytes=64)
@@ -283,10 +286,8 @@ def tile_list_modp_ggelu_noneb_kernel(
             return down_sums(c, CHUNK * n, CHUNK * (n + 1), bank(EARLY_DOWN_BANK[n][c])[:, 0:CHUNK])
 
         def with_bias(sums, c, slot):
-            if slot in ("y00", "y10"):
-                y = placed.tile(
-                    [P, CHUNK], F32, name=slot, align_bytes=64, offset=AT_Y00 - (4 * CHUNK if slot == "y10" else 0)
-                )
+            if slot == "y10":
+                y = placed.tile([P, CHUNK], F32, name=slot, align_bytes=64, offset=AT_Y00)
             else:
                 y = ring.tile([P, CHUNK], F32, name="y", tag=slot, align_bytes=64)
             nc.scalar.activation(y[:], sums, IDENT, bias=bias[:, c : c + 1])
@@ -332,10 +333,9 @@ def tile_list_modp_ggelu_noneb_kernel(
             up_pass(blk, 1)
         product(0)
         product(1)
-        gather_words(1, 6, 7, AT_GEL0)
+        gather_words(1, 7, 8, AT_GEL0)
         quantise_h(0, 0, CHUNK)
-        gather_words(1, 7, 8, AT_H)
-        pages.append(ring.tile([P, T], F32, name="page2", tag="tab1", align_bytes=64))
+        pages.append(placed.tile([P, T], F32, name="page2", align_bytes=64, offset=AT_H0))
         nc.gpsimd.memset(pages[2][:].bitcast(I32), 0)
         y00 = with_bias(early_sums(0, 0), 0, "y00")
         sums20 = early_sums(2, 0)

@@ -26,8 +26,9 @@ BLOCKS = J // BLOCK
 CHUNK = 2 * BLOCK
 HALF = J // 2
 PAGES = 3
-SCALAR_M = (88, 48)
-VECTOR_BLOCKS = 4
+SCALAR_M = (88, 40)
+VECTOR_BLOCKS = BLOCKS // 2
+EARLY_GATHERS = ((0, 1), (1, 2), (2, 4), (4, BLOCKS - 1))
 GATE_BANK = (0, 1, 2, 3, 4, 1, 1, 2)
 UP_BANK = (4, 5, 6, 7, 0, 2, 0, 1)
 EARLY_DOWN_BANK = ((0, 1, 2), (3, 6, 7))
@@ -41,8 +42,8 @@ AT_H0 = AT_GEL0 + 4 * BANK
 AT_WG_SC = AT_H0 + 4 * T + 8 * BLOCK
 AT_WU0 = AT_WG_SC + 32 * BLOCK
 AT_WU1 = AT_WU0 + 16 * R
-AT_Y00 = AT_WU1 + 16 * R
-AT_TAB = (AT_Y00 + 4 * CHUNK, AT_Y00 + 4 * CHUNK + 4 * T)
+AT_Y10 = AT_WU1 + 16 * R
+AT_TAB = (AT_Y10 + 4 * CHUNK, AT_Y10 + 4 * CHUNK + 4 * T)
 AT_H1 = AT_TAB[1] + 4 * T - OVERLAP
 AT_H2 = AT_H1 + 8 * CHUNK - OVERLAP
 
@@ -137,7 +138,7 @@ def tile_list_modp_ggelu_noneb_kernel(
             wg_sc_raw[:].rearrange("p (a m t) -> p a t m", a=PASSES, t=4),
         )
         gather_words(0, 2, 4, AT_WG_SC - 8 * BLOCK + OVERLAP)
-        gather_words(0, 4, 8, AT_WG_SC + OVERLAP)
+        gather_words(0, 4, BLOCKS, AT_WG_SC + OVERLAP)
 
         wu_bf = [
             placed.tile([P, 4 * R], BF16, name=f"wu_bf{a}", align_bytes=64, offset=at)[:]
@@ -152,7 +153,7 @@ def tile_list_modp_ggelu_noneb_kernel(
             nc.vector.tensor_copy(rounded[:, SCALAR_M[a] : P], dealt[:, SCALAR_M[a] : P])
             nc.vector.quantize_mx(out=wu_q[a][:].bitcast(FP8X4), scales=wu_sc[a][:], in_=wu_bf[a])
 
-        for blk0, blk1 in ((0, 1), (1, 2), (2, 4), (4, 7)):
+        for blk0, blk1 in EARLY_GATHERS:
             gather_words(1, blk0, blk1, AT_WU1 + 4 * BLOCK * blk0)
 
         wd_bytes = placed.tile([P, 3 * N], U8, name="wd_bytes", align_bytes=64, offset=AT_TAB_SC + OVERLAP + J)
@@ -162,14 +163,14 @@ def tile_list_modp_ggelu_noneb_kernel(
         router_w = epilogue[:, 0:J]
         bias = epilogue[:, J : J + N // P]
         nc.sync.dma_start(wd.bitcast(I32), wd_words[0].bitcast(I32))
-        nc.sync.dma_start(router_w[:, 0:HALF], wgo[:, 0:HALF])
-        with nc.allow_non_contiguous_dma(reason="one bias value a partition"):
-            nc.sync.dma_start(bias, b.rearrange("(c p) -> p c", p=P))
         for q in range(4):
             nc.sync.dma_start(
                 wd_bytes[32 * q : 32 * q + 4, 0:N].bitcast(I32), wd_scales[0, 4 * q : 4 * q + 4, :].bitcast(I32)
             )
-        nc.sync.dma_start(router_w[:, HALF:J], wgo[:, HALF:J])
+        with nc.allow_non_contiguous_dma(reason="one bias value a partition"):
+            nc.sync.dma_start(bias, b.rearrange("(c p) -> p c", p=P))
+        for j0 in (0, HALF):
+            nc.sync.dma_start(router_w[:, j0 : j0 + HALF], wgo[:, j0 : j0 + HALF])
 
         h_bf = [
             placed.tile([P, 4 * width], BF16, name=f"h_bf{n}", align_bytes=64, offset=at)
@@ -261,14 +262,11 @@ def tile_list_modp_ggelu_noneb_kernel(
         def product_on_gpsimd(blk):
             nc.gpsimd.tensor_tensor(h_block(blk), factors[blk][:, 0, :], factors[blk][:, 1, :], MULT)
 
-        def quantise_h(n, j0, j1):
-            if n == 1:
-                h_q[j0] = placed.tile(
-                    [P, j1 - j0], U32, name="h_q1", align_bytes=64, offset=AT_Y00
-                )
-            else:
-                h_q[j0] = keep.tile([P, j1 - j0], U32, name=f"h_q{n}", align_bytes=64)
-            nc.vector.quantize_mx(out=h_q[j0][:].bitcast(FP8X4), scales=h_sc[:, j0:j1], in_=h_bf[n][:])
+        def quantise_h(n, j0, codes):
+            h_q[j0] = codes
+            nc.vector.quantize_mx(
+                out=codes[:].bitcast(FP8X4), scales=h_sc[:, j0 : j0 + codes.shape[1]], in_=h_bf[n][:]
+            )
 
         def down_sums(c, j0, j1, sums):
             nc.tensor.matmul_mx(
@@ -285,13 +283,12 @@ def tile_list_modp_ggelu_noneb_kernel(
         def early_sums(c, n):
             return down_sums(c, CHUNK * n, CHUNK * (n + 1), bank(EARLY_DOWN_BANK[n][c])[:, 0:CHUNK])
 
-        def with_bias(sums, c, slot):
-            if slot == "y10":
-                y = placed.tile([P, CHUNK], F32, name=slot, align_bytes=64, offset=AT_Y00)
-            else:
-                y = ring.tile([P, CHUNK], F32, name="y", tag=slot, align_bytes=64)
-            nc.scalar.activation(y[:], sums, IDENT, bias=bias[:, c : c + 1])
-            return y[:]
+        def with_bias(sums, c, y):
+            nc.scalar.activation(y, sums, IDENT, bias=bias[:, c : c + 1])
+            return y
+
+        def y_in_slot(slot):
+            return ring.tile([P, CHUNK], F32, name="y", tag=slot, align_bytes=64)[:]
 
         def scaled_on_gpsimd(y, c, n):
             scaled = keep.tile([P, CHUNK], F32, name=f"scaled{c}_{n}")
@@ -321,38 +318,42 @@ def tile_list_modp_ggelu_noneb_kernel(
                 starts = [j for j in h_q if s <= j < s + BANK]
                 for a0, a1 in zip(starts, starts[1:] + [s + BANK]):
                     down_sums(c, a0, a1, sums[:, a0 - s : a1 - s])
-                nc.scalar.activation(y[:, s - j0 : s - j0 + BANK], sums[:], IDENT, bias=bias[:, c : c + 1])
+                with_bias(sums[:], c, y[:, s - j0 : s - j0 + BANK])
             return y[:]
 
         for blk in range(VECTOR_BLOCKS):
             gate_pass(blk, 0)
         for blk in range(VECTOR_BLOCKS):
             up_pass(blk, 0)
-        for blk in range(VECTOR_BLOCKS):
-            gate_pass(blk, 1)
-            up_pass(blk, 1)
+        for first in range(0, VECTOR_BLOCKS, 2):
+            for last_pass in (gate_pass, up_pass):
+                for blk in (first, first + 1):
+                    last_pass(blk, 1)
         product(0)
         product(1)
-        gather_words(1, 7, 8, AT_GEL0)
-        quantise_h(0, 0, CHUNK)
+        gather_words(1, BLOCKS - 1, BLOCKS, AT_GEL0)
+        quantise_h(0, 0, keep.tile([P, CHUNK], U32, name="h_q0", align_bytes=64))
         pages.append(placed.tile([P, T], F32, name="page2", align_bytes=64, offset=AT_H0))
         nc.gpsimd.memset(pages[2][:].bitcast(I32), 0)
-        y00 = with_bias(early_sums(0, 0), 0, "y00")
+        sums00 = early_sums(0, 0)
+        y00 = with_bias(sums00, 0, y_in_slot("y00"))
         sums20 = early_sums(2, 0)
-        scaled10 = scaled_on_gpsimd(with_bias(early_sums(1, 0), 1, "y10"), 1, 0)
+        sums10 = early_sums(1, 0)
+        y10 = placed.tile([P, CHUNK], F32, name="y10", align_bytes=64, offset=AT_Y10)
+        scaled10 = scaled_on_gpsimd(with_bias(sums10, 1, y10[:]), 1, 0)
         product(2)
         product(3)
         scaled20 = scaled_on_vector(sums20, 2, 0)
         put(y00, 0, 0, CHUNK)
         put_scaled(scaled20, 2, 0)
-        quantise_h(1, CHUNK, HALF)
+        quantise_h(1, CHUNK, placed.tile([P, CHUNK], U32, name="h_q1", align_bytes=64, offset=AT_Y10))
         put_scaled(scaled10, 1, 0)
         both_sums(4)
         product_on_gpsimd(4)
         gate_sums(5)
-        sums = [early_sums(c, 1) for c in range(PAGES)]
-        scaled01 = scaled_on_vector(sums[0], 0, 1)
-        scaled11 = scaled_on_vector(sums[1], 1, 1)
+        sums01, sums11, sums21 = [early_sums(c, 1) for c in range(PAGES)]
+        scaled01 = scaled_on_vector(sums01, 0, 1)
+        scaled11 = scaled_on_vector(sums11, 1, 1)
         put_scaled(scaled01, 0, 1)
         put_scaled(scaled11, 1, 1)
         up_sums(5)
@@ -360,8 +361,8 @@ def tile_list_modp_ggelu_noneb_kernel(
         for blk in (6, 7):
             both_sums(blk)
             product_on_gpsimd(blk)
-        quantise_h(2, HALF, J)
-        put(with_bias(sums[2], 2, f"factors{BLOCKS - 1}"), 2, CHUNK, HALF)
+        quantise_h(2, HALF, keep.tile([P, HALF], U32, name="h_q2", align_bytes=64))
+        put(with_bias(sums21, 2, y_in_slot(f"factors{BLOCKS - 1}")), 2, CHUNK, HALF)
         for c in range(PAGES):
             put(down(c, HALF, J), c, HALF, J)
         put(down(PAGES, 0, J), PAGES, 0, J)

@@ -25,27 +25,29 @@ BLOCK = 128
 BLOCKS = J // BLOCK
 CHUNK = 2 * BLOCK
 HALF = J // 2
-PAGES = 3
-SCALAR_M = (88, 40)
-VECTOR_BLOCKS = BLOCKS // 2
-EARLY_GATHERS = ((0, 1), (1, 2), (2, 4), (4, BLOCKS - 1))
-GATE_BANK = (0, 1, 2, 3, 4, 1, 1, 2)
-UP_BANK = (4, 5, 6, 7, 0, 2, 0, 1)
-EARLY_DOWN_BANK = ((0, 1, 2), (3, 6, 7))
-LATE_DOWN_BANK = (4, 5)
+PAGES = N // P
 OVERLAP = 64
-AT_TAB_SC = 4 * J
-AT_WU_BF0 = AT_TAB_SC + 2 * T
-AT_WU_BF1 = AT_WU_BF0 + 8 * R
-AT_GEL0 = AT_WU_BF1 + 8 * R
-AT_H0 = AT_GEL0 + 4 * BANK
-AT_WG_SC = AT_H0 + 4 * T + 8 * BLOCK
-AT_WU0 = AT_WG_SC + 32 * BLOCK
-AT_WU1 = AT_WU0 + 16 * R
-AT_Y10 = AT_WU1 + 16 * R
-AT_TAB = (AT_Y10 + 4 * CHUNK, AT_Y10 + 4 * CHUNK + 4 * T)
-AT_H1 = AT_TAB[1] + 4 * T - OVERLAP
-AT_H2 = AT_H1 + 8 * CHUNK - OVERLAP
+WORD_ROW = BLOCK + OVERLAP // 4
+BYTE_ROW = CHUNK + OVERLAP
+SCALAR_M1 = 44
+GATE_BANK = (0, 1, 2, 3, 4, 0, 4, 4)
+UP_BANK = (4, 5, 6, 7, 5, 1, 5, 5)
+LATE_DOWN_BANK = (2, 3, 6, 7)
+AT_H2 = 0
+AT_SCALED30 = AT_H2 + 8 * HALF
+AT_H1 = AT_SCALED30 - OVERLAP
+AT_SCALED20 = AT_SCALED30 + 4 * CHUNK
+AT_TAB1 = AT_H1 + 8 * CHUNK - OVERLAP
+AT_TAB_SC = AT_TAB1 + 4 * T - OVERLAP
+AT_WD = AT_TAB_SC + OVERLAP
+AT_EPILOGUE = AT_WD + 3 * N
+AT_WG_RAW = AT_EPILOGUE + 4 * J + OVERLAP
+AT_PAGE2 = AT_WG_RAW + 4 * R - OVERLAP
+AT_PAGE3 = AT_PAGE2 + 4 * T
+AT_WG_SC = AT_PAGE3 + 4 * T - OVERLAP
+AT_WU1 = AT_WG_SC + OVERLAP + 4 * WORD_ROW * 5
+AT_GEL0 = AT_WU1 + 16 * R
+AT_Y10 = AT_GEL0 + 4 * BANK
 
 
 def tile_list_modp_ggelu_noneb_kernel(
@@ -58,26 +60,36 @@ def tile_list_modp_ggelu_noneb_kernel(
         placed = ctx.enter_context(tc.tile_pool(name="placed", bufs=1))
         psum = ctx.enter_context(tc.psum_pool(name="psum", bufs=1))
 
+        def at(offset, shape, dtype, name):
+            return placed.tile(shape, dtype, name=name, align_bytes=64, offset=offset)
+
+        def held(shape, dtype, name):
+            return keep.tile(shape, dtype, name=name, align_bytes=64)
+
         offsets = keep.tile([P, J // 16], U16, name="offsets")
         nc.sync.dma_start(offsets[:], offs)
 
         def listed(j0, j1):
             return offsets[:, j0 // 16 : j1 // 16]
 
-        wg_raw = keep.tile([P, PASSES * 2 * R], U8, name="wg_raw", align_bytes=64)
+        def zero_on_own_port(words):
+            count = words.shape[1]
+            nc.vector.memset(words[:, 0 : count - 1], 0)
+            nc.vector.memset(words[:, count - 1 : count], 0)
+
+        wg_raw = at(AT_WG_RAW, [P, PASSES * 2 * R], U8, "wg_raw")
         nc.sync.dma_start(
             wg_raw[:].bitcast(I32).rearrange("p (a n) -> p a n", a=PASSES),
             wg_words.rearrange("a p n -> p a n").bitcast(I32),
         )
-        tab_sc = placed.tile([P, T], U8, name="tab_sc", align_bytes=64, offset=AT_TAB_SC)
+        tab_sc = at(AT_TAB_SC, [P, T], U8, "tab_sc")
         nc.gpsimd.memset(tab_sc[:].bitcast(I32), 0)
         for r in range(4):
             nc.sync.dma_start(
                 tab_sc[r:P:16, :].bitcast(I32), tab_scales[:, r:16:4, :].rearrange("a q t -> q a t").bitcast(I32)
             )
 
-        def load_tab(a):
-            words = placed.tile([P, T], I32, name=f"tab{a}", align_bytes=64, offset=AT_TAB[a])
+        def load_tab(a, words):
             nc.sync.dma_start(words[:], tab_words[a].rearrange("p t i -> p (t i)").bitcast(I32))
             return words
 
@@ -85,111 +97,117 @@ def tile_list_modp_ggelu_noneb_kernel(
             nc.sync.dma_start(raw[:], wu[512 * a : 512 * (a + 1), :].rearrange("(p i) r -> p i r", i=4))
             return raw
 
-        tab = [load_tab(0)]
-        wg_sc_raw = placed.tile([P, PASSES * R], U8, name="wg_sc_raw", align_bytes=64, offset=AT_WG_SC)
-        nc.gpsimd.memset(wg_sc_raw[:].bitcast(I32), 0)
+        tab = [load_tab(0, held([P, T], I32, "tab0"))]
+        wg_sc_raw = at(AT_WG_SC, [P, PASSES * R], U8, "wg_sc_raw")
+        zero_on_own_port(wg_sc_raw[:].bitcast(I32))
         for q in range(4):
             nc.sync.dma_start(
                 wg_sc_raw[32 * q : 32 * q + 4, :].bitcast(I32).rearrange("p (a n) -> p a n", a=PASSES),
                 wg_scales[:, 4 * q : 4 * q + 4, :].rearrange("a g n -> g a n").bitcast(I32),
             )
-        wu_raw = [
-            load_wu(0, placed.tile([P, 4, R], F32, name="wu_raw0", align_bytes=64, offset=AT_WU0)),
-            load_wu(1, placed.tile([P, 4, R], F32, name="wu_raw1", align_bytes=64, offset=AT_WU1)),
-        ]
-        tab.append(load_tab(1))
+        wu_raw = [load_wu(0, held([P, 4, R], F32, "wu_raw0")), load_wu(1, at(AT_WU1, [P, 4, R], F32, "wu_raw1"))]
 
-        pages = [keep.tile([P, T], F32, name=f"page{c}") for c in range(PAGES - 1)]
-        nc.vector.memset(pages[0][:, 0 : T - 1].bitcast(I32), 0)
-        nc.vector.memset(pages[0][:, T - 1 : T].bitcast(I32), 0)
+        pages = [held([P, T], F32, "page0"), held([P, T], F32, "page1")]
+        zero_on_own_port(pages[0][:].bitcast(I32))
         nc.gpsimd.memset(pages[1][:].bitcast(I32), 0)
 
-        picked_sc = keep.tile([P, J], U8, name="picked_sc", align_bytes=64)
-        nc.vector.tensor_copy(picked_sc[:], tab_sc[:].indirect(offsets[:]))
-        moved_sc = placed.tile([P, J], U8, name="moved_sc", align_bytes=64, offset=AT_TAB_SC + OVERLAP)
-        for q in range(4):
-            nc.sync.dma_start(
-                moved_sc[32 * q : 32 * q + 4, :].bitcast(I32), picked_sc[32 * q + 16 : 32 * q + 20, :].bitcast(I32)
-            )
-        v_sc = [picked_sc, moved_sc]
-
-        wg = keep.tile([P, PASSES * 2 * R], U8, name="wg", align_bytes=64)
+        wg = held([P, PASSES * 2 * R], U8, "wg")
         nc.scalar.copy(
             wg[:].bitcast(U16).rearrange("p (a t m) -> p a t m", a=PASSES, t=4),
             wg_raw[:].bitcast(U16).rearrange("p (a m t) -> p a t m", a=PASSES, t=4),
         )
+        pages.append(at(AT_PAGE2, [P, T], F32, "page2"))
+        nc.gpsimd.memset(pages[2][:].bitcast(I32), 0)
+
+        picked_sc = held([P, 4, BYTE_ROW], U8, "picked_sc")
+        nc.vector.tensor_copy(picked_sc[:, 0, 0:CHUNK], tab_sc[:].indirect(listed(0, CHUNK)))
+        nc.vector.tensor_copy(picked_sc[:, 1:4, 0:CHUNK], tab_sc[:].indirect(listed(CHUNK, J)))
+        moved_sc = at(AT_WG_RAW, [P, J], U8, "moved_sc")
+        for q in range(4):
+            nc.sync.dma_start(
+                moved_sc[32 * q : 32 * q + 4, :].bitcast(I32).rearrange("p (n c) -> p n c", n=4),
+                picked_sc[32 * q + 16 : 32 * q + 20, :, 0:CHUNK].bitcast(I32),
+            )
+
+        tab.append(load_tab(1, at(AT_TAB1, [P, T], I32, "tab1")))
+
+        def v_sc(a, blk):
+            if a == 0:
+                return picked_sc[:, blk // 2, BLOCK * (blk % 2) : BLOCK * (blk % 2 + 1)]
+            return moved_sc[:, BLOCK * blk : BLOCK * (blk + 1)]
 
         v = {}
 
-        def gather_words(a, blk0, blk1, at=None):
-            shape = [P, BLOCK * (blk1 - blk0)]
-            if at is None:
-                picked = keep.tile(shape, U32, name=f"v{a}_{blk0}", align_bytes=64)
-            else:
-                picked = placed.tile(shape, U32, name=f"v{a}_{blk0}", align_bytes=64, offset=at)
-            nc.vector.tensor_copy(picked[:], tab[a][:].bitcast(U32).indirect(listed(BLOCK * blk0, BLOCK * blk1)))
+        def gather_words(a, blk0, blk1, picked):
+            window = tab[a][:].bitcast(U32).indirect(listed(BLOCK * blk0, BLOCK * blk1))
+            nc.vector.tensor_copy(picked[:, :, 0:BLOCK], window)
             for blk in range(blk0, blk1):
-                v[a, blk] = picked[:, BLOCK * (blk - blk0) : BLOCK * (blk - blk0 + 1)]
+                v[a, blk] = picked[:, blk - blk0, 0:BLOCK]
 
-        gather_words(0, 0, 2)
-        wg_sc = keep.tile([P, PASSES * R], U8, name="wg_sc", align_bytes=64)
+        gather_words(0, 0, 3, held([P, 3, WORD_ROW], U32, "v0_0"))
+        wg_sc = held([P, PASSES * R], U8, "wg_sc")
         nc.vector.tensor_copy(
             wg_sc[:].rearrange("p (a t m) -> p a t m", a=PASSES, t=4),
             wg_sc_raw[:].rearrange("p (a m t) -> p a t m", a=PASSES, t=4),
         )
-        gather_words(0, 2, 4, AT_WG_SC - 8 * BLOCK + OVERLAP)
-        gather_words(0, 4, BLOCKS, AT_WG_SC + OVERLAP)
+        gather_words(0, 3, BLOCKS, at(AT_WG_SC + OVERLAP, [P, 5, WORD_ROW], U32, "v0_3"))
+        pages.append(at(AT_PAGE3, [P, T], F32, "page3"))
+        nc.gpsimd.memset(pages[3][:].bitcast(I32), 0)
 
-        wu_bf = [
-            placed.tile([P, 4 * R], BF16, name=f"wu_bf{a}", align_bytes=64, offset=at)[:]
-            for a, at in enumerate((AT_WU_BF0, AT_WU_BF1))
-        ]
-        wu_q = [keep.tile([P, R], U32, name=f"wu_q{a}", align_bytes=64) for a in range(PASSES)]
-        wu_sc = [keep.tile([P, R], U8, name=f"wu_sc{a}", align_bytes=64) for a in range(PASSES)]
+        wu_bf = [held([P, 4 * R], BF16, f"wu_bf{a}") for a in range(PASSES)]
+        wu_q = [held([P, R], U32, f"wu_q{a}") for a in range(PASSES)]
+        wu_sc = [held([P, R], U8, f"wu_sc{a}") for a in range(PASSES)]
+        rounded = [wu_bf[a][:].rearrange("p (t m i) -> p m i t", t=4, i=4) for a in range(PASSES)]
+        dealt = [wu_raw[a][:].rearrange("p i (m t) -> p m i t", t=4) for a in range(PASSES)]
+        nc.scalar.copy(rounded[0], dealt[0])
+        nc.scalar.copy(rounded[1][:, 0:SCALAR_M1], dealt[1][:, 0:SCALAR_M1])
+        nc.vector.tensor_copy(rounded[1][:, SCALAR_M1:P], dealt[1][:, SCALAR_M1:P])
         for a in range(PASSES):
-            rounded = wu_bf[a].rearrange("p (t m i) -> p m i t", t=4, i=4)
-            dealt = wu_raw[a][:].rearrange("p i (m t) -> p m i t", t=4)
-            nc.scalar.copy(rounded[:, 0 : SCALAR_M[a]], dealt[:, 0 : SCALAR_M[a]])
-            nc.vector.tensor_copy(rounded[:, SCALAR_M[a] : P], dealt[:, SCALAR_M[a] : P])
-            nc.vector.quantize_mx(out=wu_q[a][:].bitcast(FP8X4), scales=wu_sc[a][:], in_=wu_bf[a])
+            nc.vector.quantize_mx(out=wu_q[a][:].bitcast(FP8X4), scales=wu_sc[a][:], in_=wu_bf[a][:])
 
-        for blk0, blk1 in EARLY_GATHERS:
-            gather_words(1, blk0, blk1, AT_WU1 + 4 * BLOCK * blk0)
+        for blk0, blk1 in ((0, 1), (1, 2), (2, 4), (4, 7)):
+            gather_words(1, blk0, blk1, at(AT_WU1 + 4 * BLOCK * blk0, [P, blk1 - blk0, BLOCK], U32, f"v1_{blk0}"))
 
-        wd_bytes = placed.tile([P, 3 * N], U8, name="wd_bytes", align_bytes=64, offset=AT_TAB_SC + OVERLAP + J)
+        wd_bytes = at(AT_WD, [P, 3 * N], U8, "wd_bytes")
         wd_sc = wd_bytes[:, 0:N]
         wd = wd_bytes[:, N : 3 * N]
-        epilogue = placed.tile([P, J + N // P], F32, name="epilogue", align_bytes=64, offset=AT_TAB_SC - 4 * J)
+        epilogue = at(AT_EPILOGUE, [P, J + N // P], F32, "epilogue")
         router_w = epilogue[:, 0:J]
         bias = epilogue[:, J : J + N // P]
+        nc.sync.dma_start(router_w[:, 0:HALF], wgo[:, 0:HALF])
+        with nc.allow_non_contiguous_dma(reason="one bias value a partition"):
+            nc.sync.dma_start(bias, b.rearrange("(c p) -> p c", p=P))
         nc.sync.dma_start(wd.bitcast(I32), wd_words[0].bitcast(I32))
         for q in range(4):
             nc.sync.dma_start(
                 wd_bytes[32 * q : 32 * q + 4, 0:N].bitcast(I32), wd_scales[0, 4 * q : 4 * q + 4, :].bitcast(I32)
             )
-        with nc.allow_non_contiguous_dma(reason="one bias value a partition"):
-            nc.sync.dma_start(bias, b.rearrange("(c p) -> p c", p=P))
-        for j0 in (0, HALF):
-            nc.sync.dma_start(router_w[:, j0 : j0 + HALF], wgo[:, j0 : j0 + HALF])
+        nc.sync.dma_start(router_w[:, HALF:J], wgo[:, HALF:J])
 
         h_bf = [
-            placed.tile([P, 4 * width], BF16, name=f"h_bf{n}", align_bytes=64, offset=at)
-            for n, (width, at) in enumerate(((CHUNK, AT_H0), (CHUNK, AT_H1), (HALF, AT_H2)))
+            held([P, 4 * CHUNK], BF16, "h_bf0")[:],
+            at(AT_H1, [P, 4 * CHUNK], BF16, "h_bf1")[:],
+            at(AT_H2, [P, 4 * HALF], BF16, "h_bf2")[:],
         ]
         h_q = {}
-        h_sc = keep.tile([P, J], U8, name="h_sc", align_bytes=64)
-        gel = [placed.tile([P, BANK], F32, name="gel0", align_bytes=64, offset=AT_GEL0)] + [
-            keep.tile([P, BANK], F32, name=f"gel{blk}", align_bytes=64) for blk in range(1, VECTOR_BLOCKS)
-        ]
+        h_sc = held([P, J], U8, "h_sc")
+        gel = {0: at(AT_GEL0, [P, BANK], F32, "gel0")}
+        for blk in (1, 2):
+            gel[blk] = held([P, BANK], F32, f"gel{blk}")
+        runs = {3: 1, 4: 2, 6: 2}
         factors = {
-            blk: ring.tile([P, 2, BANK], F32, name="factors", tag=f"factors{blk}", align_bytes=64)
-            for blk in range(VECTOR_BLOCKS, BLOCKS)
+            first: ring.tile([P, 2, count * BANK], F32, name="factors", tag=f"factors{first}", align_bytes=64)
+            for first, count in runs.items()
         }
         ga = {}
         ub = {}
         from_bank = "p (t n e) -> p n t e"
         by_pairs = "p (n t e) -> p n t e"
         by_token = "p (n e t) -> p n t e"
+
+        def factor(blk, which):
+            first = blk if blk in runs else blk - 1
+            return factors[first][:, which, BANK * (blk - first) : BANK * (blk - first + 1)]
 
         def bank(n):
             return psum.tile([P, BANK], F32, name="bank", tag=f"bank{n}")
@@ -201,7 +219,7 @@ def tile_list_modp_ggelu_noneb_kernel(
                     lhsT=codes(t),
                     lhsT_scale=scales[:, P * t : P * (t + 1)],
                     rhs=v[a, blk].bitcast(FP8X4),
-                    rhs_scale=v_sc[a][:, BLOCK * blk : BLOCK * (blk + 1)],
+                    rhs_scale=v_sc(a, blk),
                     start=(a == 0 and t == 0),
                     stop=(a == PASSES - 1 and t == 3),
                 )
@@ -216,10 +234,10 @@ def tile_list_modp_ggelu_noneb_kernel(
 
             first_stage_pass(ga[blk], blk, a, codes, wg_sc[:, R * a : R * (a + 1)])
             if a == PASSES - 1:
-                if blk < VECTOR_BLOCKS:
+                if blk in gel:
                     result = gel[blk][:].rearrange(by_pairs, t=4, e=2)
                 else:
-                    result = factors[blk][:, 0, :].rearrange(by_token, t=4, e=2)
+                    result = factor(blk, 0).rearrange(by_token, t=4, e=2)
                 nc.scalar.activation(result, ga[blk][:].rearrange(from_bank, t=4, e=2), GELU)
 
         def up_pass(blk, a):
@@ -230,43 +248,32 @@ def tile_list_modp_ggelu_noneb_kernel(
                 return wu_q[a][:, P * t : P * (t + 1)].bitcast(FP8X4)
 
             first_stage_pass(ub[blk], blk, a, codes, wu_sc[a])
-            if a == PASSES - 1 and blk >= VECTOR_BLOCKS:
-                nc.scalar.copy(
-                    factors[blk][:, 1, :].rearrange(by_token, t=4, e=2), ub[blk][:].rearrange(from_bank, t=4, e=2)
-                )
-
-        def gate_sums(blk):
-            for a in range(PASSES):
-                gate_pass(blk, a)
-
-        def up_sums(blk):
-            for a in range(PASSES):
-                up_pass(blk, a)
+            if a == PASSES - 1 and blk not in gel:
+                nc.scalar.copy(factor(blk, 1).rearrange(by_token, t=4, e=2), ub[blk][:].rearrange(from_bank, t=4, e=2))
 
         def both_sums(blk):
-            gate_sums(blk)
-            up_sums(blk)
+            for stage in (gate_pass, up_pass):
+                for a in range(PASSES):
+                    stage(blk, a)
 
-        def h_block(blk):
+        def h_blocks(blk, count):
             n = min(blk // 2, 2)
-            return h_bf[n][:, BANK * (blk - 2 * n) : BANK * (blk - 2 * n + 1)]
+            return h_bf[n][:, BANK * (blk - 2 * n) : BANK * (blk - 2 * n + count)]
 
         def product(blk):
             nc.vector.tensor_tensor(
-                h_block(blk).rearrange(by_token, t=4, e=2),
+                h_blocks(blk, 1).rearrange(by_token, t=4, e=2),
                 ub[blk][:].rearrange(from_bank, t=4, e=2),
                 gel[blk][:].rearrange(by_pairs, t=4, e=2),
                 MULT,
             )
 
-        def product_on_gpsimd(blk):
-            nc.gpsimd.tensor_tensor(h_block(blk), factors[blk][:, 0, :], factors[blk][:, 1, :], MULT)
+        def product_on_gpsimd(first):
+            nc.gpsimd.tensor_tensor(h_blocks(first, runs[first]), factors[first][:, 0, :], factors[first][:, 1, :], MULT)
 
         def quantise_h(n, j0, codes):
             h_q[j0] = codes
-            nc.vector.quantize_mx(
-                out=codes[:].bitcast(FP8X4), scales=h_sc[:, j0 : j0 + codes.shape[1]], in_=h_bf[n][:]
-            )
+            nc.vector.quantize_mx(out=codes[:].bitcast(FP8X4), scales=h_sc[:, j0 : j0 + codes.shape[1]], in_=h_bf[n])
 
         def down_sums(c, j0, j1, sums):
             nc.tensor.matmul_mx(
@@ -280,89 +287,77 @@ def tile_list_modp_ggelu_noneb_kernel(
             )
             return sums
 
-        def early_sums(c, n):
-            return down_sums(c, CHUNK * n, CHUNK * (n + 1), bank(EARLY_DOWN_BANK[n][c])[:, 0:CHUNK])
+        def early_sums(rows, n, in_bank):
+            sums = bank(in_bank)
+            return [
+                down_sums(c, CHUNK * n, CHUNK * (n + 1), sums[:, CHUNK * i : CHUNK * (i + 1)])
+                for i, c in enumerate(rows)
+            ]
 
         def with_bias(sums, c, y):
             nc.scalar.activation(y, sums, IDENT, bias=bias[:, c : c + 1])
             return y
 
-        def y_in_slot(slot):
-            return ring.tile([P, CHUNK], F32, name="y", tag=slot, align_bytes=64)[:]
-
-        def scaled_on_gpsimd(y, c, n):
-            scaled = keep.tile([P, CHUNK], F32, name=f"scaled{c}_{n}")
+        def scaled_on_gpsimd(y, n, scaled):
             nc.gpsimd.tensor_tensor(scaled[:], y, router_w[:, CHUNK * n : CHUNK * (n + 1)], MULT)
             return scaled
 
-        def scaled_on_vector(sums, c, n):
-            scaled = keep.tile([P, CHUNK], F32, name=f"scaled{c}_{n}")
-            nc.vector.scalar_tensor_tensor(
-                scaled[:], sums, bias[:, c : c + 1], router_w[:, CHUNK * n : CHUNK * (n + 1)], ADD, MULT
-            )
-            return scaled
+        def fresh(c, n):
+            return held([P, CHUNK], F32, f"scaled{c}{n}")
 
         def put_scaled(scaled, c, n):
             nc.vector.tensor_copy(pages[c][:].indirect(listed(CHUNK * n, CHUNK * (n + 1))), scaled[:])
 
         def put(y, c, j0, j1):
-            page = pages[c % PAGES]
-            nc.vector.tensor_tensor(page[:].indirect(listed(j0, j1)), y, router_w[:, j0:j1], MULT)
-            if j1 == J:
-                nc.sync.dma_start(out[P * c : P * (c + 1), :], page[:])
+            nc.vector.tensor_tensor(pages[c][:].indirect(listed(j0, j1)), y, router_w[:, j0:j1], MULT)
 
-        def down(c, j0, j1):
-            y = keep.tile([P, j1 - j0], F32, name=f"late_y{c}")
-            for s in range(j0, j1, BANK):
-                sums = bank(LATE_DOWN_BANK[(c + s // BANK) % 2])
-                starts = [j for j in h_q if s <= j < s + BANK]
-                for a0, a1 in zip(starts, starts[1:] + [s + BANK]):
-                    down_sums(c, a0, a1, sums[:, a0 - s : a1 - s])
-                with_bias(sums[:], c, y[:, s - j0 : s - j0 + BANK])
-            return y[:]
-
-        for blk in range(VECTOR_BLOCKS):
+        for blk in range(4):
             gate_pass(blk, 0)
-        for blk in range(VECTOR_BLOCKS):
-            up_pass(blk, 0)
-        for first in range(0, VECTOR_BLOCKS, 2):
-            for last_pass in (gate_pass, up_pass):
-                for blk in (first, first + 1):
-                    last_pass(blk, 1)
+        for pair in ((0, 1), (2, 3)):
+            for blk in pair:
+                gate_pass(blk, 1)
+            for a in range(PASSES):
+                for blk in pair:
+                    up_pass(blk, a)
         product(0)
         product(1)
-        gather_words(1, BLOCKS - 1, BLOCKS, AT_GEL0)
-        quantise_h(0, 0, keep.tile([P, CHUNK], U32, name="h_q0", align_bytes=64))
-        pages.append(placed.tile([P, T], F32, name="page2", align_bytes=64, offset=AT_H0))
-        nc.gpsimd.memset(pages[2][:].bitcast(I32), 0)
-        sums00 = early_sums(0, 0)
-        y00 = with_bias(sums00, 0, y_in_slot("y00"))
-        sums20 = early_sums(2, 0)
-        sums10 = early_sums(1, 0)
-        y10 = placed.tile([P, CHUNK], F32, name="y10", align_bytes=64, offset=AT_Y10)
-        scaled10 = scaled_on_gpsimd(with_bias(sums10, 1, y10[:]), 1, 0)
+        gather_words(1, 7, BLOCKS, at(AT_GEL0, [P, 1, BLOCK], U32, "v1_7"))
+        quantise_h(0, 0, held([P, CHUNK], U32, "h_q0"))
         product(2)
-        product(3)
-        scaled20 = scaled_on_vector(sums20, 2, 0)
-        put(y00, 0, 0, CHUNK)
-        put_scaled(scaled20, 2, 0)
-        quantise_h(1, CHUNK, placed.tile([P, CHUNK], U32, name="h_q1", align_bytes=64, offset=AT_Y10))
+        product_on_gpsimd(3)
+        scaled00 = fresh(0, 0)
+        (sums00,) = early_sums((0,), 0, 4)
+        nc.vector.scalar_tensor_tensor(scaled00[:], sums00, bias[:, 0:1], router_w[:, 0:CHUNK], ADD, MULT)
+        put_scaled(scaled00, 0, 0)
+        y10 = with_bias(early_sums((1,), 0, 5)[0], 1, at(AT_Y10, [P, CHUNK], F32, "y10")[:])
+        y20 = with_bias(early_sums((2,), 0, 0)[0], 2, held([P, CHUNK], F32, "y20")[:])
+        y30 = with_bias(early_sums((3,), 0, 1)[0], 3, held([P, CHUNK], F32, "y30")[:])
+        scaled10 = ring.tile([P, CHUNK], F32, name="scaled10", tag="factors3", align_bytes=64)
+        scaled_on_gpsimd(y10, 0, scaled10)
+        quantise_h(1, CHUNK, at(AT_Y10, [P, CHUNK], U32, "h_q1"))
+        scaled20 = scaled_on_gpsimd(y20, 0, at(AT_SCALED20, [P, CHUNK], F32, "scaled20"))
+        scaled30 = scaled_on_gpsimd(y30, 0, at(AT_SCALED30, [P, CHUNK], F32, "scaled30"))
         put_scaled(scaled10, 1, 0)
+        put_scaled(scaled20, 2, 0)
+        put_scaled(scaled30, 3, 0)
         both_sums(4)
+        both_sums(5)
+        sums01, sums11 = early_sums((0, 1), 1, 1)
+        sums21, sums31 = early_sums((2, 3), 1, 0)
+        y01 = with_bias(sums01, 0, h_blocks(5, 1).bitcast(F32))
+        put_scaled(scaled_on_gpsimd(y01, 1, fresh(0, 1)), 0, 1)
+        y11 = with_bias(sums11, 1, h_blocks(7, 1).bitcast(F32))
+        y21 = with_bias(sums21, 2, h_blocks(6, 1).bitcast(F32))
         product_on_gpsimd(4)
-        gate_sums(5)
-        sums01, sums11, sums21 = [early_sums(c, 1) for c in range(PAGES)]
-        scaled01 = scaled_on_vector(sums01, 0, 1)
-        scaled11 = scaled_on_vector(sums11, 1, 1)
-        put_scaled(scaled01, 0, 1)
-        put_scaled(scaled11, 1, 1)
-        up_sums(5)
-        product_on_gpsimd(5)
-        for blk in (6, 7):
-            both_sums(blk)
-            product_on_gpsimd(blk)
-        quantise_h(2, HALF, keep.tile([P, HALF], U32, name="h_q2", align_bytes=64))
-        put(with_bias(sums21, 2, y_in_slot(f"factors{BLOCKS - 1}")), 2, CHUNK, HALF)
+        put_scaled(scaled_on_gpsimd(y11, 1, fresh(1, 1)), 1, 1)
+        put_scaled(scaled_on_gpsimd(y21, 1, fresh(2, 1)), 2, 1)
+        both_sums(6)
+        both_sums(7)
+        product_on_gpsimd(6)
+        quantise_h(2, HALF, held([P, HALF], U32, "h_q2"))
+        y31 = ring.tile([P, CHUNK], F32, name="y31", tag="factors6", align_bytes=64)
+        put(with_bias(sums31, 3, y31[:]), 3, CHUNK, HALF)
         for c in range(PAGES):
-            put(down(c, HALF, J), c, HALF, J)
-        put(down(PAGES, 0, J), PAGES, 0, J)
+            sums = down_sums(c, HALF, J, bank(LATE_DOWN_BANK[c])[:])
+            put(with_bias(sums, c, held([P, HALF], F32, f"late_y{c}")[:]), c, HALF, J)
+            nc.sync.dma_start(out[P * c : P * (c + 1), :], pages[c][:])

@@ -38,8 +38,8 @@ AT_SCALED30 = AT_H2 + 8 * HALF
 AT_H1 = AT_SCALED30 - OVERLAP
 AT_SCALED20 = AT_SCALED30 + 4 * CHUNK
 AT_TAB1 = AT_H1 + 8 * CHUNK - OVERLAP
-AT_TAB_SC = AT_TAB1 + 4 * T - OVERLAP
-AT_WD = AT_TAB_SC + OVERLAP
+AT_TAB_SC = AT_TAB1 + 4 * T
+AT_WD = AT_TAB_SC
 AT_EPILOGUE = AT_WD + 3 * N
 AT_WG_RAW = AT_EPILOGUE + 4 * J + OVERLAP
 AT_PAGE2 = AT_WG_RAW + 4 * R - OVERLAP
@@ -67,7 +67,6 @@ def tile_list_modp_ggelu_noneb_kernel(
             return keep.tile(shape, dtype, name=name, align_bytes=64)
 
         offsets = keep.tile([P, J // 16], U16, name="offsets")
-        nc.sync.dma_start(offsets[:], offs)
 
         def listed(j0, j1):
             return offsets[:, j0 // 16 : j1 // 16]
@@ -82,6 +81,7 @@ def tile_list_modp_ggelu_noneb_kernel(
             wg_raw[:].bitcast(I32).rearrange("p (a n) -> p a n", a=PASSES),
             wg_words.rearrange("a p n -> p a n").bitcast(I32),
         )
+        nc.sync.dma_start(offsets[:], offs)
         tab_sc = at(AT_TAB_SC, [P, T], U8, "tab_sc")
         nc.gpsimd.memset(tab_sc[:].bitcast(I32), 0)
         for r in range(4):
@@ -106,6 +106,7 @@ def tile_list_modp_ggelu_noneb_kernel(
                 wg_scales[:, 4 * q : 4 * q + 4, :].rearrange("a g n -> g a n").bitcast(I32),
             )
         wu_raw = [load_wu(0, held([P, 4, R], F32, "wu_raw0")), load_wu(1, at(AT_WU1, [P, 4, R], F32, "wu_raw1"))]
+        tab.append(load_tab(1, at(AT_TAB1, [P, T], I32, "tab1")))
 
         pages = [held([P, T], F32, "page0"), held([P, T], F32, "page1")]
         zero_on_own_port(pages[0][:].bitcast(I32))
@@ -128,8 +129,6 @@ def tile_list_modp_ggelu_noneb_kernel(
                 moved_sc[32 * q : 32 * q + 4, :].bitcast(I32).rearrange("p (n c) -> p n c", n=4),
                 picked_sc[32 * q + 16 : 32 * q + 20, :, 0:CHUNK].bitcast(I32),
             )
-
-        tab.append(load_tab(1, at(AT_TAB1, [P, T], I32, "tab1")))
 
         def v_sc(a, blk):
             if a == 0:

@@ -29,7 +29,7 @@ PAGES = N // P
 OVERLAP = 64
 WORD_ROW = BLOCK + OVERLAP // 4
 BYTE_ROW = CHUNK + OVERLAP
-SCALAR_M1 = 44
+SCALAR_M = (97, 60)
 GATE_BANK = (0, 1, 2, 3, 4, 0, 4, 4)
 UP_BANK = (4, 5, 6, 7, 5, 1, 5, 5)
 LATE_DOWN_BANK = (2, 3, 6, 7)
@@ -158,10 +158,9 @@ def tile_list_modp_ggelu_noneb_kernel(
         wu_sc = [held([P, R], U8, f"wu_sc{a}") for a in range(PASSES)]
         rounded = [wu_bf[a][:].rearrange("p (t m i) -> p m i t", t=4, i=4) for a in range(PASSES)]
         dealt = [wu_raw[a][:].rearrange("p i (m t) -> p m i t", t=4) for a in range(PASSES)]
-        nc.scalar.copy(rounded[0], dealt[0])
-        nc.scalar.copy(rounded[1][:, 0:SCALAR_M1], dealt[1][:, 0:SCALAR_M1])
-        nc.vector.tensor_copy(rounded[1][:, SCALAR_M1:P], dealt[1][:, SCALAR_M1:P])
         for a in range(PASSES):
+            nc.scalar.copy(rounded[a][:, 0 : SCALAR_M[a]], dealt[a][:, 0 : SCALAR_M[a]])
+            nc.vector.tensor_copy(rounded[a][:, SCALAR_M[a] : P], dealt[a][:, SCALAR_M[a] : P])
             nc.vector.quantize_mx(out=wu_q[a][:].bitcast(FP8X4), scales=wu_sc[a][:], in_=wu_bf[a][:])
 
         for blk0, blk1 in ((0, 1), (1, 2), (2, 4), (4, 7)):
@@ -359,4 +358,8 @@ def tile_list_modp_ggelu_noneb_kernel(
         for c in range(PAGES):
             sums = down_sums(c, HALF, J, bank(LATE_DOWN_BANK[c])[:])
             put(with_bias(sums, c, held([P, HALF], F32, f"late_y{c}")[:]), c, HALF, J)
-            nc.sync.dma_start(out[P * c : P * (c + 1), :], pages[c][:])
+            if c < PAGES - 1:
+                nc.sync.dma_start(out[P * c : P * (c + 1), :], pages[c][:])
+            else:
+                for queue, t0 in ((nc.sync, 0), (nc.scalar, T // 2)):
+                    queue.dma_start(out[P * c : P * (c + 1), t0 : t0 + T // 2], pages[c][:, t0 : t0 + T // 2])

@@ -29,14 +29,13 @@ PAGES = N // P
 OVERLAP = 64
 WORD_ROW = BLOCK + OVERLAP // 4
 BYTE_ROW = CHUNK + OVERLAP
-SCALAR_M = (97, 60)
+SCALAR_M = (91, 68)
 GATE_BANK = (0, 1, 2, 3, 4, 0, 4, 4)
 UP_BANK = (4, 5, 6, 7, 5, 1, 5, 5)
-LATE_DOWN_BANK = (2, 3, 6, 7)
+LATE_DOWN_BANK = (3, 6, 7, 2)
 AT_H2 = 0
-AT_SCALED30 = AT_H2 + 8 * HALF
-AT_H1 = AT_SCALED30 - OVERLAP
-AT_SCALED20 = AT_SCALED30 + 4 * CHUNK
+AT_SCALED23 = AT_H2 + 8 * HALF
+AT_H1 = AT_SCALED23 - OVERLAP
 AT_TAB1 = AT_H1 + 8 * CHUNK - OVERLAP
 AT_TAB_SC = AT_TAB1 + 4 * T
 AT_WD = AT_TAB_SC
@@ -300,11 +299,16 @@ def tile_list_modp_ggelu_noneb_kernel(
             nc.gpsimd.tensor_tensor(scaled[:], y, router_w[:, CHUNK * n : CHUNK * (n + 1)], MULT)
             return scaled
 
+        def two_scaled_on_gpsimd(y, n, scaled):
+            weights = router_w[:, CHUNK * n : CHUNK * (n + 1)].unsqueeze(1).to_broadcast([P, 2, CHUNK])
+            nc.gpsimd.tensor_tensor(scaled[:], y, weights, MULT)
+            return scaled
+
         def fresh(c, n):
             return held([P, CHUNK], F32, f"scaled{c}{n}")
 
         def put_scaled(scaled, c, n):
-            nc.vector.tensor_copy(pages[c][:].indirect(listed(CHUNK * n, CHUNK * (n + 1))), scaled[:])
+            nc.vector.tensor_copy(pages[c][:].indirect(listed(CHUNK * n, CHUNK * (n + 1))), scaled[:, :])
 
         def put(y, c, j0, j1):
             nc.vector.tensor_tensor(pages[c][:].indirect(listed(j0, j1)), y, router_w[:, j0:j1], MULT)
@@ -328,27 +332,30 @@ def tile_list_modp_ggelu_noneb_kernel(
         nc.vector.scalar_tensor_tensor(scaled00[:], sums00, bias[:, 0:1], router_w[:, 0:CHUNK], ADD, MULT)
         put_scaled(scaled00, 0, 0)
         y10 = with_bias(early_sums((1,), 0, 5)[0], 1, at(AT_Y10, [P, CHUNK], F32, "y10")[:])
-        y20 = with_bias(early_sums((2,), 0, 0)[0], 2, held([P, CHUNK], F32, "y20")[:])
-        y30 = with_bias(early_sums((3,), 0, 1)[0], 3, held([P, CHUNK], F32, "y30")[:])
+        y23 = held([P, 2, CHUNK], F32, "y23")
+        with_bias(early_sums((2,), 0, 0)[0], 2, y23[:, 0, :])
+        with_bias(early_sums((3,), 0, 1)[0], 3, y23[:, 1, :])
         scaled10 = ring.tile([P, CHUNK], F32, name="scaled10", tag="factors3", align_bytes=64)
         scaled_on_gpsimd(y10, 0, scaled10)
         quantise_h(1, CHUNK, at(AT_Y10, [P, CHUNK], U32, "h_q1"))
-        scaled20 = scaled_on_gpsimd(y20, 0, at(AT_SCALED20, [P, CHUNK], F32, "scaled20"))
-        scaled30 = scaled_on_gpsimd(y30, 0, at(AT_SCALED30, [P, CHUNK], F32, "scaled30"))
+        scaled23 = two_scaled_on_gpsimd(y23[:], 0, at(AT_SCALED23, [P, 2, CHUNK], F32, "scaled23"))
         put_scaled(scaled10, 1, 0)
-        put_scaled(scaled20, 2, 0)
-        put_scaled(scaled30, 3, 0)
+        put_scaled(scaled23[:, 0, :], 2, 0)
+        put_scaled(scaled23[:, 1, :], 3, 0)
         both_sums(4)
         both_sums(5)
-        sums01, sums11 = early_sums((0, 1), 1, 1)
-        sums21, sums31 = early_sums((2, 3), 1, 0)
+        (sums01,) = early_sums((0,), 1, 2)
+        sums11, sums21 = early_sums((1, 2), 1, 1)
+        (sums31,) = early_sums((3,), 1, 0)
         y01 = with_bias(sums01, 0, h_blocks(5, 1).bitcast(F32))
         put_scaled(scaled_on_gpsimd(y01, 1, fresh(0, 1)), 0, 1)
-        y11 = with_bias(sums11, 1, h_blocks(7, 1).bitcast(F32))
-        y21 = with_bias(sums21, 2, h_blocks(6, 1).bitcast(F32))
+        y12 = h_blocks(6, 2).bitcast(F32).rearrange("p (c j) -> p c j", c=2)
+        with_bias(sums11, 1, y12[:, 0, :])
+        with_bias(sums21, 2, y12[:, 1, :])
         product_on_gpsimd(4)
-        put_scaled(scaled_on_gpsimd(y11, 1, fresh(1, 1)), 1, 1)
-        put_scaled(scaled_on_gpsimd(y21, 1, fresh(2, 1)), 2, 1)
+        scaled12 = two_scaled_on_gpsimd(y12, 1, held([P, 2, CHUNK], F32, "scaled12"))
+        put_scaled(scaled12[:, 0, :], 1, 1)
+        put_scaled(scaled12[:, 1, :], 2, 1)
         both_sums(6)
         both_sums(7)
         product_on_gpsimd(6)
@@ -358,8 +365,4 @@ def tile_list_modp_ggelu_noneb_kernel(
         for c in range(PAGES):
             sums = down_sums(c, HALF, J, bank(LATE_DOWN_BANK[c])[:])
             put(with_bias(sums, c, held([P, HALF], F32, f"late_y{c}")[:]), c, HALF, J)
-            if c < PAGES - 1:
-                nc.sync.dma_start(out[P * c : P * (c + 1), :], pages[c][:])
-            else:
-                for queue, t0 in ((nc.sync, 0), (nc.scalar, T // 2)):
-                    queue.dma_start(out[P * c : P * (c + 1), t0 : t0 + T // 2], pages[c][:, t0 : t0 + T // 2])
+            nc.sync.dma_start(out[P * c : P * (c + 1), :], pages[c][:])

@@ -83,10 +83,9 @@ def tile_list_modp_ggelu_noneb_kernel(
         nc.sync.dma_start(offsets[:], offs)
         tab_sc = at(AT_TAB_SC, [P, T], U8, "tab_sc")
         nc.gpsimd.memset(tab_sc[:].bitcast(I32), 0)
-        for r in range(4):
-            nc.sync.dma_start(
-                tab_sc[r:P:16, :].bitcast(I32), tab_scales[:, r:16:4, :].rearrange("a q t -> q a t").bitcast(I32)
-            )
+        for q in range(4):
+            nc.sync.dma_start(tab_sc[32 * q : 32 * q + 4, :].bitcast(I32), tab_scales[0, 4 * q : 4 * q + 4, :].bitcast(I32))
+        nc.sync.dma_start(tab_sc[4:P:8, :].bitcast(I32), tab_scales[1].bitcast(I32))
 
         def load_tab(a, words):
             nc.sync.dma_start(words[:], tab_words[a].rearrange("p t i -> p (t i)").bitcast(I32))
@@ -126,7 +125,7 @@ def tile_list_modp_ggelu_noneb_kernel(
         for q in range(4):
             nc.sync.dma_start(
                 moved_sc[32 * q : 32 * q + 4, :].bitcast(I32).rearrange("p (n c) -> p n c", n=4),
-                picked_sc[32 * q + 16 : 32 * q + 20, :, 0:CHUNK].bitcast(I32),
+                picked_sc[32 * q + 4 : 32 * q + 32 : 8, :, 0:CHUNK].bitcast(I32),
             )
 
         def v_sc(a, blk):

@@ -26,9 +26,11 @@ BLOCKS = J // BLOCK
 CHUNK = 2 * BLOCK
 HALF = J // 2
 PAGES = N // P
-OVERLAP = 64
-WORD_ROW = BLOCK + OVERLAP // 4
-BYTE_ROW = CHUNK + OVERLAP
+ALIGN = 256
+OVERLAP = ALIGN
+ROW_GAP = 64
+WORD_ROW = BLOCK + ROW_GAP // 4
+BYTE_ROW = CHUNK + ROW_GAP
 SCALAR_M = (91, 68)
 GATE_BANK = (0, 1, 2, 3, 4, 0, 4, 4)
 UP_BANK = (4, 5, 6, 7, 5, 1, 5, 5)
@@ -44,7 +46,7 @@ AT_WG_RAW = AT_EPILOGUE + 4 * J + OVERLAP
 AT_PAGE2 = AT_WG_RAW + 4 * R - OVERLAP
 AT_PAGE3 = AT_PAGE2 + 4 * T
 AT_WG_SC = AT_PAGE3 + 4 * T - OVERLAP
-AT_WU1 = AT_WG_SC + OVERLAP + 4 * WORD_ROW * 5
+AT_WU1 = AT_WG_SC + OVERLAP + 4 * WORD_ROW * 5 + 3 * ROW_GAP
 AT_GEL0 = AT_WU1 + 16 * R
 AT_Y10 = AT_GEL0 + 4 * BANK
 
@@ -60,10 +62,10 @@ def tile_list_modp_ggelu_noneb_kernel(
         psum = ctx.enter_context(tc.psum_pool(name="psum", bufs=1))
 
         def at(offset, shape, dtype, name):
-            return placed.tile(shape, dtype, name=name, align_bytes=64, offset=offset)
+            return placed.tile(shape, dtype, name=name, align_bytes=ALIGN, offset=offset)
 
         def held(shape, dtype, name):
-            return keep.tile(shape, dtype, name=name, align_bytes=64)
+            return keep.tile(shape, dtype, name=name, align_bytes=ALIGN)
 
         offsets = keep.tile([P, J // 16], U16, name="offsets")
 
@@ -192,7 +194,7 @@ def tile_list_modp_ggelu_noneb_kernel(
             gel[blk] = held([P, BANK], F32, f"gel{blk}")
         runs = {3: 1, 4: 2, 6: 2}
         factors = {
-            first: ring.tile([P, 2, count * BANK], F32, name="factors", tag=f"factors{first}", align_bytes=64)
+            first: ring.tile([P, 2, count * BANK], F32, name="factors", tag=f"factors{first}", align_bytes=ALIGN)
             for first, count in runs.items()
         }
         ga = {}
@@ -334,7 +336,7 @@ def tile_list_modp_ggelu_noneb_kernel(
         y23 = held([P, 2, CHUNK], F32, "y23")
         with_bias(early_sums((2,), 0, 0)[0], 2, y23[:, 0, :])
         with_bias(early_sums((3,), 0, 1)[0], 3, y23[:, 1, :])
-        scaled10 = ring.tile([P, CHUNK], F32, name="scaled10", tag="factors3", align_bytes=64)
+        scaled10 = ring.tile([P, CHUNK], F32, name="scaled10", tag="factors3", align_bytes=ALIGN)
         scaled_on_gpsimd(y10, 0, scaled10)
         quantise_h(1, CHUNK, at(AT_Y10, [P, CHUNK], U32, "h_q1"))
         scaled23 = two_scaled_on_gpsimd(y23[:], 0, at(AT_SCALED23, [P, 2, CHUNK], F32, "scaled23"))
@@ -359,7 +361,7 @@ def tile_list_modp_ggelu_noneb_kernel(
         both_sums(7)
         product_on_gpsimd(6)
         quantise_h(2, HALF, held([P, HALF], U32, "h_q2"))
-        y31 = ring.tile([P, CHUNK], F32, name="y31", tag="factors6", align_bytes=64)
+        y31 = ring.tile([P, CHUNK], F32, name="y31", tag="factors6", align_bytes=ALIGN)
         put(with_bias(sums31, 3, y31[:]), 3, CHUNK, HALF)
         for c in range(PAGES):
             sums = down_sums(c, HALF, J, bank(LATE_DOWN_BANK[c])[:])

from contextlib import ExitStack

import concourse.mybir as mybir

K, R, N, T, J = 1024, 512, 512, 2048, 1024
FLOPS = 2 * J * (2 * K * R + R * N)

F32 = mybir.dt.float32
BF16 = mybir.dt.bfloat16
I32 = mybir.dt.int32
U32 = mybir.dt.uint32
U16 = mybir.dt.uint16
U8 = mybir.dt.uint8
FP8X4 = mybir.dt.float8_e4m3fn_x4
FP4X4 = mybir.dt.float4_e2m1fn_x4
MULT = mybir.AluOpType.mult
ADD = mybir.AluOpType.add
GELU = mybir.ActivationFunctionType.Gelu_apprx_tanh
IDENT = mybir.ActivationFunctionType.Identity

P = 128
PASSES = K // 512
BANK = 512
BLOCK = 128
BLOCKS = J // BLOCK
CHUNK = 2 * BLOCK
HALF = J // 2
PAGES = N // P
ALIGN = 256
OVERLAP = ALIGN
ROW_GAP = 64
WORD_ROW = BLOCK + ROW_GAP // 4
BYTE_ROW = CHUNK + ROW_GAP
SCALAR_M = (91, 68)
GATE_BANK = (0, 1, 2, 3, 4, 0, 4, 4)
UP_BANK = (4, 5, 6, 7, 5, 1, 5, 5)
LATE_DOWN_BANK = (3, 6, 7, 2)
AT_H2 = 0
AT_SCALED23 = AT_H2 + 8 * HALF
AT_H1 = AT_SCALED23 - OVERLAP
AT_TAB1 = AT_H1 + 8 * CHUNK - OVERLAP
AT_TAB_SC = AT_TAB1 + 4 * T
AT_WD = AT_TAB_SC
AT_EPILOGUE = AT_WD + 3 * N
AT_WG_RAW = AT_EPILOGUE + 4 * J + OVERLAP
AT_PAGE2 = AT_WG_RAW + 4 * R - OVERLAP
AT_PAGE3 = AT_PAGE2 + 4 * T
AT_WG_SC = AT_PAGE3 + 4 * T - OVERLAP
AT_WU1 = AT_WG_SC + OVERLAP + 4 * WORD_ROW * 5 + 3 * ROW_GAP
AT_GEL0 = AT_WU1 + 16 * R
AT_Y10 = AT_GEL0 + 4 * BANK


def tile_list_modp_ggelu_noneb_kernel(
    tc, tab_words, tab_scales, wg_words, wg_scales, wu, wd_words, wd_scales, b, wgo, offs, out
):
    nc = tc.nc
    with ExitStack() as ctx:
        keep = ctx.enter_context(tc.tile_pool(name="keep", bufs=1))
        ring = ctx.enter_context(tc.tile_pool(name="ring", bufs=1))
        placed = ctx.enter_context(tc.tile_pool(name="placed", bufs=1))
        psum = ctx.enter_context(tc.psum_pool(name="psum", bufs=1))

        def at(offset, shape, dtype, name):
            return placed.tile(shape, dtype, name=name, align_bytes=ALIGN, offset=offset)

        def held(shape, dtype, name):
            return keep.tile(shape, dtype, name=name, align_bytes=ALIGN)

        offsets = keep.tile([P, J // 16], U16, name="offsets")

        def listed(j0, j1):
            return offsets[:, j0 // 16 : j1 // 16]

        def zero_on_own_port(words):
            count = words.shape[1]
            nc.vector.memset(words[:, 0 : count - 1], 0)
            nc.vector.memset(words[:, count - 1 : count], 0)

        wg_raw = at(AT_WG_RAW, [P, PASSES * 2 * R], U8, "wg_raw")
        nc.sync.dma_start(
            wg_raw[:].bitcast(I32).rearrange("p (a n) -> p a n", a=PASSES),
            wg_words.rearrange("a p n -> p a n").bitcast(I32),
        )
        nc.sync.dma_start(offsets[:], offs)
        tab_sc = at(AT_TAB_SC, [P, T], U8, "tab_sc")
        nc.gpsimd.memset(tab_sc[:].bitcast(I32), 0)
        for q in range(4):
            nc.sync.dma_start(tab_sc[32 * q : 32 * q + 4, :].bitcast(I32), tab_scales[0, 4 * q : 4 * q + 4, :].bitcast(I32))
        nc.sync.dma_start(tab_sc[4:P:8, :].bitcast(I32), tab_scales[1].bitcast(I32))

        def load_tab(a, words):
            nc.sync.dma_start(words[:], tab_words[a].rearrange("p t i -> p (t i)").bitcast(I32))
            return words

        def load_wu(a, raw):
            nc.sync.dma_start(raw[:], wu[512 * a : 512 * (a + 1), :].rearrange("(p i) r -> p i r", i=4))
            return raw

        tab = [load_tab(0, held([P, T], I32, "tab0"))]
        wg_sc_raw = at(AT_WG_SC, [P, PASSES * R], U8, "wg_sc_raw")
        zero_on_own_port(wg_sc_raw[:].bitcast(I32))
        for q in range(4):
            nc.sync.dma_start(
                wg_sc_raw[32 * q : 32 * q + 4, :].bitcast(I32).rearrange("p (a n) -> p a n", a=PASSES),
                wg_scales[:, 4 * q : 4 * q + 4, :].rearrange("a g n -> g a n").bitcast(I32),
            )
        wu_raw = [load_wu(0, held([P, 4, R], F32, "wu_raw0")), load_wu(1, at(AT_WU1, [P, 4, R], F32, "wu_raw1"))]
        tab.append(load_tab(1, at(AT_TAB1, [P, T], I32, "tab1")))

        pages = [held([P, T], F32, "page0"), held([P, T], F32, "page1")]
        zero_on_own_port(pages[0][:].bitcast(I32))
        nc.gpsimd.memset(pages[1][:].bitcast(I32), 0)

        wg = held([P, PASSES * 2 * R], U8, "wg")
        nc.scalar.copy(
            wg[:].bitcast(U16).rearrange("p (a t m) -> p a t m", a=PASSES, t=4),
            wg_raw[:].bitcast(U16).rearrange("p (a m t) -> p a t m", a=PASSES, t=4),
        )
        pages.append(at(AT_PAGE2, [P, T], F32, "page2"))
        nc.gpsimd.memset(pages[2][:].bitcast(I32), 0)

        picked_sc = held([P, 4, BYTE_ROW], U8, "picked_sc")
        nc.vector.tensor_copy(picked_sc[:, 0, 0:CHUNK], tab_sc[:].indirect(listed(0, CHUNK)))
        nc.vector.tensor_copy(picked_sc[:, 1:4, 0:CHUNK], tab_sc[:].indirect(listed(CHUNK, J)))
        moved_sc = at(AT_WG_RAW, [P, J], U8, "moved_sc")
        for q in range(4):
            nc.sync.dma_start(
                moved_sc[32 * q : 32 * q + 4, :].bitcast(I32).rearrange("p (n c) -> p n c", n=4),
                picked_sc[32 * q + 4 : 32 * q + 32 : 8, :, 0:CHUNK].bitcast(I32),
            )

        def v_sc(a, blk):
            if a == 0:
                return picked_sc[:, blk // 2, BLOCK * (blk % 2) : BLOCK * (blk % 2 + 1)]
            return moved_sc[:, BLOCK * blk : BLOCK * (blk + 1)]

        v = {}

        def gather_words(a, blk0, blk1, picked):
            window = tab[a][:].bitcast(U32).indirect(listed(BLOCK * blk0, BLOCK * blk1))
            nc.vector.tensor_copy(picked[:, :, 0:BLOCK], window)
            for blk in range(blk0, blk1):
                v[a, blk] = picked[:, blk - blk0, 0:BLOCK]

        gather_words(0, 0, 3, held([P, 3, WORD_ROW], U32, "v0_0"))
        wg_sc = held([P, PASSES * R], U8, "wg_sc")
        nc.vector.tensor_copy(
            wg_sc[:].rearrange("p (a t m) -> p a t m", a=PASSES, t=4),
            wg_sc_raw[:].rearrange("p (a m t) -> p a t m", a=PASSES, t=4),
        )
        gather_words(0, 3, BLOCKS, at(AT_WG_SC + OVERLAP, [P, 5, WORD_ROW], U32, "v0_3"))
        pages.append(at(AT_PAGE3, [P, T], F32, "page3"))
        nc.gpsimd.memset(pages[3][:].bitcast(I32), 0)

        wu_bf = [held([P, 4 * R], BF16, f"wu_bf{a}") for a in range(PASSES)]
        wu_q = [held([P, R], U32, f"wu_q{a}") for a in range(PASSES)]
        wu_sc = [held([P, R], U8, f"wu_sc{a}") for a in range(PASSES)]
        rounded = [wu_bf[a][:].rearrange("p (t m i) -> p m i t", t=4, i=4) for a in range(PASSES)]
        dealt = [wu_raw[a][:].rearrange("p i (m t) -> p m i t", t=4) for a in range(PASSES)]
        for a in range(PASSES):
            nc.scalar.copy(rounded[a][:, 0 : SCALAR_M[a]], dealt[a][:, 0 : SCALAR_M[a]])
            nc.vector.tensor_copy(rounded[a][:, SCALAR_M[a] : P], dealt[a][:, SCALAR_M[a] : P])
            nc.vector.quantize_mx(out=wu_q[a][:].bitcast(FP8X4), scales=wu_sc[a][:], in_=wu_bf[a][:])

        for blk0, blk1 in ((0, 1), (1, 2), (2, 4), (4, 7)):
            gather_words(1, blk0, blk1, at(AT_WU1 + 4 * BLOCK * blk0, [P, blk1 - blk0, BLOCK], U32, f"v1_{blk0}"))

        wd_bytes = at(AT_WD, [P, 3 * N], U8, "wd_bytes")
        wd_sc = wd_bytes[:, 0:N]
        wd = wd_bytes[:, N : 3 * N]
        epilogue = at(AT_EPILOGUE, [P, J + N // P], F32, "epilogue")
        router_w = epilogue[:, 0:J]
        bias = epilogue[:, J : J + N // P]
        nc.sync.dma_start(router_w[:, 0:HALF], wgo[:, 0:HALF])
        with nc.allow_non_contiguous_dma(reason="one bias value a partition"):
            nc.sync.dma_start(bias, b.rearrange("(c p) -> p c", p=P))
        nc.sync.dma_start(wd.bitcast(I32), wd_words[0].bitcast(I32))
        for q in range(4):
            nc.sync.dma_start(
                wd_bytes[32 * q : 32 * q + 4, 0:N].bitcast(I32), wd_scales[0, 4 * q : 4 * q + 4, :].bitcast(I32)
            )
        nc.sync.dma_start(router_w[:, HALF:J], wgo[:, HALF:J])

        h_bf = [
            held([P, 4 * CHUNK], BF16, "h_bf0")[:],
            at(AT_H1, [P, 4 * CHUNK], BF16, "h_bf1")[:],
            at(AT_H2, [P, 4 * HALF], BF16, "h_bf2")[:],
        ]
        h_q = {}
        h_sc = held([P, J], U8, "h_sc")
        gel = {0: at(AT_GEL0, [P, BANK], F32, "gel0")}
        for blk in (1, 2):
            gel[blk] = held([P, BANK], F32, f"gel{blk}")
        runs = {3: 1, 4: 2, 6: 2}
        factors = {
            first: ring.tile([P, 2, count * BANK], F32, name="factors", tag=f"factors{first}", align_bytes=ALIGN)
            for first, count in runs.items()
        }
        ga = {}
        ub = {}
        from_bank = "p (t n e) -> p n t e"
        by_pairs = "p (n t e) -> p n t e"
        by_token = "p (n e t) -> p n t e"

        def factor(blk, which):
            first = blk if blk in runs else blk - 1
            return factors[first][:, which, BANK * (blk - first) : BANK * (blk - first + 1)]

        def bank(n):
            return psum.tile([P, BANK], F32, name="bank", tag=f"bank{n}")

        def first_stage_pass(sums, blk, a, codes, scales):
            for t in range(4):
                nc.tensor.matmul_mx(
                    out=sums[:, BLOCK * t : BLOCK * (t + 1)],
                    lhsT=codes(t),
                    lhsT_scale=scales[:, P * t : P * (t + 1)],
                    rhs=v[a, blk].bitcast(FP8X4),
                    rhs_scale=v_sc(a, blk),
                    start=(a == 0 and t == 0),
                    stop=(a == PASSES - 1 and t == 3),
                )

        def gate_pass(blk, a):
            if a == 0:
                ga[blk] = bank(GATE_BANK[blk])

            def codes(t):
                c0 = R * a + P * t
                return wg[:, 2 * c0 : 2 * (c0 + P)].bitcast(FP4X4)

            first_stage_pass(ga[blk], blk, a, codes, wg_sc[:, R * a : R * (a + 1)])
            if a == PASSES - 1:
                if blk in gel:
                    result = gel[blk][:].rearrange(by_pairs, t=4, e=2)
                else:
                    result = factor(blk, 0).rearrange(by_token, t=4, e=2)
                nc.scalar.activation(result, ga[blk][:].rearrange(from_bank, t=4, e=2), GELU)

        def up_pass(blk, a):
            if a == 0:
                ub[blk] = bank(UP_BANK[blk])

            def codes(t):
                return wu_q[a][:, P * t : P * (t + 1)].bitcast(FP8X4)

            first_stage_pass(ub[blk], blk, a, codes, wu_sc[a])
            if a == PASSES - 1 and blk not in gel:
                nc.scalar.copy(factor(blk, 1).rearrange(by_token, t=4, e=2), ub[blk][:].rearrange(from_bank, t=4, e=2))

        def both_sums(blk):
            for stage in (gate_pass, up_pass):
                for a in range(PASSES):
                    stage(blk, a)

        def h_blocks(blk, count):
            n = min(blk // 2, 2)
            return h_bf[n][:, BANK * (blk - 2 * n) : BANK * (blk - 2 * n + count)]

        def product(blk):
            nc.vector.tensor_tensor(
                h_blocks(blk, 1).rearrange(by_token, t=4, e=2),
                ub[blk][:].rearrange(from_bank, t=4, e=2),
                gel[blk][:].rearrange(by_pairs, t=4, e=2),
                MULT,
            )

        def product_on_gpsimd(first):
            nc.gpsimd.tensor_tensor(h_blocks(first, runs[first]), factors[first][:, 0, :], factors[first][:, 1, :], MULT)

        def quantise_h(n, j0, codes):
            h_q[j0] = codes
            nc.vector.quantize_mx(out=codes[:].bitcast(FP8X4), scales=h_sc[:, j0 : j0 + codes.shape[1]], in_=h_bf[n])

        def down_sums(c, j0, j1, sums):
            nc.tensor.matmul_mx(
                out=sums,
                lhsT=wd[:, 2 * P * c : 2 * P * (c + 1)].bitcast(FP4X4),
                lhsT_scale=wd_sc[:, P * c : P * (c + 1)],
                rhs=h_q[j0][:].bitcast(FP8X4),
                rhs_scale=h_sc[:, j0:j1],
                start=True,
                stop=True,
            )
            return sums

        def early_sums(rows, n, in_bank):
            sums = bank(in_bank)
            return [
                down_sums(c, CHUNK * n, CHUNK * (n + 1), sums[:, CHUNK * i : CHUNK * (i + 1)])
                for i, c in enumerate(rows)
            ]

        def with_bias(sums, c, y):
            nc.scalar.activation(y, sums, IDENT, bias=bias[:, c : c + 1])
            return y

        def scaled_on_gpsimd(y, n, scaled):
            nc.gpsimd.tensor_tensor(scaled[:], y, router_w[:, CHUNK * n : CHUNK * (n + 1)], MULT)
            return scaled

        def two_scaled_on_gpsimd(y, n, scaled):
            weights = router_w[:, CHUNK * n : CHUNK * (n + 1)].unsqueeze(1).to_broadcast([P, 2, CHUNK])
            nc.gpsimd.tensor_tensor(scaled[:], y, weights, MULT)
            return scaled

        def fresh(c, n):
            return held([P, CHUNK], F32, f"scaled{c}{n}")

        def put_scaled(scaled, c, n):
            nc.vector.tensor_copy(pages[c][:].indirect(listed(CHUNK * n, CHUNK * (n + 1))), scaled[:, :])

        def put(y, c, j0, j1):
            nc.vector.tensor_tensor(pages[c][:].indirect(listed(j0, j1)), y, router_w[:, j0:j1], MULT)

        for blk in range(4):
            gate_pass(blk, 0)
        for pair in ((0, 1), (2, 3)):
            for blk in pair:
                gate_pass(blk, 1)
            for a in range(PASSES):
                for blk in pair:
                    up_pass(blk, a)
        product(0)
        product(1)
        gather_words(1, 7, BLOCKS, at(AT_GEL0, [P, 1, BLOCK], U32, "v1_7"))
        quantise_h(0, 0, held([P, CHUNK], U32, "h_q0"))
        product(2)
        product_on_gpsimd(3)
        scaled00 = fresh(0, 0)
        (sums00,) = early_sums((0,), 0, 4)
        nc.vector.scalar_tensor_tensor(scaled00[:], sums00, bias[:, 0:1], router_w[:, 0:CHUNK], ADD, MULT)
        put_scaled(scaled00, 0, 0)
        y10 = with_bias(early_sums((1,), 0, 5)[0], 1, at(AT_Y10, [P, CHUNK], F32, "y10")[:])
        y23 = held([P, 2, CHUNK], F32, "y23")
        with_bias(early_sums((2,), 0, 0)[0], 2, y23[:, 0, :])
        with_bias(early_sums((3,), 0, 1)[0], 3, y23[:, 1, :])
        scaled10 = ring.tile([P, CHUNK], F32, name="scaled10", tag="factors3", align_bytes=ALIGN)
        scaled_on_gpsimd(y10, 0, scaled10)
        quantise_h(1, CHUNK, at(AT_Y10, [P, CHUNK], U32, "h_q1"))
        scaled23 = two_scaled_on_gpsimd(y23[:], 0, at(AT_SCALED23, [P, 2, CHUNK], F32, "scaled23"))
        put_scaled(scaled10, 1, 0)
        put_scaled(scaled23[:, 0, :], 2, 0)
        put_scaled(scaled23[:, 1, :], 3, 0)
        both_sums(4)
        both_sums(5)
        (sums01,) = early_sums((0,), 1, 2)
        sums11, sums21 = early_sums((1, 2), 1, 1)
        (sums31,) = early_sums((3,), 1, 0)
        y01 = with_bias(sums01, 0, h_blocks(5, 1).bitcast(F32))
        put_scaled(scaled_on_gpsimd(y01, 1, fresh(0, 1)), 0, 1)
        y12 = h_blocks(6, 2).bitcast(F32).rearrange("p (c j) -> p c j", c=2)
        with_bias(sums11, 1, y12[:, 0, :])
        with_bias(sums21, 2, y12[:, 1, :])
        product_on_gpsimd(4)
        scaled12 = two_scaled_on_gpsimd(y12, 1, held([P, 2, CHUNK], F32, "scaled12"))
        put_scaled(scaled12[:, 0, :], 1, 1)
        put_scaled(scaled12[:, 1, :], 2, 1)
        both_sums(6)
        both_sums(7)
        product_on_gpsimd(6)
        quantise_h(2, HALF, held([P, HALF], U32, "h_q2"))
        y31 = ring.tile([P, CHUNK], F32, name="y31", tag="factors6", align_bytes=ALIGN)
        put(with_bias(sums31, 3, y31[:]), 3, CHUNK, HALF)
        for c in range(PAGES):
            sums = down_sums(c, HALF, J, bank(LATE_DOWN_BANK[c])[:])
            put(with_bias(sums, c, held([P, HALF], F32, f"late_y{c}")[:]), c, HALF, J)
            nc.sync.dma_start(out[P * c : P * (c + 1), :], pages[c][:])
